import numpy as np
import ml_dtypes


def mxq(x, axis, fmt="e4m3"):
    dtype, down = {"e4m3": (ml_dtypes.float8_e4m3fn, 7), "e5m2": (ml_dtypes.float8_e5m2, 14)}[fmt]
    v = np.moveaxis(np.asarray(x, np.float32).astype(ml_dtypes.bfloat16).astype(np.float64), axis, -1)
    blocks = v.reshape(v.shape[:-1] + (-1, 32))
    amax = np.abs(blocks).max(-1, keepdims=True)
    byte = np.maximum(np.where(amax > 0, np.frexp(amax)[1] - 1 + 127, 0) - down, 1)
    scale = np.exp2(byte - 127.0)
    codes = (blocks / scale).astype(np.float32).astype(dtype).astype(np.float64)
    return np.moveaxis((codes * scale).reshape(v.shape), -1, axis)


WIDE = False


def mx_kscale(k):
    if not WIDE:
        return np.ones(k)
    levels = np.array([10, -10, 5, -5, 0])
    if k % 512:
        return np.exp2(np.random.permutation(np.resize(levels, k // 32))).repeat(32)
    a = np.empty((k // 512, 16))
    for p in range(k // 512):
        a[p, :8] = np.random.permutation(np.resize(levels, 8))
        for g in range(8):
            far = levels[np.abs(levels - a[p, g]) >= 10]
            a[p, g + 8] = far[np.random.randint(len(far))]
    return np.exp2(a.ravel()).repeat(32)


def f64(x):
    return np.asarray(x).astype(np.float64)


def striped(idx):
    return np.tile(idx.reshape(-1, 16).T, (8, 1)).astype(np.uint16)


def unstriped(offs):
    return offs[:16].T.reshape(-1).astype(np.int64)


def pack_weight(w):
    k, n = w.shape
    w = f64(np.asarray(w, np.float32).astype(ml_dtypes.bfloat16)).reshape(k // 32, 32, n)
    amax = np.abs(w).max(1)
    byte = np.clip(np.where(amax > 0, np.frexp(amax)[1] - 1 + 127 - 7, 1), 1, 254)
    scaled = (w * np.exp2(127.0 - byte)[:, None, :]).reshape(k, n).astype(np.float32)
    words = np.ascontiguousarray(scaled.reshape(k // 512, 128, 4, n).transpose(0, 1, 3, 2)).astype(ml_dtypes.float8_e4m3fn).view(np.uint8)
    return words, np.ascontiguousarray(byte.astype(np.uint8).reshape(k // 512, 16, n))


def unpack_weight(words, scales):
    g, p, n, _ = words.shape
    vals = np.ascontiguousarray(words).view(ml_dtypes.float8_e4m3fn).astype(np.float64) * np.repeat(np.exp2(scales.astype(np.float64) - 127.0), 8, axis=1)[..., None]
    return vals.transpose(0, 1, 3, 2).reshape(g * 512, n)


def silu(v):
    return v / (1.0 + np.exp(-np.maximum(v, -700.0)))


K, T, S, D, V, H, N = 1024, 2048, 1024, 3, 512, 512, 128
P = 2 ** 7


def setup_inputs():
    n = np.random.standard_normal
    s = mx_kscale(K)[:, None]
    u = mx_kscale(H)
    packed_xT = pack_weight(n((K, T)) * s)
    return {
        "x_words": packed_xT[0],
        "x_scales": packed_xT[1],
        "w1": (n((K, H)) / np.sqrt(K) / s * u).astype(np.float32),
        "w2": (n((H, N)) / np.sqrt(H) / u[:, None]).astype(np.float32),
        "gate": (np.tile(np.random.uniform(0.2, 1.0, (D, 1, V)) / np.sqrt(D), (1, P, 1))).astype(np.float32),
        "offs": striped(np.random.permutation(T)[:S]),
        "cen": striped(np.random.permutation(S)[:V]),
        "pos1": striped(np.random.permutation(S)[:V]),
        "pos2": striped(np.random.permutation(S)[:V]),
        "pos3": striped(np.random.permutation(S)[:V]),
    }


def reference(x_words, x_scales, w1, w2, gate, offs, cen, pos1, pos2, pos3):
    xq = unpack_weight(x_words, x_scales)[:, unstriped(offs)]
    h = silu(mxq(f64(w1), 0, "e4m3").T @ xq)
    z = h[:, unstriped(cen)] - (h[:, unstriped(pos1)] * f64(gate)[0, :1] + h[:, unstriped(pos2)] * f64(gate)[1, :1] + h[:, unstriped(pos3)] * f64(gate)[2, :1])
    return mxq(f64(w2), 0, "e4m3").T @ mxq(z, 0, "e4m3")

@@ -1,0 +1,242 @@
+from contextlib import ExitStack
+
+import concourse.mybir as mybir
+from concourse.masks import make_identity
+
+K, T, S, D, V, H, N = 1024, 2048, 1024, 3, 512, 512, 128
+FLOPS = 2 * K * H * S + 2 * H * N * V
+
+F32 = mybir.dt.float32
+BF16 = mybir.dt.bfloat16
+I32 = mybir.dt.int32
+U32 = mybir.dt.uint32
+U16 = mybir.dt.uint16
+U8 = mybir.dt.uint8
+FP8X4 = mybir.dt.float8_e4m3fn_x4
+SILU = mybir.ActivationFunctionType.Silu
+COPY = mybir.ActivationFunctionType.Copy
+MULT = mybir.AluOpType.mult
+
+P = 128
+PACK = 4
+PASSES = K // (P * PACK)
+TILES = H // P
+BLOCKS = V // P
+ENTRIES_PER_COLUMN = 16
+
+
+def tile_picked_lapl_silu_p_kernel(
+    tc, x_words, x_scales, w1, w2, gate, offs, cen, pos1, pos2, pos3, out
+):
+    nc = tc.nc
+    with ExitStack() as ctx:
+        held = ctx.enter_context(tc.tile_pool(name="held", bufs=1))
+        keep = ctx.enter_context(tc.tile_pool(name="keep", bufs=1))
+        psum = ctx.enter_context(tc.psum_pool(name="psum", bufs=1))
+
+        def sb(name, shape, dtype, tag=None):
+            return keep.tile(shape, dtype, name=name, tag=tag or name, align_bytes=64)
+
+        def bank(name, b, cols):
+            return psum.tile([P, cols], F32, name=name, tag="bank%d" % b)
+
+        def entries(lst, start, count):
+            return lst[:, start // ENTRIES_PER_COLUMN : (start + count) // ENTRIES_PER_COLUMN]
+
+        scale_win = sb("scale_win", [P, T], U8)
+        nc.vector.memset(scale_win[:].bitcast(I32), 0)
+        warm_in = sb("warm_in", [P, 1], F32)
+        warm_out = sb("warm_out", [P, 1], F32)
+        nc.gpsimd.memset(warm_in[:], 0.0)
+        nc.scalar.activation(out=warm_out[:], in_=warm_in[:], func=SILU)
+        ident = sb("ident", [P, P], F32)
+        make_identity(nc, ident[:])
+
+        offs_sb = held.tile([P, S // 16], U16, name="offs_sb")
+        lists = [held.tile([P, V // 16], U16, name="list%d" % d) for d in range(D + 1)]
+        list_src = [cen, pos1, pos2, pos3]
+        word_win = [sb("word_win%d" % z, [P, T], I32) for z in range(PASSES)]
+        chunks = [(0, 128), (128, 128), (256, 256)]
+        w1_raw = {}
+        for c, (c0, cw) in enumerate(chunks):
+            for z in range(PASSES):
+                w1_raw[c, z] = sb("w1_raw%d_%d" % (c, z), [P, PACK, cw], F32)
+        gate_raw = [sb("gate_raw%d" % d, [P, V], F32) for d in range(D)]
+        w2_raw = sb("w2_raw", [P, PACK, N], F32)
+
+        def load_words(z):
+            nc.sync.dma_start(out=word_win[z][:], in_=x_words[z].rearrange("p n t -> p (n t)").bitcast(I32))
+
+        def load_w1(c):
+            c0, cw = chunks[c]
+            for z in range(PASSES):
+                rows = w1[z * P * PACK : (z + 1) * P * PACK, c0 : c0 + cw]
+                nc.sync.dma_start(out=w1_raw[c, z][:], in_=rows.rearrange("(p j) c -> p j c", j=PACK))
+
+        nc.sync.dma_start(offs_sb[:], offs)
+        nc.sync.dma_start(lists[0][:], list_src[0])
+        nc.sync.dma_start(lists[1][:], list_src[1])
+        for q in range(4):
+            nc.sync.dma_start(
+                out=scale_win[32 * q : 32 * q + 4 * PASSES, :].bitcast(I32),
+                in_=x_scales[:, 4 * q : 4 * q + 4, :].bitcast(I32),
+            )
+        load_words(0)
+        load_w1(0)
+        load_words(1)
+        load_w1(1)
+        nc.sync.dma_start(out=gate_raw[0][:], in_=gate[0])
+        nc.sync.dma_start(lists[2][:], list_src[2])
+        nc.sync.dma_start(out=gate_raw[1][:], in_=gate[1])
+        nc.sync.dma_start(lists[3][:], list_src[3])
+        nc.sync.dma_start(out=gate_raw[2][:], in_=gate[2])
+        load_w1(2)
+        nc.sync.dma_start(out=w2_raw[:], in_=w2.rearrange("(p j) m -> p j m", j=PACK))
+
+        x_scale = sb("x_scale", [P, S], U8)
+        x_code = [sb("x_code%d" % z, [P, S], I32) for z in range(PASSES)]
+        nc.vector.tensor_copy(x_scale[:], scale_win[:].indirect(offs_sb[:]))
+        nc.vector.tensor_copy(x_code[0][:].bitcast(U32), word_win[0][:].bitcast(U32).indirect(offs_sb[:]))
+
+        w1_code = [sb("w1_code%d" % t, [P, PASSES * P], U32) for t in range(TILES)]
+        w1_scale = [sb("w1_scale%d" % t, [P, PASSES * P], U8) for t in range(TILES)]
+
+        def quantise_w1(t, copy):
+            c = min(t, 2)
+            first = t * P - chunks[c][0]
+            stage = sb("w1_stage%d" % t, [P, PASSES * P * PACK], BF16, tag="stage%d" % t)
+            for z in range(PASSES):
+                dst = stage[:, z * P * PACK : (z + 1) * P * PACK].rearrange("p (c j) -> p c j", j=PACK)
+                copy(out=dst, in_=w1_raw[c, z][:, :, first : first + P].rearrange("p j c -> p c j"))
+            nc.vector.quantize_mx(out=w1_code[t][:].bitcast(FP8X4), scales=w1_scale[t][:], in_=stage[:])
+
+        quantise_w1(0, nc.scalar.copy)
+        first_pieces = [(0, 512), (512, 256), (768, 256)]
+        for s0, n in first_pieces:
+            nc.vector.tensor_copy(
+                x_code[1][:, s0 : s0 + n].bitcast(U32), word_win[1][:].bitcast(U32).indirect(entries(offs_sb, s0, n))
+            )
+
+        h = [sb("h%d" % t, [P, S], F32) for t in range(TILES)]
+        halves = [(0, 512), (512, 512)]
+        h_banks = [(0, 1, 2), (3, 4), (0, 1), (2, 5)]
+
+        def project(t):
+            pieces = first_pieces if t == 0 else halves
+            accs = [bank("acc%d_%d" % (t, i), h_banks[t][i], n) for i, (s0, n) in enumerate(pieces)]
+            order = [(z, i) for z in range(PASSES) for i in range(len(pieces))]
+            if t > 0:
+                order = [(z, i) for i in range(len(pieces)) for z in range(PASSES)]
+            for z, i in order:
+                s0, n = pieces[i]
+                nc.tensor.matmul_mx(
+                    out=accs[i][:],
+                    lhsT=w1_code[t][:, z * P : (z + 1) * P].bitcast(FP8X4),
+                    lhsT_scale=w1_scale[t][:, z * P : (z + 1) * P],
+                    rhs=x_code[z][:, s0 : s0 + n].bitcast(FP8X4),
+                    rhs_scale=x_scale[4 * z : P, s0 : s0 + n],
+                    start=(z == 0),
+                    stop=(z == PASSES - 1),
+                )
+                if z == PASSES - 1:
+                    nc.scalar.activation(out=h[t][:, s0 : s0 + n], in_=accs[i][:], func=SILU)
+
+        project(0)
+        quantise_w1(1, nc.vector.tensor_copy)
+        neg_gate = [sb("neg_gate%d" % d, [P, V], F32) for d in range(D)]
+        for d in range(D):
+            nc.scalar.activation(out=neg_gate[d][:], in_=gate_raw[d][:], func=COPY, scale=-1.0)
+        project(1)
+        quantise_w1(2, nc.scalar.copy)
+        quantise_w1(3, nc.scalar.copy)
+        w2_stage = sb("w2_stage", [P, N * PACK], BF16)
+        w2_scale = sb("w2_scale", [P, N], U8)
+        nc.scalar.copy(out=w2_stage[:].rearrange("p (m j) -> p m j", j=PACK), in_=w2_raw[:].rearrange("p j m -> p m j"))
+
+        z_rows = [sb("z_rows%d" % b, [P, H], BF16) for b in range(BLOCKS)]
+        reuse = {(0, 1): "stage1", (1, 0): "stage2", (2, 0): "stage3"}
+        terms = {}
+
+        def fetch(t, d, v0, n):
+            if (t, d) not in terms:
+                terms[t, d] = sb("term%d_%d" % (t, d), [P, V], F32, tag=reuse.get((t, d)))
+            dst = terms[t, d][:, v0 : v0 + n]
+            src = h[t][:].indirect(entries(lists[d], v0, n))
+            if d == 0:
+                nc.vector.tensor_copy(dst, src)
+            else:
+                nc.vector.tensor_tensor(dst, src, neg_gate[d - 1][:, v0 : v0 + n], MULT)
+
+        def turn_and_add(acc, t, d, b, first, last):
+            nc.tensor.matmul(
+                out=acc,
+                lhsT=terms[t, d][:, b * P : (b + 1) * P],
+                rhs=ident[:],
+                is_transpose=True,
+                start=first,
+                stop=last,
+            )
+
+        def round_rows(acc, t, b):
+            q = P // PACK
+            dst = z_rows[b][:].rearrange("v (u p e) -> v u p e", u=2, e=2)[:, :, q * t : q * (t + 1), :]
+            nc.scalar.copy(out=dst, in_=acc.rearrange("v (p u e) -> v u p e", u=2, e=2))
+
+        sum_banks = [4, 1, 5]
+        for t in range(TILES - 1):
+            if t >= 1:
+                project(t + 1)
+            acc = bank("sum%d" % t, sum_banks[t], V)
+            for d in range(D + 1):
+                fetch(t, d, 0, V)
+                for b in range(BLOCKS):
+                    turn_and_add(acc[:, b * P : (b + 1) * P], t, d, b, d == 0 and b == 0, d == D and b == BLOCKS - 1)
+            for b in range(BLOCKS):
+                round_rows(acc[:, b * P : (b + 1) * P], t, b)
+
+        last_banks = [6, 7, 7, 4]
+        back_banks = [2, 4, 1, 5]
+        t = TILES - 1
+        z_cols = [sb("z_cols%d" % b, [P, P * PACK], BF16) for b in range(BLOCKS)]
+        for blocks in [(0, 1), (2,), (3,)]:
+            accs = {b: bank("last%d" % b, last_banks[b], P) for b in blocks}
+            for d in range(D + 1):
+                fetch(t, d, blocks[0] * P, len(blocks) * P)
+                for b in blocks:
+                    turn_and_add(accs[b][:], t, d, b, d == 0, d == D)
+            for b in blocks:
+                round_rows(accs[b][:], t, b)
+                back = bank("back%d" % b, back_banks[b], 2 * P)
+                for u in range(2):
+                    nc.tensor.transpose(
+                        back[:, u * P : (u + 1) * P], z_rows[b][:].bitcast(F32)[:, u * P : (u + 1) * P], ident[:]
+                    )
+                nc.scalar.copy(
+                    out=z_cols[b][:].bitcast(F32).rearrange("p (v u) -> p v u", u=2),
+                    in_=back[:].rearrange("p (u v) -> p v u", u=2),
+                )
+
+        codes = sb("codes", [P, N + V], U32, tag="h%d" % t)
+        z_scale = [sb("z_scale%d" % b, [P, P], U8) for b in range(BLOCKS)]
+        w2_code = codes[:, :N]
+        nc.vector.quantize_mx(out=w2_code.bitcast(FP8X4), scales=w2_scale[:], in_=w2_stage[:])
+        result = sb("result", [P, V], F32)
+        early = bank("early", 0, V - P)
+        late = bank("late", 3, P)
+        for b in range(BLOCKS):
+            z_code = codes[:, N + b * P : N + (b + 1) * P]
+            nc.vector.quantize_mx(out=z_code.bitcast(FP8X4), scales=z_scale[b][:], in_=z_cols[b][:])
+            nc.tensor.matmul_mx(
+                out=early[:, b * P : (b + 1) * P] if b < BLOCKS - 1 else late[:],
+                lhsT=w2_code.bitcast(FP8X4),
+                lhsT_scale=w2_scale[:],
+                rhs=z_code.bitcast(FP8X4),
+                rhs_scale=z_scale[b][:],
+                start=True,
+                stop=True,
+            )
+            if b == BLOCKS - 2:
+                nc.vector.tensor_copy(out=result[:, : V - P], in_=early[:])
+                nc.sync.dma_start(out=out[:, : V - P], in_=result[:, : V - P])
+        nc.scalar.copy(out=result[:, V - P :], in_=late[:])
+        nc.sync.dma_start(out=out[:, V - P :], in_=result[:, V - P :])

@@ -153,8 +153,9 @@ def tile_picked_lapl_silu_p_kernel(
         w2_scale = sb("w2_scale", [P, N], U8)
         nc.scalar.copy(out=w2_stage[:].rearrange("p (m j) -> p m j", j=PACK), in_=w2_raw[:].rearrange("p j m -> p m j"))
 
-        z_rows = [sb("z_rows%d" % b, [P, H], BF16) for b in range(BLOCKS)]
-        reuse = {(0, 1): "stage1", (1, 0): "stage2", (2, 0): "stage3"}
+        z_all = sb("z_all", [P, BLOCKS * H], BF16, tag="w1_raw2_1")
+        z_rows = [z_all[:, b * H : (b + 1) * H] for b in range(BLOCKS)]
+        reuse = {(0, 1): "stage1", (1, 0): "stage2", (1, 1): "stage3"}
         terms = {}
 
         def fetch(t, d, v0, n):
@@ -179,13 +180,14 @@ def tile_picked_lapl_silu_p_kernel(
 
         def round_rows(acc, t, b):
             q = P // PACK
-            dst = z_rows[b][:].rearrange("v (u p e) -> v u p e", u=2, e=2)[:, :, q * t : q * (t + 1), :]
+            dst = z_rows[b].rearrange("v (u p e) -> v u p e", u=2, e=2)[:, :, q * t : q * (t + 1), :]
             nc.scalar.copy(out=dst, in_=acc.rearrange("v (p u e) -> v u p e", u=2, e=2))
 
-        sum_banks = [4, 1, 5]
+        sum_banks = [4, 5, 6]
         for t in range(TILES - 1):
-            if t >= 1:
-                project(t + 1)
+            if t == 1:
+                project(2)
+                project(3)
             acc = bank("sum%d" % t, sum_banks[t], V)
             for d in range(D + 1):
                 fetch(t, d, 0, V)
@@ -194,8 +196,8 @@ def tile_picked_lapl_silu_p_kernel(
             for b in range(BLOCKS):
                 round_rows(acc[:, b * P : (b + 1) * P], t, b)
 
-        last_banks = [6, 7, 7, 4]
-        back_banks = [2, 4, 1, 5]
+        last_banks = [7, 3, 7, 3]
+        back_banks = [0, 1, 2, 4]
         t = TILES - 1
         z_cols = [sb("z_cols%d" % b, [P, P * PACK], BF16) for b in range(BLOCKS)]
         for blocks in [(0, 1), (2,), (3,)]:
@@ -209,7 +211,7 @@ def tile_picked_lapl_silu_p_kernel(
                 back = bank("back%d" % b, back_banks[b], 2 * P)
                 for u in range(2):
                     nc.tensor.transpose(
-                        back[:, u * P : (u + 1) * P], z_rows[b][:].bitcast(F32)[:, u * P : (u + 1) * P], ident[:]
+                        back[:, u * P : (u + 1) * P], z_rows[b].bitcast(F32)[:, u * P : (u + 1) * P], ident[:]
                     )
                 nc.scalar.copy(
                     out=z_cols[b][:].bitcast(F32).rearrange("p (v u) -> p v u", u=2),
@@ -221,13 +223,13 @@ def tile_picked_lapl_silu_p_kernel(
         w2_code = codes[:, :N]
         nc.vector.quantize_mx(out=w2_code.bitcast(FP8X4), scales=w2_scale[:], in_=w2_stage[:])
         result = sb("result", [P, V], F32)
-        early = bank("early", 0, V - P)
-        late = bank("late", 3, P)
+        early = bank("early", 5, 2 * P)
+        prods = [early[:, :P], early[:, P:], bank("prod2", 6, P)[:], bank("prod3", 0, P)[:]]
         for b in range(BLOCKS):
             z_code = codes[:, N + b * P : N + (b + 1) * P]
             nc.vector.quantize_mx(out=z_code.bitcast(FP8X4), scales=z_scale[b][:], in_=z_cols[b][:])
             nc.tensor.matmul_mx(
-                out=early[:, b * P : (b + 1) * P] if b < BLOCKS - 1 else late[:],
+                out=prods[b],
                 lhsT=w2_code.bitcast(FP8X4),
                 lhsT_scale=w2_scale[:],
                 rhs=z_code.bitcast(FP8X4),
@@ -235,8 +237,9 @@ def tile_picked_lapl_silu_p_kernel(
                 start=True,
                 stop=True,
             )
-            if b == BLOCKS - 2:
-                nc.vector.tensor_copy(out=result[:, : V - P], in_=early[:])
-                nc.sync.dma_start(out=out[:, : V - P], in_=result[:, : V - P])
-        nc.scalar.copy(out=result[:, V - P :], in_=late[:])
-        nc.sync.dma_start(out=out[:, V - P :], in_=result[:, V - P :])
+            if b == 1:
+                nc.vector.tensor_copy(out=result[:, : 2 * P], in_=early[:])
+                nc.sync.dma_start(out=out[:, : 2 * P], in_=result[:, : 2 * P])
+        nc.vector.tensor_copy(out=result[:, 2 * P : 3 * P], in_=prods[2])
+        nc.scalar.copy(out=result[:, 3 * P :], in_=prods[3])
+        nc.sync.dma_start(out=out[:, 2 * P :], in_=result[:, 2 * P :])

@@ -45,6 +45,8 @@ def tile_picked_lapl_silu_p_kernel(
 
         scale_win = sb("scale_win", [P, T], U8)
         nc.vector.memset(scale_win[:].bitcast(I32), 0)
+        minus_one = sb("minus_one", [P, V], F32)
+        nc.vector.memset(minus_one[:], -1.0)
         warm_in = sb("warm_in", [P, 1], F32)
         warm_out = sb("warm_out", [P, 1], F32)
         nc.gpsimd.memset(warm_in[:], 0.0)
@@ -143,15 +145,17 @@ def tile_picked_lapl_silu_p_kernel(
 
         project(0)
         quantise_w1(1, nc.vector.tensor_copy)
-        neg_gate = [sb("neg_gate%d" % d, [P, V], F32) for d in range(D)]
-        for d in range(D):
-            nc.scalar.activation(out=neg_gate[d][:], in_=gate_raw[d][:], func=COPY, scale=-1.0)
         project(1)
         quantise_w1(2, nc.scalar.copy)
         quantise_w1(3, nc.scalar.copy)
         w2_stage = sb("w2_stage", [P, N * PACK], BF16)
         w2_scale = sb("w2_scale", [P, N], U8)
-        nc.scalar.copy(out=w2_stage[:].rearrange("p (m j) -> p m j", j=PACK), in_=w2_raw[:].rearrange("p j m -> p m j"))
+        nc.scalar.activation(
+            out=w2_stage[:].rearrange("p (m j) -> p m j", j=PACK),
+            in_=w2_raw[:].rearrange("p j m -> p m j"),
+            func=COPY,
+            scale=-1.0,
+        )
 
         z_all = sb("z_all", [P, BLOCKS * H], BF16, tag="w1_raw2_1")
         z_rows = [z_all[:, b * H : (b + 1) * H] for b in range(BLOCKS)]
@@ -163,10 +167,7 @@ def tile_picked_lapl_silu_p_kernel(
                 terms[t, d] = sb("term%d_%d" % (t, d), [P, V], F32, tag=reuse.get((t, d)))
             dst = terms[t, d][:, v0 : v0 + n]
             src = h[t][:].indirect(entries(lists[d], v0, n))
-            if d == 0:
-                nc.vector.tensor_copy(dst, src)
-            else:
-                nc.vector.tensor_tensor(dst, src, neg_gate[d - 1][:, v0 : v0 + n], MULT)
+            nc.vector.tensor_tensor(dst, src, ([minus_one] + gate_raw)[d][:, v0 : v0 + n], MULT)
 
         def turn_and_add(acc, t, d, b, first, last):
             nc.tensor.matmul(

@@ -44,7 +44,8 @@ def tile_picked_lapl_silu_p_kernel(
             return lst[:, start // ENTRIES_PER_COLUMN : (start + count) // ENTRIES_PER_COLUMN]
 
         scale_win = sb("scale_win", [P, T], U8)
-        nc.vector.memset(scale_win[:].bitcast(I32), 0)
+        nc.gpsimd.memset(scale_win[:, : T * 3 // 4].bitcast(I32), 0)
+        nc.vector.memset(scale_win[:, T * 3 // 4 :].bitcast(I32), 0)
         minus_one = sb("minus_one", [P, V], F32)
         nc.vector.memset(minus_one[:], -1.0)
         warm_in = sb("warm_in", [P, 1], F32)
@@ -63,91 +64,114 @@ def tile_picked_lapl_silu_p_kernel(
         for c, (c0, cw) in enumerate(chunks):
             for z in range(PASSES):
                 w1_raw[c, z] = sb("w1_raw%d_%d" % (c, z), [P, PACK, cw], F32)
-        gate_raw = [sb("gate_raw%d" % d, [P, V], F32) for d in range(D)]
+        gates = sb("gates", [P, D, V], F32)
+        gate_raw = [gates[:, d, :] for d in range(D)]
         w2_raw = sb("w2_raw", [P, PACK, N], F32)
 
         def load_words(z):
             nc.sync.dma_start(out=word_win[z][:], in_=x_words[z].rearrange("p n t -> p (n t)").bitcast(I32))
 
-        def load_w1(c):
+        def load_w1(c, z):
             c0, cw = chunks[c]
-            for z in range(PASSES):
-                rows = w1[z * P * PACK : (z + 1) * P * PACK, c0 : c0 + cw]
-                nc.sync.dma_start(out=w1_raw[c, z][:], in_=rows.rearrange("(p j) c -> p j c", j=PACK))
+            rows = w1[z * P * PACK : (z + 1) * P * PACK, c0 : c0 + cw]
+            nc.sync.dma_start(out=w1_raw[c, z][:], in_=rows.rearrange("(p j) c -> p j c", j=PACK))
 
         nc.sync.dma_start(offs_sb[:], offs)
-        nc.sync.dma_start(lists[0][:], list_src[0])
-        nc.sync.dma_start(lists[1][:], list_src[1])
         for q in range(4):
             nc.sync.dma_start(
                 out=scale_win[32 * q : 32 * q + 4 * PASSES, :].bitcast(I32),
                 in_=x_scales[:, 4 * q : 4 * q + 4, :].bitcast(I32),
             )
         load_words(0)
-        load_w1(0)
+        load_w1(0, 0)
         load_words(1)
-        load_w1(1)
-        nc.sync.dma_start(out=gate_raw[0][:], in_=gate[0])
+        load_w1(0, 1)
+        load_w1(1, 0)
+        load_w1(1, 1)
+        nc.sync.dma_start(lists[0][:], list_src[0])
+        nc.sync.dma_start(lists[1][:], list_src[1])
+        nc.sync.dma_start(out=gates[:], in_=gate.rearrange("d p v -> p d v"))
         nc.sync.dma_start(lists[2][:], list_src[2])
-        nc.sync.dma_start(out=gate_raw[1][:], in_=gate[1])
         nc.sync.dma_start(lists[3][:], list_src[3])
-        nc.sync.dma_start(out=gate_raw[2][:], in_=gate[2])
-        load_w1(2)
+        load_w1(2, 0)
+        load_w1(2, 1)
         nc.sync.dma_start(out=w2_raw[:], in_=w2.rearrange("(p j) m -> p j m", j=PACK))
 
         x_scale = sb("x_scale", [P, S], U8)
-        x_code = [sb("x_code%d" % z, [P, S], I32) for z in range(PASSES)]
+        x_early = sb("x_early", [P, S], U32)
         nc.vector.tensor_copy(x_scale[:], scale_win[:].indirect(offs_sb[:]))
-        nc.vector.tensor_copy(x_code[0][:].bitcast(U32), word_win[0][:].bitcast(U32).indirect(offs_sb[:]))
+        nc.vector.tensor_copy(x_early[:], word_win[0][:].bitcast(U32).indirect(offs_sb[:]))
 
         w1_code = [sb("w1_code%d" % t, [P, PASSES * P], U32) for t in range(TILES)]
         w1_scale = [sb("w1_scale%d" % t, [P, PASSES * P], U8) for t in range(TILES)]
 
-        def quantise_w1(t, copy):
-            c = min(t, 2)
-            first = t * P - chunks[c][0]
+        def round_w1(t, z, stage, copy):
+            if t < 2:
+                src = w1_raw[t, z][:].rearrange("p j (q e) -> p q j e", e=4)
+                dst = stage.rearrange("p (q e j) -> p q j e", e=4, j=PACK)
+            else:
+                src = w1_raw[2, z][:].rearrange("p j (q u e) -> p u q j e", u=2, e=2)[:, t - 2]
+                dst = stage.rearrange("p (q e j) -> p q j e", e=2, j=PACK)
+            copy(out=dst, in_=src)
+
+        def quantise_w1(t):
             stage = sb("w1_stage%d" % t, [P, PASSES * P * PACK], BF16, tag="stage%d" % t)
             for z in range(PASSES):
-                dst = stage[:, z * P * PACK : (z + 1) * P * PACK].rearrange("p (c j) -> p c j", j=PACK)
-                copy(out=dst, in_=w1_raw[c, z][:, :, first : first + P].rearrange("p j c -> p c j"))
+                copy = nc.vector.tensor_copy if (t, z) in [(1, 1)] else nc.scalar.copy
+                round_w1(t, z, stage[:, z * P * PACK : (z + 1) * P * PACK], copy)
             nc.vector.quantize_mx(out=w1_code[t][:].bitcast(FP8X4), scales=w1_scale[t][:], in_=stage[:])
 
-        quantise_w1(0, nc.scalar.copy)
-        first_pieces = [(0, 512), (512, 256), (768, 256)]
-        for s0, n in first_pieces:
-            nc.vector.tensor_copy(
-                x_code[1][:, s0 : s0 + n].bitcast(U32), word_win[1][:].bitcast(U32).indirect(entries(offs_sb, s0, n))
+        for z in range(PASSES):
+            stage = sb("w1_stage0_%d" % z, [P, P * PACK], BF16, tag="stage0_%d" % z)
+            round_w1(0, z, stage[:], nc.scalar.copy)
+            nc.vector.quantize_mx(
+                out=w1_code[0][:, z * P : (z + 1) * P].bitcast(FP8X4),
+                scales=w1_scale[0][:, z * P : (z + 1) * P],
+                in_=stage[:],
             )
+        gather_pieces = [(0, 768), (768, 256)]
+        half = S // 2
+        cut = gather_pieces[1][0]
+        x_late = [sb("x_late0", [P, cut], U32), sb("x_late1", [P, S - cut], U32, tag="stage0_1")]
+
+        def x_code(z, s0, n):
+            if z == 0:
+                return x_early[:, s0 : s0 + n]
+            return x_late[s0 // cut][:, s0 % cut : s0 % cut + n]
+
+        for s0, n in gather_pieces:
+            nc.vector.tensor_copy(x_code(1, s0, n), word_win[1][:].bitcast(U32).indirect(entries(offs_sb, s0, n)))
 
         h = [sb("h%d" % t, [P, S], F32) for t in range(TILES)]
-        halves = [(0, 512), (512, 512)]
-        h_banks = [(0, 1, 2), (3, 4), (0, 1), (2, 5)]
+        first_groups = [[(0, 256)], [(256, 256)], [(512, 256)], [(768, 256)]]
+        later_groups = [[(0, half)], [(half, cut - half), (cut, S - cut)]]
+        h_banks = [(0, 1, 2, 6), (3, 4), (0, 1), (2, 3)]
 
         def project(t):
-            pieces = first_pieces if t == 0 else halves
-            accs = [bank("acc%d_%d" % (t, i), h_banks[t][i], n) for i, (s0, n) in enumerate(pieces)]
-            order = [(z, i) for z in range(PASSES) for i in range(len(pieces))]
-            if t > 0:
-                order = [(z, i) for i in range(len(pieces)) for z in range(PASSES)]
-            for z, i in order:
-                s0, n = pieces[i]
+            groups = first_groups if t == 0 else later_groups
+            accs = [bank("acc%d_%d" % (t, i), h_banks[t][i], sum(n for s0, n in g)) for i, g in enumerate(groups)]
+            order = [(z, i, piece) for i, g in enumerate(groups) for piece in g for z in range(PASSES)]
+            if t == 0:
+                order = sorted(order)
+            for z, i, (s0, n) in order:
+                g0 = groups[i][0][0]
                 nc.tensor.matmul_mx(
-                    out=accs[i][:],
+                    out=accs[i][:, s0 - g0 : s0 - g0 + n],
                     lhsT=w1_code[t][:, z * P : (z + 1) * P].bitcast(FP8X4),
                     lhsT_scale=w1_scale[t][:, z * P : (z + 1) * P],
-                    rhs=x_code[z][:, s0 : s0 + n].bitcast(FP8X4),
+                    rhs=x_code(z, s0, n).bitcast(FP8X4),
                     rhs_scale=x_scale[4 * z : P, s0 : s0 + n],
                     start=(z == 0),
                     stop=(z == PASSES - 1),
                 )
-                if z == PASSES - 1:
-                    nc.scalar.activation(out=h[t][:, s0 : s0 + n], in_=accs[i][:], func=SILU)
+                if z == PASSES - 1 and (s0, n) == groups[i][-1]:
+                    nc.scalar.activation(out=h[t][:, g0 : s0 + n], in_=accs[i][:], func=SILU)
 
         project(0)
-        quantise_w1(1, nc.vector.tensor_copy)
+        quantise_w1(1)
         project(1)
-        quantise_w1(2, nc.scalar.copy)
-        quantise_w1(3, nc.scalar.copy)
+        quantise_w1(2)
+        quantise_w1(3)
         w2_stage = sb("w2_stage", [P, N * PACK], BF16)
         w2_scale = sb("w2_scale", [P, N], U8)
         nc.scalar.activation(
@@ -159,12 +183,14 @@ def tile_picked_lapl_silu_p_kernel(
 
         z_all = sb("z_all", [P, BLOCKS * H], BF16, tag="w1_raw2_1")
         z_rows = [z_all[:, b * H : (b + 1) * H] for b in range(BLOCKS)]
-        reuse = {(0, 1): "stage1", (1, 0): "stage2", (1, 1): "stage3"}
+        term_tags = ["stage1", "stage2", "stage3", None]
         terms = {}
+        for t in range(TILES):
+            four = sb("terms%d" % t, [P, (D + 1) * V], F32, tag=term_tags[t])
+            for d in range(D + 1):
+                terms[t, d] = four[:, d * V : (d + 1) * V]
 
         def fetch(t, d, v0, n):
-            if (t, d) not in terms:
-                terms[t, d] = sb("term%d_%d" % (t, d), [P, V], F32, tag=reuse.get((t, d)))
             dst = terms[t, d][:, v0 : v0 + n]
             src = h[t][:].indirect(entries(lists[d], v0, n))
             nc.vector.tensor_tensor(dst, src, ([minus_one] + gate_raw)[d][:, v0 : v0 + n], MULT)
@@ -180,9 +206,18 @@ def tile_picked_lapl_silu_p_kernel(
             )
 
         def round_rows(acc, t, b):
-            q = P // PACK
-            dst = z_rows[b].rearrange("v (u p e) -> v u p e", u=2, e=2)[:, :, q * t : q * (t + 1), :]
-            nc.scalar.copy(out=dst, in_=acc.rearrange("v (p u e) -> v u p e", u=2, e=2))
+            if t < 2:
+                q = P // PACK
+                dst = z_rows[b].rearrange("v (u p e) -> v u p e", u=2, e=2)[:, :, q * t : q * (t + 1), :]
+                nc.scalar.copy(out=dst, in_=acc.rearrange("v (p u e) -> v u p e", u=2, e=2))
+            else:
+                at = (t - 2) * 2 * P + P
+                nc.scalar.copy(out=z_rows[b][:, at : at + P], in_=acc)
+
+        def turn_back(b, u):
+            nc.tensor.transpose(
+                backs[b][:, u * P : (u + 1) * P], z_rows[b].bitcast(F32)[:, u * P : (u + 1) * P], ident[:]
+            )
 
         sum_banks = [4, 5, 6]
         for t in range(TILES - 1):
@@ -199,6 +234,9 @@ def tile_picked_lapl_silu_p_kernel(
 
         last_banks = [7, 3, 7, 3]
         back_banks = [0, 1, 2, 4]
+        backs = [bank("back%d" % b, back_banks[b], 2 * P) for b in range(BLOCKS)]
+        for b in range(BLOCKS):
+            turn_back(b, 0)
         t = TILES - 1
         z_cols = [sb("z_cols%d" % b, [P, P * PACK], BF16) for b in range(BLOCKS)]
         for blocks in [(0, 1), (2,), (3,)]:
@@ -209,14 +247,10 @@ def tile_picked_lapl_silu_p_kernel(
                     turn_and_add(accs[b][:], t, d, b, d == 0, d == D)
             for b in blocks:
                 round_rows(accs[b][:], t, b)
-                back = bank("back%d" % b, back_banks[b], 2 * P)
-                for u in range(2):
-                    nc.tensor.transpose(
-                        back[:, u * P : (u + 1) * P], z_rows[b].bitcast(F32)[:, u * P : (u + 1) * P], ident[:]
-                    )
+                turn_back(b, 1)
                 nc.scalar.copy(
                     out=z_cols[b][:].bitcast(F32).rearrange("p (v u) -> p v u", u=2),
-                    in_=back[:].rearrange("p (u v) -> p v u", u=2),
+                    in_=backs[b][:].rearrange("p (u v) -> p v u", u=2),
                 )
 
         codes = sb("codes", [P, N + V], U32, tag="h%d" % t)
@@ -224,7 +258,7 @@ def tile_picked_lapl_silu_p_kernel(
         w2_code = codes[:, :N]
         nc.vector.quantize_mx(out=w2_code.bitcast(FP8X4), scales=w2_scale[:], in_=w2_stage[:])
         result = sb("result", [P, V], F32)
-        early = bank("early", 5, 2 * P)
+        early = bank("early", 3, 2 * P)
         prods = [early[:, :P], early[:, P:], bank("prod2", 6, P)[:], bank("prod3", 0, P)[:]]
         for b in range(BLOCKS):
             z_code = codes[:, N + b * P : N + (b + 1) * P]
@@ -242,5 +276,6 @@ def tile_picked_lapl_silu_p_kernel(
                 nc.vector.tensor_copy(out=result[:, : 2 * P], in_=early[:])
                 nc.sync.dma_start(out=out[:, : 2 * P], in_=result[:, : 2 * P])
         nc.vector.tensor_copy(out=result[:, 2 * P : 3 * P], in_=prods[2])
+        nc.sync.dma_start(out=out[:, 2 * P : 3 * P], in_=result[:, 2 * P : 3 * P])
         nc.scalar.copy(out=result[:, 3 * P :], in_=prods[3])
-        nc.sync.dma_start(out=out[:, 2 * P :], in_=result[:, 2 * P :])
+        nc.sync.dma_start(out=out[:, 3 * P :], in_=result[:, 3 * P :])

@@ -44,8 +44,10 @@ def tile_picked_lapl_silu_p_kernel(
             return lst[:, start // ENTRIES_PER_COLUMN : (start + count) // ENTRIES_PER_COLUMN]
 
         scale_win = sb("scale_win", [P, T], U8)
-        nc.gpsimd.memset(scale_win[:, : T * 3 // 4].bitcast(I32), 0)
-        nc.vector.memset(scale_win[:, T * 3 // 4 :].bitcast(I32), 0)
+        nc.gpsimd.memset(scale_win[64:, :].bitcast(I32), 0)
+        nc.vector.memset(scale_win[32:64, :].bitcast(I32), 0)
+        x_plane = sb("x_plane", [P, PASSES * S], U8)
+        nc.vector.memset(x_plane[:].bitcast(I32), 0)
         minus_one = sb("minus_one", [P, V], F32)
         nc.vector.memset(minus_one[:], -1.0)
         warm_in = sb("warm_in", [P, 1], F32)
@@ -61,12 +63,8 @@ def tile_picked_lapl_silu_p_kernel(
         word_win = [sb("word_win%d" % z, [P, T], I32) for z in range(PASSES)]
         chunks = [(0, 128), (128, 128), (256, 256)]
         w1_raw = {}
-        for c, (c0, cw) in enumerate(chunks):
-            for z in range(PASSES):
-                w1_raw[c, z] = sb("w1_raw%d_%d" % (c, z), [P, PACK, cw], F32)
-        gates = sb("gates", [P, D, V], F32)
-        gate_raw = [gates[:, d, :] for d in range(D)]
-        w2_raw = sb("w2_raw", [P, PACK, N], F32)
+        for z in range(PASSES):
+            w1_raw[0, z] = sb("w1_raw0_%d" % z, [P, PACK, chunks[0][1]], F32)[:]
 
         def load_words(z):
             nc.sync.dma_start(out=word_win[z][:], in_=x_words[z].rearrange("p n t -> p (n t)").bitcast(I32))
@@ -74,43 +72,47 @@ def tile_picked_lapl_silu_p_kernel(
         def load_w1(c, z):
             c0, cw = chunks[c]
             rows = w1[z * P * PACK : (z + 1) * P * PACK, c0 : c0 + cw]
-            nc.sync.dma_start(out=w1_raw[c, z][:], in_=rows.rearrange("(p j) c -> p j c", j=PACK))
+            nc.sync.dma_start(out=w1_raw[c, z], in_=rows.rearrange("(p j) c -> p j c", j=PACK))
 
         nc.sync.dma_start(offs_sb[:], offs)
-        for q in range(4):
-            nc.sync.dma_start(
-                out=scale_win[32 * q : 32 * q + 4 * PASSES, :].bitcast(I32),
-                in_=x_scales[:, 4 * q : 4 * q + 4, :].bitcast(I32),
-            )
+        nc.sync.dma_start(
+            out=scale_win[:32, :].bitcast(I32), in_=x_scales.bitcast(I32).rearrange("z b n -> b z n")
+        )
         load_words(0)
+        for d in range(D + 1):
+            nc.sync.dma_start(lists[d][:], list_src[d])
         load_w1(0, 0)
         load_words(1)
         load_w1(0, 1)
-        load_w1(1, 0)
-        load_w1(1, 1)
-        nc.sync.dma_start(lists[0][:], list_src[0])
-        nc.sync.dma_start(lists[1][:], list_src[1])
-        nc.sync.dma_start(out=gates[:], in_=gate.rearrange("d p v -> p d v"))
-        nc.sync.dma_start(lists[2][:], list_src[2])
-        nc.sync.dma_start(lists[3][:], list_src[3])
-        load_w1(2, 0)
-        load_w1(2, 1)
-        nc.sync.dma_start(out=w2_raw[:], in_=w2.rearrange("(p j) m -> p j m", j=PACK))
 
         x_scale = sb("x_scale", [P, S], U8)
         x_early = sb("x_early", [P, S], U32)
         nc.vector.tensor_copy(x_scale[:], scale_win[:].indirect(offs_sb[:]))
         nc.vector.tensor_copy(x_early[:], word_win[0][:].bitcast(U32).indirect(offs_sb[:]))
+        for q in range(4):
+            nc.sync.dma_start(
+                out=x_plane[32 * q : 32 * q + 4, :].bitcast(I32).rearrange("p (z n) -> p z n", z=PASSES),
+                in_=x_scale[8 * q : 8 * q + 8, :].bitcast(I32),
+            )
 
         w1_code = [sb("w1_code%d" % t, [P, PASSES * P], U32) for t in range(TILES)]
         w1_scale = [sb("w1_scale%d" % t, [P, PASSES * P], U8) for t in range(TILES)]
 
+        def late_w1(c, tag):
+            cw = chunks[c][1]
+            both = sb("w1_raw%d" % c, [P, PASSES * PACK * cw], F32, tag=tag)
+            for z in range(PASSES):
+                w1_raw[c, z] = both[:, z * PACK * cw : (z + 1) * PACK * cw].rearrange("p (j c) -> p j c", j=PACK)
+                load_w1(c, z)
+
+        late_w1(1, "scale_win")
+
         def round_w1(t, z, stage, copy):
             if t < 2:
-                src = w1_raw[t, z][:].rearrange("p j (q e) -> p q j e", e=4)
+                src = w1_raw[t, z].rearrange("p j (q e) -> p q j e", e=4)
                 dst = stage.rearrange("p (q e j) -> p q j e", e=4, j=PACK)
             else:
-                src = w1_raw[2, z][:].rearrange("p j (q u e) -> p u q j e", u=2, e=2)[:, t - 2]
+                src = w1_raw[2, z].rearrange("p j (q u e) -> p u q j e", u=2, e=2)[:, t - 2]
                 dst = stage.rearrange("p (q e j) -> p q j e", e=2, j=PACK)
             copy(out=dst, in_=src)
 
@@ -129,6 +131,12 @@ def tile_picked_lapl_silu_p_kernel(
                 scales=w1_scale[0][:, z * P : (z + 1) * P],
                 in_=stage[:],
             )
+        gates = sb("gates", [P, D, V], F32, tag="w1_raw0_0")
+        gate_raw = [gates[:, d, :] for d in range(D)]
+        nc.sync.dma_start(out=gates[:], in_=gate.rearrange("d p v -> p d v"))
+        late_w1(2, "word_win0")
+        w2_raw = sb("w2_raw", [P, PACK, N], F32, tag="w1_raw0_1")
+        nc.sync.dma_start(out=w2_raw[:], in_=w2.rearrange("(p j) m -> p j m", j=PACK))
         gather_pieces = [(0, 768), (768, 256)]
         half = S // 2
         cut = gather_pieces[1][0]
@@ -160,7 +168,7 @@ def tile_picked_lapl_silu_p_kernel(
                     lhsT=w1_code[t][:, z * P : (z + 1) * P].bitcast(FP8X4),
                     lhsT_scale=w1_scale[t][:, z * P : (z + 1) * P],
                     rhs=x_code(z, s0, n).bitcast(FP8X4),
-                    rhs_scale=x_scale[4 * z : P, s0 : s0 + n],
+                    rhs_scale=x_plane[:, z * S + s0 : z * S + s0 + n],
                     start=(z == 0),
                     stop=(z == PASSES - 1),
                 )
@@ -181,7 +189,7 @@ def tile_picked_lapl_silu_p_kernel(
             scale=-1.0,
         )
 
-        z_all = sb("z_all", [P, BLOCKS * H], BF16, tag="w1_raw2_1")
+        z_all = sb("z_all", [P, BLOCKS * H], BF16, tag="word_win0")
         z_rows = [z_all[:, b * H : (b + 1) * H] for b in range(BLOCKS)]
         term_tags = ["stage1", "stage2", "stage3", None]
         terms = {}

@@ -63,8 +63,7 @@ def tile_picked_lapl_silu_p_kernel(
         word_win = [sb("word_win%d" % z, [P, T], I32) for z in range(PASSES)]
         chunks = [(0, 128), (128, 128), (256, 256)]
         w1_raw = {}
-        for z in range(PASSES):
-            w1_raw[0, z] = sb("w1_raw0_%d" % z, [P, PACK, chunks[0][1]], F32)[:]
+        w1_raw[0, 0] = sb("w1_raw0_0", [P, PACK, chunks[0][1]], F32)[:]
 
         def load_words(z):
             nc.sync.dma_start(out=word_win[z][:], in_=x_words[z].rearrange("p n t -> p (n t)").bitcast(I32))
@@ -83,7 +82,6 @@ def tile_picked_lapl_silu_p_kernel(
             nc.sync.dma_start(lists[d][:], list_src[d])
         load_w1(0, 0)
         load_words(1)
-        load_w1(0, 1)
 
         x_scale = sb("x_scale", [P, S], U8)
         x_early = sb("x_early", [P, S], U32)
@@ -95,17 +93,21 @@ def tile_picked_lapl_silu_p_kernel(
                 in_=x_scale[8 * q : 8 * q + 8, :].bitcast(I32),
             )
 
-        w1_code = [sb("w1_code%d" % t, [P, PASSES * P], U32) for t in range(TILES)]
-        w1_scale = [sb("w1_scale%d" % t, [P, PASSES * P], U8) for t in range(TILES)]
+        upper_code = sb("upper_code", [P, 2 * PASSES * P], U32)
+        upper_scale = sb("upper_scale", [P, 2 * PASSES * P], U8)
+        w1_code = [sb("w1_code%d" % t, [P, PASSES * P], U32) for t in range(2)]
+        w1_scale = [sb("w1_scale%d" % t, [P, PASSES * P], U8) for t in range(2)]
+        w1_code.extend([upper_code[:, : PASSES * P], upper_code[:, PASSES * P :]])
+        w1_scale.extend([upper_scale[:, : PASSES * P], upper_scale[:, PASSES * P :]])
 
-        def late_w1(c, tag):
-            cw = chunks[c][1]
-            both = sb("w1_raw%d" % c, [P, PASSES * PACK * cw], F32, tag=tag)
-            for z in range(PASSES):
-                w1_raw[c, z] = both[:, z * PACK * cw : (z + 1) * PACK * cw].rearrange("p (j c) -> p j c", j=PACK)
+        def late_w1(parts, tag):
+            width = PACK * chunks[parts[0][0]][1]
+            room = sb("w1_late_" + tag, [P, len(parts) * width], F32, tag=tag)
+            for i, (c, z) in enumerate(parts):
+                w1_raw[c, z] = room[:, i * width : (i + 1) * width].rearrange("p (j c) -> p j c", j=PACK)
                 load_w1(c, z)
 
-        late_w1(1, "scale_win")
+        late_w1([(0, 1)], "scale_win")
 
         def round_w1(t, z, stage, copy):
             if t < 2:
@@ -131,16 +133,16 @@ def tile_picked_lapl_silu_p_kernel(
                 scales=w1_scale[0][:, z * P : (z + 1) * P],
                 in_=stage[:],
             )
-        gates = sb("gates", [P, D, V], F32, tag="w1_raw0_0")
+        late_w1([(1, 0), (1, 1)], "w1_raw0_0")
+        gates = sb("gates", [P, D, V], F32, tag="word_win0")
         gate_raw = [gates[:, d, :] for d in range(D)]
         nc.sync.dma_start(out=gates[:], in_=gate.rearrange("d p v -> p d v"))
-        late_w1(2, "word_win0")
-        w2_raw = sb("w2_raw", [P, PACK, N], F32, tag="w1_raw0_1")
+        w2_raw = sb("w2_raw", [P, PACK, N], F32, tag="x_scale")
         nc.sync.dma_start(out=w2_raw[:], in_=w2.rearrange("(p j) m -> p j m", j=PACK))
         gather_pieces = [(0, 768), (768, 256)]
         half = S // 2
         cut = gather_pieces[1][0]
-        x_late = [sb("x_late0", [P, cut], U32), sb("x_late1", [P, S - cut], U32, tag="stage0_1")]
+        x_late = [sb("x_late0", [P, cut], U32), sb("x_late1", [P, S - cut], U32, tag="scale_win")]
 
         def x_code(z, s0, n):
             if z == 0:
@@ -150,6 +152,7 @@ def tile_picked_lapl_silu_p_kernel(
         for s0, n in gather_pieces:
             nc.vector.tensor_copy(x_code(1, s0, n), word_win[1][:].bitcast(U32).indirect(entries(offs_sb, s0, n)))
 
+        late_w1([(2, 0), (2, 1)], "word_win1")
         h = [sb("h%d" % t, [P, S], F32) for t in range(TILES)]
         first_groups = [[(0, 256)], [(256, 256)], [(512, 256)], [(768, 256)]]
         later_groups = [[(0, half)], [(half, cut - half), (cut, S - cut)]]
@@ -178,8 +181,12 @@ def tile_picked_lapl_silu_p_kernel(
         project(0)
         quantise_w1(1)
         project(1)
-        quantise_w1(2)
-        quantise_w1(3)
+        upper_stage = sb("upper_stage", [P, 2 * PASSES * P * PACK], BF16)
+        for t in (2, 3):
+            for z in range(PASSES):
+                at = ((t - 2) * PASSES + z) * P * PACK
+                round_w1(t, z, upper_stage[:, at : at + P * PACK], nc.scalar.copy)
+        nc.vector.quantize_mx(out=upper_code[:].bitcast(FP8X4), scales=upper_scale[:], in_=upper_stage[:])
         w2_stage = sb("w2_stage", [P, N * PACK], BF16)
         w2_scale = sb("w2_scale", [P, N], U8)
         nc.scalar.activation(
@@ -189,14 +196,15 @@ def tile_picked_lapl_silu_p_kernel(
             scale=-1.0,
         )
 
-        z_all = sb("z_all", [P, BLOCKS * H], BF16, tag="word_win0")
+        z_all = sb("z_all", [P, BLOCKS * H], BF16, tag="upper_stage")
         z_rows = [z_all[:, b * H : (b + 1) * H] for b in range(BLOCKS)]
-        term_tags = ["stage1", "stage2", "stage3", None]
+        term_tags = {(0, 0): "w1_raw0_0", (1, 1): "word_win1"}
         terms = {}
         for t in range(TILES):
-            four = sb("terms%d" % t, [P, (D + 1) * V], F32, tag=term_tags[t])
-            for d in range(D + 1):
-                terms[t, d] = four[:, d * V : (d + 1) * V]
+            for d0, d1 in [(0, 1), (1, D + 1)] if t == 1 else [(0, D + 1)]:
+                room = sb("terms%d_%d" % (t, d0), [P, (d1 - d0) * V], F32, tag=term_tags.get((t, d0)))
+                for d in range(d0, d1):
+                    terms[t, d] = room[:, (d - d0) * V : (d - d0 + 1) * V]
 
         def fetch(t, d, v0, n):
             dst = terms[t, d][:, v0 : v0 + n]

@@ -137,8 +137,6 @@ def tile_picked_lapl_silu_p_kernel(
         gates = sb("gates", [P, D, V], F32, tag="word_win0")
         gate_raw = [gates[:, d, :] for d in range(D)]
         nc.sync.dma_start(out=gates[:], in_=gate.rearrange("d p v -> p d v"))
-        w2_raw = sb("w2_raw", [P, PACK, N], F32, tag="x_scale")
-        nc.sync.dma_start(out=w2_raw[:], in_=w2.rearrange("(p j) m -> p j m", j=PACK))
         gather_pieces = [(0, 768), (768, 256)]
         half = S // 2
         cut = gather_pieces[1][0]
@@ -180,6 +178,8 @@ def tile_picked_lapl_silu_p_kernel(
 
         project(0)
         quantise_w1(1)
+        w2_raw = sb("w2_raw", [P, PACK, N], F32, tag="stage1")
+        nc.sync.dma_start(out=w2_raw[:], in_=w2.rearrange("(p j) m -> p j m", j=PACK))
         project(1)
         upper_stage = sb("upper_stage", [P, 2 * PASSES * P * PACK], BF16)
         for t in (2, 3):
@@ -248,50 +248,62 @@ def tile_picked_lapl_silu_p_kernel(
             for b in range(BLOCKS):
                 round_rows(acc[:, b * P : (b + 1) * P], t, b)
 
-        last_banks = [7, 3, 7, 3]
-        back_banks = [0, 1, 2, 4]
-        backs = [bank("back%d" % b, back_banks[b], 2 * P) for b in range(BLOCKS)]
+        t = TILES - 1
+        groups = [(0, 1), (2,), (3,)]
+        back_tiles = [bank("back%d" % g, g, len(blocks) * 2 * P) for g, blocks in enumerate(groups)]
+        backs = [back_tiles[0][:, : 2 * P], back_tiles[0][:, 2 * P :], back_tiles[1][:], back_tiles[2][:]]
         for b in range(BLOCKS):
             turn_back(b, 0)
-        t = TILES - 1
-        z_cols = [sb("z_cols%d" % b, [P, P * PACK], BF16) for b in range(BLOCKS)]
-        for blocks in [(0, 1), (2,), (3,)]:
-            accs = {b: bank("last%d" % b, last_banks[b], P) for b in blocks}
-            for d in range(D + 1):
+        last_banks = [7, 3, 5]
+        lasts = [bank("last%d" % g, last_banks[g], len(blocks) * P) for g, blocks in enumerate(groups)]
+        z_cols = [sb("z_cols%d" % g, [P, len(blocks) * P * PACK], BF16) for g, blocks in enumerate(groups)]
+        whole = 2
+
+        def add_group(g, d):
+            for i, b in enumerate(groups[g]):
+                first = d == 0 and i == 0
+                last = d == D and i == len(groups[g]) - 1
+                turn_and_add(lasts[g][:, i * P : (i + 1) * P], t, d, b, first, last)
+
+        for d in range(whole):
+            fetch(t, d, 0, V)
+            for g in range(len(groups)):
+                add_group(g, d)
+        for g, blocks in enumerate(groups):
+            for d in range(whole, D + 1):
                 fetch(t, d, blocks[0] * P, len(blocks) * P)
-                for b in blocks:
-                    turn_and_add(accs[b][:], t, d, b, d == 0, d == D)
+                add_group(g, d)
+            rows = z_all[:].rearrange("v (b c) -> v b c", b=BLOCKS)[:, blocks[0] : blocks[-1] + 1, 3 * P :]
+            nc.scalar.copy(out=rows, in_=lasts[g][:].rearrange("v (b c) -> v b c", c=P))
             for b in blocks:
-                round_rows(accs[b][:], t, b)
                 turn_back(b, 1)
-                nc.scalar.copy(
-                    out=z_cols[b][:].bitcast(F32).rearrange("p (v u) -> p v u", u=2),
-                    in_=backs[b][:].rearrange("p (u v) -> p v u", u=2),
-                )
+            copy = nc.vector.tensor_copy if g == 0 else nc.scalar.copy
+            copy(
+                out=z_cols[g][:].bitcast(F32).rearrange("p (b v u) -> p b v u", u=2, v=P),
+                in_=back_tiles[g][:].rearrange("p (b u v) -> p b v u", u=2, v=P),
+            )
 
         codes = sb("codes", [P, N + V], U32, tag="h%d" % t)
-        z_scale = [sb("z_scale%d" % b, [P, P], U8) for b in range(BLOCKS)]
+        z_scale = [sb("z_scale%d" % g, [P, len(blocks) * P], U8) for g, blocks in enumerate(groups)]
         w2_code = codes[:, :N]
         nc.vector.quantize_mx(out=w2_code.bitcast(FP8X4), scales=w2_scale[:], in_=w2_stage[:])
         result = sb("result", [P, V], F32)
-        early = bank("early", 3, 2 * P)
-        prods = [early[:, :P], early[:, P:], bank("prod2", 6, P)[:], bank("prod3", 0, P)[:]]
-        for b in range(BLOCKS):
-            z_code = codes[:, N + b * P : N + (b + 1) * P]
-            nc.vector.quantize_mx(out=z_code.bitcast(FP8X4), scales=z_scale[b][:], in_=z_cols[b][:])
+        prods = [bank("prod0", 4, 2 * P)[:], bank("prod1", 7, P)[:], bank("prod2", 6, P)[:]]
+        for g, blocks in enumerate(groups):
+            z_code = codes[:, N + blocks[0] * P : N + (blocks[-1] + 1) * P]
+            nc.vector.quantize_mx(out=z_code.bitcast(FP8X4), scales=z_scale[g][:], in_=z_cols[g][:])
             nc.tensor.matmul_mx(
-                out=prods[b],
+                out=prods[g],
                 lhsT=w2_code.bitcast(FP8X4),
                 lhsT_scale=w2_scale[:],
                 rhs=z_code.bitcast(FP8X4),
-                rhs_scale=z_scale[b][:],
+                rhs_scale=z_scale[g][:],
                 start=True,
                 stop=True,
             )
-            if b == 1:
-                nc.vector.tensor_copy(out=result[:, : 2 * P], in_=early[:])
-                nc.sync.dma_start(out=out[:, : 2 * P], in_=result[:, : 2 * P])
-        nc.vector.tensor_copy(out=result[:, 2 * P : 3 * P], in_=prods[2])
+        nc.scalar.copy(out=result[:, : 2 * P], in_=prods[0])
+        nc.sync.dma_start(out=out[:, : 2 * P], in_=result[:, : 2 * P])
+        nc.vector.tensor_copy(out=result[:, 2 * P : 3 * P], in_=prods[1])
         nc.sync.dma_start(out=out[:, 2 * P : 3 * P], in_=result[:, 2 * P : 3 * P])
-        nc.scalar.copy(out=result[:, 3 * P :], in_=prods[3])
+        nc.scalar.copy(out=result[:, 3 * P :], in_=prods[2])
         nc.sync.dma_start(out=out[:, 3 * P :], in_=result[:, 3 * P :])

@@ -134,7 +134,7 @@ def tile_picked_lapl_silu_p_kernel(
                 in_=stage[:],
             )
         late_w1([(1, 0), (1, 1)], "w1_raw0_0")
-        gates = sb("gates", [P, D, V], F32, tag="word_win0")
+        gates = sb("gates", [P, D, V], F32, tag="stage0_0")
         gate_raw = [gates[:, d, :] for d in range(D)]
         nc.sync.dma_start(out=gates[:], in_=gate.rearrange("d p v -> p d v"))
         gather_pieces = [(0, 768), (768, 256)]
@@ -150,7 +150,7 @@ def tile_picked_lapl_silu_p_kernel(
         for s0, n in gather_pieces:
             nc.vector.tensor_copy(x_code(1, s0, n), word_win[1][:].bitcast(U32).indirect(entries(offs_sb, s0, n)))
 
-        late_w1([(2, 0), (2, 1)], "word_win1")
+        late_w1([(2, 0), (2, 1)], "x_scale")
         h = [sb("h%d" % t, [P, S], F32) for t in range(TILES)]
         first_groups = [[(0, 256)], [(256, 256)], [(512, 256)], [(768, 256)]]
         later_groups = [[(0, half)], [(half, cut - half), (cut, S - cut)]]
@@ -186,7 +186,11 @@ def tile_picked_lapl_silu_p_kernel(
             for z in range(PASSES):
                 at = ((t - 2) * PASSES + z) * P * PACK
                 round_w1(t, z, upper_stage[:, at : at + P * PACK], nc.scalar.copy)
-        nc.vector.quantize_mx(out=upper_code[:].bitcast(FP8X4), scales=upper_scale[:], in_=upper_stage[:])
+        for t in (2, 3):
+            at = (t - 2) * PASSES * P * PACK
+            nc.vector.quantize_mx(
+                out=w1_code[t].bitcast(FP8X4), scales=w1_scale[t], in_=upper_stage[:, at : at + PASSES * P * PACK]
+            )
         w2_stage = sb("w2_stage", [P, N * PACK], BF16)
         w2_scale = sb("w2_scale", [P, N], U8)
         nc.scalar.activation(
@@ -198,7 +202,7 @@ def tile_picked_lapl_silu_p_kernel(
 
         z_all = sb("z_all", [P, BLOCKS * H], BF16, tag="upper_stage")
         z_rows = [z_all[:, b * H : (b + 1) * H] for b in range(BLOCKS)]
-        term_tags = {(0, 0): "w1_raw0_0", (1, 1): "word_win1"}
+        term_tags = {(0, 0): "w1_raw0_0", (1, 1): "x_scale"}
         terms = {}
         for t in range(TILES):
             for d0, d1 in [(0, 1), (1, D + 1)] if t == 1 else [(0, D + 1)]:

@@ -16,6 +16,8 @@ FP8X4 = mybir.dt.float8_e4m3fn_x4
 SILU = mybir.ActivationFunctionType.Silu
 COPY = mybir.ActivationFunctionType.Copy
 MULT = mybir.AluOpType.mult
+ADD = mybir.AluOpType.add
+SUBTRACT = mybir.AluOpType.subtract
 
 P = 128
 PACK = 4
@@ -50,6 +52,8 @@ def tile_picked_lapl_silu_p_kernel(
         nc.vector.memset(x_plane[:].bitcast(I32), 0)
         minus_one = sb("minus_one", [P, V], F32)
         nc.vector.memset(minus_one[:], -1.0)
+        minus = sb("minus", [P, 2 * P], F32)
+        nc.gpsimd.memset(minus[:, :P], 0.0)
         warm_in = sb("warm_in", [P, 1], F32)
         warm_out = sb("warm_out", [P, 1], F32)
         nc.gpsimd.memset(warm_in[:], 0.0)
@@ -61,17 +65,21 @@ def tile_picked_lapl_silu_p_kernel(
         lists = [held.tile([P, V // 16], U16, name="list%d" % d) for d in range(D + 1)]
         list_src = [cen, pos1, pos2, pos3]
         word_win = [sb("word_win%d" % z, [P, T], I32) for z in range(PASSES)]
-        chunks = [(0, 128), (128, 128), (256, 256)]
+        chunks = [(0, 176), (176, 336), (336, 512)]
+        pitch = 6 * 32
         w1_raw = {}
-        w1_raw[0, 0] = sb("w1_raw0_0", [P, PACK, chunks[0][1]], F32)[:]
+        w1_raw[0, 0] = sb("w1_raw0_0", [P, PACK, pitch], F32)[:]
 
         def load_words(z):
             nc.sync.dma_start(out=word_win[z][:], in_=x_words[z].rearrange("p n t -> p (n t)").bitcast(I32))
 
         def load_w1(c, z):
-            c0, cw = chunks[c]
-            rows = w1[z * P * PACK : (z + 1) * P * PACK, c0 : c0 + cw]
-            nc.sync.dma_start(out=w1_raw[c, z], in_=rows.rearrange("(p j) c -> p j c", j=PACK))
+            c0, c1 = chunks[c]
+            rows = w1[z * P * PACK : (z + 1) * P * PACK, c0:c1]
+            at = c0 % 32
+            nc.sync.dma_start(
+                out=w1_raw[c, z][:, :, at : at + c1 - c0], in_=rows.rearrange("(p j) c -> p j c", j=PACK)
+            )
 
         nc.sync.dma_start(offs_sb[:], offs)
         nc.sync.dma_start(
@@ -101,7 +109,7 @@ def tile_picked_lapl_silu_p_kernel(
         w1_scale.extend([upper_scale[:, : PASSES * P], upper_scale[:, PASSES * P :]])
 
         def late_w1(parts, tag):
-            width = PACK * chunks[parts[0][0]][1]
+            width = PACK * pitch
             room = sb("w1_late_" + tag, [P, len(parts) * width], F32, tag=tag)
             for i, (c, z) in enumerate(parts):
                 w1_raw[c, z] = room[:, i * width : (i + 1) * width].rearrange("p (j c) -> p j c", j=PACK)
@@ -109,30 +117,43 @@ def tile_picked_lapl_silu_p_kernel(
 
         late_w1([(0, 1)], "scale_win")
 
-        def round_w1(t, z, stage, copy):
-            if t < 2:
-                src = w1_raw[t, z].rearrange("p j (q e) -> p q j e", e=4)
-                dst = stage.rearrange("p (q e j) -> p q j e", e=4, j=PACK)
-            else:
-                src = w1_raw[2, z].rearrange("p j (q u e) -> p u q j e", u=2, e=2)[:, t - 2]
-                dst = stage.rearrange("p (q e j) -> p q j e", e=2, j=PACK)
-            copy(out=dst, in_=src)
+        pieces = [
+            [(0, 0, 0, 6, 0, 16), (96, 0, 0, 4, 16, 8)],
+            [(0, 0, 4, 5, 16, 8), (8, 1, 0, 5, 16, 8), (48, 1, 1, 6, 0, 16)],
+            [(0, 2, 1, 6, 0, 16), (80, 2, 0, 6, 16, 8)],
+            [(0, 0, 0, 5, 24, 8), (40, 1, 0, 5, 24, 8), (80, 2, 0, 6, 24, 8)],
+        ]
+        first_stage = [sb("w1_stage0_%d" % z, [P, P * PACK], BF16, tag="stage0_%d" % z) for z in range(PASSES)]
+        second_stage = sb("w1_stage1", [P, PASSES * P * PACK], BF16, tag="stage1")
+        upper_stage = sb("upper_stage", [P, 2 * PASSES * P * PACK], BF16)
 
-        def quantise_w1(t):
-            stage = sb("w1_stage%d" % t, [P, PASSES * P * PACK], BF16, tag="stage%d" % t)
-            for z in range(PASSES):
-                copy = nc.vector.tensor_copy if (t, z) in [(1, 1)] else nc.scalar.copy
-                round_w1(t, z, stage[:, z * P * PACK : (z + 1) * P * PACK], copy)
-            nc.vector.quantize_mx(out=w1_code[t][:].bitcast(FP8X4), scales=w1_scale[t][:], in_=stage[:])
+        def stage_of(t, z):
+            if t == 0:
+                return first_stage[z][:]
+            if t == 1:
+                return second_stage[:, z * P * PACK : (z + 1) * P * PACK]
+            at = ((t - 2) * PASSES + z) * P * PACK
+            return upper_stage[:, at : at + P * PACK]
+
+        def round_w1(t, z, chunk, copy):
+            for m0, c, o0, o1, r0, n in pieces[t]:
+                if c == chunk:
+                    src = w1_raw[c, z].rearrange("p j (o q e) -> p q o j e", q=8, e=4)
+                    dst = stage_of(t, z)[:, m0 * PACK : (m0 + (o1 - o0) * n) * PACK]
+                    copy(
+                        out=dst.rearrange("p (o q e j) -> p q o j e", q=n // 4, e=4, j=PACK),
+                        in_=src[:, r0 // 4 : (r0 + n) // 4, o0:o1],
+                    )
 
         for z in range(PASSES):
-            stage = sb("w1_stage0_%d" % z, [P, P * PACK], BF16, tag="stage0_%d" % z)
-            round_w1(0, z, stage[:], nc.scalar.copy)
+            round_w1(0, z, 0, nc.scalar.copy)
             nc.vector.quantize_mx(
                 out=w1_code[0][:, z * P : (z + 1) * P].bitcast(FP8X4),
                 scales=w1_scale[0][:, z * P : (z + 1) * P],
-                in_=stage[:],
+                in_=first_stage[z][:],
             )
+            round_w1(1, z, 0, nc.scalar.copy)
+            round_w1(3, z, 0, nc.scalar.copy)
         late_w1([(1, 0), (1, 1)], "w1_raw0_0")
         gates = sb("gates", [P, D, V], F32, tag="stage0_0")
         gate_raw = [gates[:, d, :] for d in range(D)]
@@ -154,7 +175,7 @@ def tile_picked_lapl_silu_p_kernel(
         h = [sb("h%d" % t, [P, S], F32) for t in range(TILES)]
         first_groups = [[(0, 256)], [(256, 256)], [(512, 256)], [(768, 256)]]
         later_groups = [[(0, half)], [(half, cut - half), (cut, S - cut)]]
-        h_banks = [(0, 1, 2, 6), (3, 4), (0, 1), (2, 3)]
+        h_banks = [(0, 1, 2, 3), (0, 1), (2, 3), (0, 1)]
 
         def project(t):
             groups = first_groups if t == 0 else later_groups
@@ -177,15 +198,20 @@ def tile_picked_lapl_silu_p_kernel(
                     nc.scalar.activation(out=h[t][:, g0 : s0 + n], in_=accs[i][:], func=SILU)
 
         project(0)
-        quantise_w1(1)
-        w2_raw = sb("w2_raw", [P, PACK, N], F32, tag="stage1")
-        nc.sync.dma_start(out=w2_raw[:], in_=w2.rearrange("(p j) m -> p j m", j=PACK))
+        round_w1(1, 0, 1, nc.scalar.copy)
+        round_w1(1, 1, 1, nc.vector.tensor_copy)
+        nc.vector.quantize_mx(out=w1_code[1][:].bitcast(FP8X4), scales=w1_scale[1][:], in_=second_stage[:])
+        w2_raw = sb("w2_raw", [P, PACK * N], F32, tag="stage0_1")
+        for j in range(PACK):
+            nc.sync.dma_start(
+                out=w2_raw[:, j * N : (j + 1) * N], in_=w2.rearrange("(o j i) m -> j o i m", j=PACK, i=8)[j]
+            )
         project(1)
-        upper_stage = sb("upper_stage", [P, 2 * PASSES * P * PACK], BF16)
+        for z in range(PASSES):
+            round_w1(3, z, 1, nc.scalar.copy)
         for t in (2, 3):
             for z in range(PASSES):
-                at = ((t - 2) * PASSES + z) * P * PACK
-                round_w1(t, z, upper_stage[:, at : at + P * PACK], nc.scalar.copy)
+                round_w1(t, z, 2, nc.scalar.copy)
         for t in (2, 3):
             at = (t - 2) * PASSES * P * PACK
             nc.vector.quantize_mx(
@@ -195,119 +221,153 @@ def tile_picked_lapl_silu_p_kernel(
         w2_scale = sb("w2_scale", [P, N], U8)
         nc.scalar.activation(
             out=w2_stage[:].rearrange("p (m j) -> p m j", j=PACK),
-            in_=w2_raw[:].rearrange("p j m -> p m j"),
+            in_=w2_raw[:].rearrange("p (j m) -> p m j", j=PACK),
             func=COPY,
             scale=-1.0,
         )
 
-        z_all = sb("z_all", [P, BLOCKS * H], BF16, tag="upper_stage")
-        z_rows = [z_all[:, b * H : (b + 1) * H] for b in range(BLOCKS)]
-        term_tags = {(0, 0): "w1_raw0_0", (1, 1): "x_scale"}
+        direct = BLOCKS - 1
+        z_rows = [sb("z_rows%d" % b, [P, H], BF16) for b in range(direct)]
+        z_rows.append(sb("direct_pairs", [P, 2 * P], BF16))
+        direct_third = sb("direct_third", [P, P], F32)
         terms = {}
-        for t in range(TILES):
-            for d0, d1 in [(0, 1), (1, D + 1)] if t == 1 else [(0, D + 1)]:
-                room = sb("terms%d_%d" % (t, d0), [P, (d1 - d0) * V], F32, tag=term_tags.get((t, d0)))
-                for d in range(d0, d1):
-                    terms[t, d] = room[:, (d - d0) * V : (d - d0 + 1) * V]
+
+        def term_room(t, d0, d1, width, tag, spare=0):
+            room = sb("terms%d_%d" % (t, d0), [P, (d1 - d0) * width + spare], F32, tag=tag)
+            for d in range(d0, d1):
+                terms[t, d] = room[:, (d - d0) * width : (d - d0 + 1) * width]
+            return room[:, (d1 - d0) * width :]
+
+        term_room(0, 0, D + 1, V, "stage1")
+        term_room(1, 0, 1, V, None)
+        term_room(1, 1, D + 1, V, "x_scale")
+        term_room(2, 0, D + 1, V, None)
+        term_room(3, 0, 2, direct * P, None)
+        factors = [minus_one] + gate_raw
+        sums = [bank("sum%d" % b, 4 + b, H) for b in range(BLOCKS)]
 
         def fetch(t, d, v0, n):
-            dst = terms[t, d][:, v0 : v0 + n]
             src = h[t][:].indirect(entries(lists[d], v0, n))
-            nc.vector.tensor_tensor(dst, src, ([minus_one] + gate_raw)[d][:, v0 : v0 + n], MULT)
+            nc.vector.tensor_tensor(terms[t, d][:, v0 : v0 + n], src, factors[d][:, v0 : v0 + n], MULT)
 
-        def turn_and_add(acc, t, d, b, first, last):
+        def turn_and_add(t, d, b):
             nc.tensor.matmul(
-                out=acc,
+                out=sums[b][:, t * P : (t + 1) * P],
                 lhsT=terms[t, d][:, b * P : (b + 1) * P],
                 rhs=ident[:],
                 is_transpose=True,
-                start=first,
-                stop=last,
+                start=(d == 0),
+                stop=(d == D),
             )
 
-        def round_rows(acc, t, b):
-            if t < 2:
-                q = P // PACK
-                dst = z_rows[b].rearrange("v (u p e) -> v u p e", u=2, e=2)[:, :, q * t : q * (t + 1), :]
-                nc.scalar.copy(out=dst, in_=acc.rearrange("v (p u e) -> v u p e", u=2, e=2))
-            else:
-                at = (t - 2) * 2 * P + P
-                nc.scalar.copy(out=z_rows[b][:, at : at + P], in_=acc)
+        block_order = [direct] + list(range(direct))
+        third_runs = [(0, 80, 96), (80, P, 336)]
+        pair_runs = [(0, 0, 6), (P + 48, 6, 11), (2 * P, 11, 16)]
+
+        def round_pairs(t, b):
+            at, o0, o1 = pair_runs[t]
+            src = sums[b][:, at : at + 16 * (o1 - o0)]
+            nc.scalar.copy(
+                out=z_rows[b][:, 16 * o0 : 16 * o1].rearrange("v (o i e) -> v o i e", i=8, e=2),
+                in_=src.rearrange("v (o e i) -> v o i e", i=8, e=2),
+            )
+
+        def round_upper(b):
+            low = sums[b][:, :480].rearrange("v (a w) -> v w a", w=96)[:, :80, 1:5:3]
+            nc.scalar.copy(out=z_rows[b][:, 2 * P : 2 * P + 160].rearrange("v (p e) -> v p e", e=2), in_=low)
+            high = sums[b][:, 2 * P :].rearrange("v (e c) -> v c e", e=2)[:, 80:]
+            nc.scalar.copy(out=z_rows[b][:, 2 * P + 160 :].rearrange("v (p e) -> v p e", e=2), in_=high)
 
         def turn_back(b, u):
             nc.tensor.transpose(
-                backs[b][:, u * P : (u + 1) * P], z_rows[b].bitcast(F32)[:, u * P : (u + 1) * P], ident[:]
+                backs[b][:, u * P : (u + 1) * P], z_rows[b][:].bitcast(F32)[:, u * P : (u + 1) * P], ident[:]
             )
 
-        sum_banks = [4, 5, 6]
         for t in range(TILES - 1):
             if t == 1:
                 project(2)
                 project(3)
-            acc = bank("sum%d" % t, sum_banks[t], V)
             for d in range(D + 1):
                 fetch(t, d, 0, V)
-                for b in range(BLOCKS):
-                    turn_and_add(acc[:, b * P : (b + 1) * P], t, d, b, d == 0 and b == 0, d == D and b == BLOCKS - 1)
-            for b in range(BLOCKS):
-                round_rows(acc[:, b * P : (b + 1) * P], t, b)
+                for b in block_order:
+                    turn_and_add(t, d, b)
+            if t > 0:
+                p0, p1, at = third_runs[t - 1]
+                nc.scalar.copy(out=direct_third[:, p0:p1], in_=sums[direct][:, at : at + p1 - p0])
+            for b in block_order:
+                round_pairs(t, b)
 
         t = TILES - 1
-        groups = [(0, 1), (2,), (3,)]
-        back_tiles = [bank("back%d" % g, g, len(blocks) * 2 * P) for g, blocks in enumerate(groups)]
-        backs = [back_tiles[0][:, : 2 * P], back_tiles[0][:, 2 * P :], back_tiles[1][:], back_tiles[2][:]]
-        for b in range(BLOCKS):
+        groups = [(0, 1), (2,)]
+        back_tiles = [bank("back%d" % g, 2 + g, len(blocks) * 2 * P) for g, blocks in enumerate(groups)]
+        backs = [back_tiles[0][:, : 2 * P], back_tiles[0][:, 2 * P :], back_tiles[1][:]]
+        direct_back = bank("direct_back", 0, 2 * P)
+        backs.append(direct_back[:])
+        turn_back(direct, 0)
+        nc.tensor.transpose(direct_back[:, P:], direct_third[:], ident[:])
+        for b in range(direct):
             turn_back(b, 0)
-        last_banks = [7, 3, 5]
-        lasts = [bank("last%d" % g, last_banks[g], len(blocks) * P) for g, blocks in enumerate(groups)]
+        near = term_room(3, 2, D + 1, direct * P, "direct_pairs", P)
+        far = sb("far", [P, 2 * P], F32, tag="direct_third")
+        direct_cols = sb("direct_cols", [P, P * PACK], BF16)
+        plus = sb("plus", [P, 2 * P], F32)
+        nc.scalar.copy(out=plus[:, :P], in_=direct_back[:, P:])
+        nc.scalar.copy(
+            out=direct_cols[:].bitcast(F32).rearrange("p (v u) -> p v u", u=2)[:, :, 0], in_=direct_back[:, :P]
+        )
         z_cols = [sb("z_cols%d" % g, [P, len(blocks) * P * PACK], BF16) for g, blocks in enumerate(groups)]
         whole = 2
 
-        def add_group(g, d):
-            for i, b in enumerate(groups[g]):
-                first = d == 0 and i == 0
-                last = d == D and i == len(groups[g]) - 1
-                turn_and_add(lasts[g][:, i * P : (i + 1) * P], t, d, b, first, last)
-
         for d in range(whole):
-            fetch(t, d, 0, V)
-            for g in range(len(groups)):
-                add_group(g, d)
+            fetch(t, d, 0, direct * P)
+            for b in range(direct):
+                turn_and_add(t, d, b)
         for g, blocks in enumerate(groups):
             for d in range(whole, D + 1):
                 fetch(t, d, blocks[0] * P, len(blocks) * P)
-                add_group(g, d)
-            rows = z_all[:].rearrange("v (b c) -> v b c", b=BLOCKS)[:, blocks[0] : blocks[-1] + 1, 3 * P :]
-            nc.scalar.copy(out=rows, in_=lasts[g][:].rearrange("v (b c) -> v b c", c=P))
+                for b in blocks:
+                    turn_and_add(t, d, b)
             for b in blocks:
+                round_upper(b)
                 turn_back(b, 1)
-            copy = nc.vector.tensor_copy if g == 0 else nc.scalar.copy
-            copy(
+            nc.scalar.copy(
                 out=z_cols[g][:].bitcast(F32).rearrange("p (b v u) -> p b v u", u=2, v=P),
                 in_=back_tiles[g][:].rearrange("p (b u v) -> p b v u", u=2, v=P),
             )
 
-        codes = sb("codes", [P, N + V], U32, tag="h%d" % t)
-        z_scale = [sb("z_scale%d" % g, [P, len(blocks) * P], U8) for g, blocks in enumerate(groups)]
-        w2_code = codes[:, :N]
-        nc.vector.quantize_mx(out=w2_code.bitcast(FP8X4), scales=w2_scale[:], in_=w2_stage[:])
+        v0 = direct * P
+        for d, dst in ((2, far[:, :P]), (3, far[:, P:]), (1, near)):
+            nc.vector.tensor_tensor(dst, h[t][:].indirect(entries(lists[d], v0, P)), factors[d][:, v0:], MULT)
+        nc.vector.tensor_tensor(plus[:, P:], far[:, :P], far[:, P:], ADD)
+        nc.vector.tensor_tensor(minus[:, P:], h[t][:].indirect(entries(lists[0], v0, P)), near, SUBTRACT)
+        w2_code = sb("w2_code", [P, N], U32, tag="direct_third")
+        nc.vector.quantize_mx(out=w2_code[:].bitcast(FP8X4), scales=w2_scale[:], in_=w2_stage[:])
+        nc.vector.tensor_tensor(
+            direct_cols[:].rearrange("p (v u e) -> p v u e", u=2, e=2)[:, :, 1, :],
+            plus[:].rearrange("p (e v) -> p v e", e=2),
+            minus[:].rearrange("p (e v) -> p v e", e=2),
+            SUBTRACT,
+        )
+
+        codes = sb("codes", [P, V], U32, tag="h%d" % t)
         result = sb("result", [P, V], F32)
-        prods = [bank("prod0", 4, 2 * P)[:], bank("prod1", 7, P)[:], bank("prod2", 6, P)[:]]
-        for g, blocks in enumerate(groups):
-            z_code = codes[:, N + blocks[0] * P : N + (blocks[-1] + 1) * P]
-            nc.vector.quantize_mx(out=z_code.bitcast(FP8X4), scales=z_scale[g][:], in_=z_cols[g][:])
+        ends = [
+            (z_cols[0], 0, 2 * P, 4, nc.scalar.copy),
+            (z_cols[1], 2 * P, P, 6, nc.vector.tensor_copy),
+            (direct_cols, v0, P, 1, nc.scalar.copy),
+        ]
+        for cols, c0, n, b, copy in ends:
+            z_scale = sb("z_scale%d" % c0, [P, n], U8, tag="z_cols0" if c0 == v0 else None)
+            prod = bank("prod%d" % c0, b, n)
+            nc.vector.quantize_mx(out=codes[:, c0 : c0 + n].bitcast(FP8X4), scales=z_scale[:], in_=cols[:])
             nc.tensor.matmul_mx(
-                out=prods[g],
-                lhsT=w2_code.bitcast(FP8X4),
+                out=prod[:],
+                lhsT=w2_code[:].bitcast(FP8X4),
                 lhsT_scale=w2_scale[:],
-                rhs=z_code.bitcast(FP8X4),
-                rhs_scale=z_scale[g][:],
+                rhs=codes[:, c0 : c0 + n].bitcast(FP8X4),
+                rhs_scale=z_scale[:],
                 start=True,
                 stop=True,
             )
-        nc.scalar.copy(out=result[:, : 2 * P], in_=prods[0])
-        nc.sync.dma_start(out=out[:, : 2 * P], in_=result[:, : 2 * P])
-        nc.vector.tensor_copy(out=result[:, 2 * P : 3 * P], in_=prods[1])
-        nc.sync.dma_start(out=out[:, 2 * P : 3 * P], in_=result[:, 2 * P : 3 * P])
-        nc.scalar.copy(out=result[:, 3 * P :], in_=prods[2])
-        nc.sync.dma_start(out=out[:, 3 * P :], in_=result[:, 3 * P :])
+            copy(out=result[:, c0 : c0 + n], in_=prod[:])
+            nc.sync.dma_start(out=out[:, c0 : c0 + n], in_=result[:, c0 : c0 + n])

@@ -272,11 +272,9 @@ def tile_picked_lapl_silu_p_kernel(
                 in_=src.rearrange("v (o e i) -> v o i e", i=8, e=2),
             )
 
-        def round_upper(b):
-            low = sums[b][:, :480].rearrange("v (a w) -> v w a", w=96)[:, :80, 1:5:3]
-            nc.scalar.copy(out=z_rows[b][:, 2 * P : 2 * P + 160].rearrange("v (p e) -> v p e", e=2), in_=low)
-            high = sums[b][:, 2 * P :].rearrange("v (e c) -> v c e", e=2)[:, 80:]
-            nc.scalar.copy(out=z_rows[b][:, 2 * P + 160 :].rearrange("v (p e) -> v p e", e=2), in_=high)
+        def round_slot(b, e, p0, p1, at):
+            dst = z_rows[b][:, 2 * P :].rearrange("v (p e) -> v p e", e=2)[:, p0:p1, e]
+            nc.scalar.copy(out=dst, in_=sums[b][:, at : at + p1 - p0])
 
         def turn_back(b, u):
             nc.tensor.transpose(
@@ -296,6 +294,8 @@ def tile_picked_lapl_silu_p_kernel(
                 nc.scalar.copy(out=direct_third[:, p0:p1], in_=sums[direct][:, at : at + p1 - p0])
             for b in block_order:
                 round_pairs(t, b)
+                if t > 0 and b < direct:
+                    round_slot(b, 0, *third_runs[t - 1])
 
         t = TILES - 1
         groups = [(0, 1), (2,)]
@@ -328,7 +328,7 @@ def tile_picked_lapl_silu_p_kernel(
                 for b in blocks:
                     turn_and_add(t, d, b)
             for b in blocks:
-                round_upper(b)
+                round_slot(b, 1, 0, P, 3 * P)
                 turn_back(b, 1)
             nc.scalar.copy(
                 out=z_cols[g][:].bitcast(F32).rearrange("p (b v u) -> p b v u", u=2, v=P),

@@ -301,19 +301,18 @@ def tile_picked_lapl_silu_p_kernel(
         groups = [(0, 1), (2,)]
         back_tiles = [bank("back%d" % g, 2 + g, len(blocks) * 2 * P) for g, blocks in enumerate(groups)]
         backs = [back_tiles[0][:, : 2 * P], back_tiles[0][:, 2 * P :], back_tiles[1][:]]
-        direct_back = bank("direct_back", 0, 2 * P)
+        direct_back = bank("direct_back", 0, P)
         backs.append(direct_back[:])
         turn_back(direct, 0)
-        nc.tensor.transpose(direct_back[:, P:], direct_third[:], ident[:])
         for b in range(direct):
             turn_back(b, 0)
-        near = term_room(3, 2, D + 1, direct * P, "direct_pairs", P)
-        far = sb("far", [P, 2 * P], F32, tag="direct_third")
+        spare = term_room(3, 2, D + 1, direct * P, "direct_pairs", 3 * P)
+        near = spare[:, :P]
+        far = spare[:, P:]
         direct_cols = sb("direct_cols", [P, P * PACK], BF16)
         plus = sb("plus", [P, 2 * P], F32)
-        nc.scalar.copy(out=plus[:, :P], in_=direct_back[:, P:])
         nc.scalar.copy(
-            out=direct_cols[:].bitcast(F32).rearrange("p (v u) -> p v u", u=2)[:, :, 0], in_=direct_back[:, :P]
+            out=direct_cols[:].bitcast(F32).rearrange("p (v u) -> p v u", u=2)[:, :, 0], in_=direct_back[:]
         )
         z_cols = [sb("z_cols%d" % g, [P, len(blocks) * P * PACK], BF16) for g, blocks in enumerate(groups)]
         whole = 2
@@ -334,13 +333,17 @@ def tile_picked_lapl_silu_p_kernel(
                 out=z_cols[g][:].bitcast(F32).rearrange("p (b v u) -> p b v u", u=2, v=P),
                 in_=back_tiles[g][:].rearrange("p (b u v) -> p b v u", u=2, v=P),
             )
+            if g == 0:
+                third_back = bank("third_back", 5, P)
+                nc.tensor.transpose(third_back[:], direct_third[:], ident[:])
+                nc.scalar.copy(out=plus[:, :P], in_=third_back[:])
 
         v0 = direct * P
         for d, dst in ((2, far[:, :P]), (3, far[:, P:]), (1, near)):
             nc.vector.tensor_tensor(dst, h[t][:].indirect(entries(lists[d], v0, P)), factors[d][:, v0:], MULT)
         nc.vector.tensor_tensor(plus[:, P:], far[:, :P], far[:, P:], ADD)
         nc.vector.tensor_tensor(minus[:, P:], h[t][:].indirect(entries(lists[0], v0, P)), near, SUBTRACT)
-        w2_code = sb("w2_code", [P, N], U32, tag="direct_third")
+        w2_code = sb("w2_code", [P, N], U32, tag="stage0_0")
         nc.vector.quantize_mx(out=w2_code[:].bitcast(FP8X4), scales=w2_scale[:], in_=w2_stage[:])
         nc.vector.tensor_tensor(
             direct_cols[:].rearrange("p (v u e) -> p v u e", u=2, e=2)[:, :, 1, :],
@@ -357,7 +360,7 @@ def tile_picked_lapl_silu_p_kernel(
             (direct_cols, v0, P, 1, nc.scalar.copy),
         ]
         for cols, c0, n, b, copy in ends:
-            z_scale = sb("z_scale%d" % c0, [P, n], U8, tag="z_cols0" if c0 == v0 else None)
+            z_scale = sb("z_scale%d" % c0, [P, n], U8)
             prod = bank("prod%d" % c0, b, n)
             nc.vector.quantize_mx(out=codes[:, c0 : c0 + n].bitcast(FP8X4), scales=z_scale[:], in_=cols[:])
             nc.tensor.matmul_mx(

@@ -16,8 +16,6 @@ FP8X4 = mybir.dt.float8_e4m3fn_x4
 SILU = mybir.ActivationFunctionType.Silu
 COPY = mybir.ActivationFunctionType.Copy
 MULT = mybir.AluOpType.mult
-ADD = mybir.AluOpType.add
-SUBTRACT = mybir.AluOpType.subtract
 
 P = 128
 PACK = 4
@@ -34,10 +32,14 @@ def tile_picked_lapl_silu_p_kernel(
     with ExitStack() as ctx:
         held = ctx.enter_context(tc.tile_pool(name="held", bufs=1))
         keep = ctx.enter_context(tc.tile_pool(name="keep", bufs=1))
+        laid = ctx.enter_context(tc.tile_pool(name="laid", bufs=1))
         psum = ctx.enter_context(tc.psum_pool(name="psum", bufs=1))
 
         def sb(name, shape, dtype, tag=None):
             return keep.tile(shape, dtype, name=name, tag=tag or name, align_bytes=64)
+
+        def placed(name, shape, dtype, offset):
+            return laid.tile(shape, dtype, name=name, tag=name, align_bytes=64, offset=offset)
 
         def bank(name, b, cols):
             return psum.tile([P, cols], F32, name=name, tag="bank%d" % b)
@@ -45,15 +47,12 @@ def tile_picked_lapl_silu_p_kernel(
         def entries(lst, start, count):
             return lst[:, start // ENTRIES_PER_COLUMN : (start + count) // ENTRIES_PER_COLUMN]
 
-        scale_win = sb("scale_win", [P, T], U8)
+        part = PACK * P
+        scale_win = placed("scale_win", [P, T], U8, 2048)
         nc.gpsimd.memset(scale_win[64:, :].bitcast(I32), 0)
         nc.vector.memset(scale_win[32:64, :].bitcast(I32), 0)
         x_plane = sb("x_plane", [P, PASSES * S], U8)
         nc.vector.memset(x_plane[:].bitcast(I32), 0)
-        minus_one = sb("minus_one", [P, V], F32)
-        nc.vector.memset(minus_one[:], -1.0)
-        minus = sb("minus", [P, 2 * P], F32)
-        nc.gpsimd.memset(minus[:, :P], 0.0)
         warm_in = sb("warm_in", [P, 1], F32)
         warm_out = sb("warm_out", [P, 1], F32)
         nc.gpsimd.memset(warm_in[:], 0.0)
@@ -65,31 +64,46 @@ def tile_picked_lapl_silu_p_kernel(
         lists = [held.tile([P, V // 16], U16, name="list%d" % d) for d in range(D + 1)]
         list_src = [cen, pos1, pos2, pos3]
         word_win = [sb("word_win%d" % z, [P, T], I32) for z in range(PASSES)]
-        chunks = [(0, 176), (176, 336), (336, 512)]
-        pitch = 6 * 32
         w1_raw = {}
-        w1_raw[0, 0] = sb("w1_raw0_0", [P, PACK, pitch], F32)[:]
 
         def load_words(z):
             nc.sync.dma_start(out=word_win[z][:], in_=x_words[z].rearrange("p n t -> p (n t)").bitcast(I32))
 
-        def load_w1(c, z):
-            c0, c1 = chunks[c]
-            rows = w1[z * P * PACK : (z + 1) * P * PACK, c0:c1]
-            at = c0 % 32
-            nc.sync.dma_start(
-                out=w1_raw[c, z][:, :, at : at + c1 - c0], in_=rows.rearrange("(p j) c -> p j c", j=PACK)
-            )
+        def load_w1(t, z, room):
+            w1_raw[t, z] = room.rearrange("p (j c) -> p j c", j=PACK)
+            rows = w1[z * part : (z + 1) * part, t * P : (t + 1) * P]
+            nc.sync.dma_start(out=w1_raw[t, z], in_=rows.rearrange("(p j) c -> p j c", j=PACK))
 
         nc.sync.dma_start(offs_sb[:], offs)
         nc.sync.dma_start(
             out=scale_win[:32, :].bitcast(I32), in_=x_scales.bitcast(I32).rearrange("z b n -> b z n")
         )
         load_words(0)
+        gate_col = sb("gate_col", [P, D * PACK], F32)
+        nc.sync.dma_start(
+            out=gate_col[:].rearrange("p (d j) -> p d j", j=PACK),
+            in_=gate[:, 0, :].rearrange("d (p j) -> p d j", j=PACK),
+        )
         for d in range(D + 1):
             nc.sync.dma_start(lists[d][:], list_src[d])
-        load_w1(0, 0)
+        first_raw = sb("first_raw", [P, part], F32)
+        load_w1(0, 0, first_raw[:])
         load_words(1)
+
+        factors = [None]
+        for d in range(D):
+            spread = bank("spread%d" % d, 4 + d, V)
+            for j in range(PACK):
+                column = gate_col[:, d * PACK + j : d * PACK + j + 1]
+                nc.tensor.transpose(spread[:, j * P : (j + 1) * P], column.to_broadcast([P, P]), ident[:])
+            factor = sb("factor%d" % d, [P, V], F32)
+            nc.scalar.activation(
+                out=factor[:].rearrange("p (n j) -> p n j", j=PACK),
+                in_=spread[:].rearrange("p (j n) -> p n j", j=PACK),
+                func=COPY,
+                scale=-1.0,
+            )
+            factors.append(factor)
 
         x_scale = sb("x_scale", [P, S], U8)
         x_early = sb("x_early", [P, S], U32)
@@ -100,93 +114,74 @@ def tile_picked_lapl_silu_p_kernel(
                 out=x_plane[32 * q : 32 * q + 4, :].bitcast(I32).rearrange("p (z n) -> p z n", z=PASSES),
                 in_=x_scale[8 * q : 8 * q + 8, :].bitcast(I32),
             )
+        second_raw = placed("second_raw", [P, part], F32, 64)
+        load_w1(0, 1, second_raw[:])
+        late_raw = placed("late_raw", [P, (2 * (TILES - 1) + 1) * part], F32, 4032)
+        for t in range(1, TILES):
+            for z in range(PASSES):
+                at = (2 * (t - 1) + z) * part
+                load_w1(t, z, late_raw[:, at : at + part])
+        w2_raw = late_raw[:, 2 * (TILES - 1) * part :]
+        nc.sync.dma_start(out=w2_raw, in_=w2.rearrange("(p j) m -> p (j m)", j=PACK))
 
-        upper_code = sb("upper_code", [P, 2 * PASSES * P], U32)
-        upper_scale = sb("upper_scale", [P, 2 * PASSES * P], U8)
-        w1_code = [sb("w1_code%d" % t, [P, PASSES * P], U32) for t in range(2)]
-        w1_scale = [sb("w1_scale%d" % t, [P, PASSES * P], U8) for t in range(2)]
-        w1_code.extend([upper_code[:, : PASSES * P], upper_code[:, PASSES * P :]])
-        w1_scale.extend([upper_scale[:, : PASSES * P], upper_scale[:, PASSES * P :]])
+        w1_code = [sb("w1_code%d" % t, [P, PASSES * P], U32) for t in range(TILES)]
+        w1_scale = [sb("w1_scale%d" % t, [P, PASSES * P], U8) for t in range(TILES)]
+        stage = {}
 
-        def late_w1(parts, tag):
-            width = PACK * pitch
-            room = sb("w1_late_" + tag, [P, len(parts) * width], F32, tag=tag)
-            for i, (c, z) in enumerate(parts):
-                w1_raw[c, z] = room[:, i * width : (i + 1) * width].rearrange("p (j c) -> p j c", j=PACK)
-                load_w1(c, z)
-
-        late_w1([(0, 1)], "scale_win")
-
-        pieces = [
-            [(0, 0, 0, 6, 0, 16), (96, 0, 0, 4, 16, 8)],
-            [(0, 0, 4, 5, 16, 8), (8, 1, 0, 5, 16, 8), (48, 1, 1, 6, 0, 16)],
-            [(0, 2, 1, 6, 0, 16), (80, 2, 0, 6, 16, 8)],
-            [(0, 0, 0, 5, 24, 8), (40, 1, 0, 5, 24, 8), (80, 2, 0, 6, 24, 8)],
-        ]
-        first_stage = [sb("w1_stage0_%d" % z, [P, P * PACK], BF16, tag="stage0_%d" % z) for z in range(PASSES)]
-        second_stage = sb("w1_stage1", [P, PASSES * P * PACK], BF16, tag="stage1")
-        upper_stage = sb("upper_stage", [P, 2 * PASSES * P * PACK], BF16)
-
-        def stage_of(t, z):
-            if t == 0:
-                return first_stage[z][:]
-            if t == 1:
-                return second_stage[:, z * P * PACK : (z + 1) * P * PACK]
-            at = ((t - 2) * PASSES + z) * P * PACK
-            return upper_stage[:, at : at + P * PACK]
-
-        def round_w1(t, z, chunk, copy):
-            for m0, c, o0, o1, r0, n in pieces[t]:
-                if c == chunk:
-                    src = w1_raw[c, z].rearrange("p j (o q e) -> p q o j e", q=8, e=4)
-                    dst = stage_of(t, z)[:, m0 * PACK : (m0 + (o1 - o0) * n) * PACK]
-                    copy(
-                        out=dst.rearrange("p (o q e j) -> p q o j e", q=n // 4, e=4, j=PACK),
-                        in_=src[:, r0 // 4 : (r0 + n) // 4, o0:o1],
-                    )
-
-        for z in range(PASSES):
-            round_w1(0, z, 0, nc.scalar.copy)
-            nc.vector.quantize_mx(
-                out=w1_code[0][:, z * P : (z + 1) * P].bitcast(FP8X4),
-                scales=w1_scale[0][:, z * P : (z + 1) * P],
-                in_=first_stage[z][:],
+        def round_weights(dst, src, copy):
+            copy(
+                out=dst.rearrange("p (c i j) -> p c j i", i=4, j=PACK),
+                in_=src.rearrange("p j (c i) -> p c j i", i=4),
             )
-            round_w1(1, z, 0, nc.scalar.copy)
-            round_w1(3, z, 0, nc.scalar.copy)
-        late_w1([(1, 0), (1, 1)], "w1_raw0_0")
-        gates = sb("gates", [P, D, V], F32, tag="stage0_0")
-        gate_raw = [gates[:, d, :] for d in range(D)]
-        nc.sync.dma_start(out=gates[:], in_=gate.rearrange("d p v -> p d v"))
-        gather_pieces = [(0, 768), (768, 256)]
+
+        def round_w1(t, z, copy, tag=None):
+            stage[t, z] = sb("stage%d_%d" % (t, z), [P, part], BF16, tag=tag)
+            round_weights(stage[t, z][:], w1_raw[t, z], copy)
+
+        def quantise_w1(t, z):
+            nc.vector.quantize_mx(
+                out=w1_code[t][:, z * P : (z + 1) * P].bitcast(FP8X4),
+                scales=w1_scale[t][:, z * P : (z + 1) * P],
+                in_=stage[t, z][:],
+            )
+
+        cut = 768
         half = S // 2
-        cut = gather_pieces[1][0]
-        x_late = [sb("x_late0", [P, cut], U32), sb("x_late1", [P, S - cut], U32, tag="scale_win")]
+        x_late = [sb("x_late0", [P, cut], U32)]
 
         def x_code(z, s0, n):
             if z == 0:
                 return x_early[:, s0 : s0 + n]
             return x_late[s0 // cut][:, s0 % cut : s0 % cut + n]
 
-        for s0, n in gather_pieces:
+        def gather_late(s0, n):
             nc.vector.tensor_copy(x_code(1, s0, n), word_win[1][:].bitcast(U32).indirect(entries(offs_sb, s0, n)))
 
-        late_w1([(2, 0), (2, 1)], "x_scale")
+        round_w1(0, 0, nc.scalar.copy)
+        quantise_w1(0, 0)
+        gather_late(0, cut)
+        round_w1(0, 1, nc.scalar.copy)
+        quantise_w1(0, 1)
+        x_late.append(placed("x_late1", [P, S - cut], U32, 64))
+        gather_late(cut, S - cut)
+        round_w1(1, 0, nc.scalar.copy)
+
         h = [sb("h%d" % t, [P, S], F32) for t in range(TILES)]
         first_groups = [[(0, 256)], [(256, 256)], [(512, 256)], [(768, 256)]]
         later_groups = [[(0, half)], [(half, cut - half), (cut, S - cut)]]
         h_banks = [(0, 1, 2, 3), (0, 1), (2, 3), (0, 1)]
+        accs = {}
 
         def project(t):
             groups = first_groups if t == 0 else later_groups
-            accs = [bank("acc%d_%d" % (t, i), h_banks[t][i], sum(n for s0, n in g)) for i, g in enumerate(groups)]
+            accs[t] = [bank("acc%d_%d" % (t, i), h_banks[t][i], sum(n for s0, n in g)) for i, g in enumerate(groups)]
             order = [(z, i, piece) for i, g in enumerate(groups) for piece in g for z in range(PASSES)]
             if t == 0:
                 order = sorted(order)
             for z, i, (s0, n) in order:
                 g0 = groups[i][0][0]
                 nc.tensor.matmul_mx(
-                    out=accs[i][:, s0 - g0 : s0 - g0 + n],
+                    out=accs[t][i][:, s0 - g0 : s0 - g0 + n],
                     lhsT=w1_code[t][:, z * P : (z + 1) * P].bitcast(FP8X4),
                     lhsT_scale=w1_scale[t][:, z * P : (z + 1) * P],
                     rhs=x_code(z, s0, n).bitcast(FP8X4),
@@ -194,183 +189,128 @@ def tile_picked_lapl_silu_p_kernel(
                     start=(z == 0),
                     stop=(z == PASSES - 1),
                 )
-                if z == PASSES - 1 and (s0, n) == groups[i][-1]:
-                    nc.scalar.activation(out=h[t][:, g0 : s0 + n], in_=accs[i][:], func=SILU)
 
-        project(0)
-        round_w1(1, 0, 1, nc.scalar.copy)
-        round_w1(1, 1, 1, nc.vector.tensor_copy)
-        nc.vector.quantize_mx(out=w1_code[1][:].bitcast(FP8X4), scales=w1_scale[1][:], in_=second_stage[:])
-        w2_raw = sb("w2_raw", [P, PACK * N], F32, tag="stage0_1")
-        for j in range(PACK):
-            nc.sync.dma_start(
-                out=w2_raw[:, j * N : (j + 1) * N], in_=w2.rearrange("(o j i) m -> j o i m", j=PACK, i=8)[j]
-            )
-        project(1)
-        for z in range(PASSES):
-            round_w1(3, z, 1, nc.scalar.copy)
-        for t in (2, 3):
-            for z in range(PASSES):
-                round_w1(t, z, 2, nc.scalar.copy)
-        for t in (2, 3):
-            at = (t - 2) * PASSES * P * PACK
-            nc.vector.quantize_mx(
-                out=w1_code[t].bitcast(FP8X4), scales=w1_scale[t], in_=upper_stage[:, at : at + PASSES * P * PACK]
-            )
-        w2_stage = sb("w2_stage", [P, N * PACK], BF16)
-        w2_scale = sb("w2_scale", [P, N], U8)
-        nc.scalar.activation(
-            out=w2_stage[:].rearrange("p (m j) -> p m j", j=PACK),
-            in_=w2_raw[:].rearrange("p (j m) -> p m j", j=PACK),
-            func=COPY,
-            scale=-1.0,
-        )
+        def activate(t):
+            width = S // len(accs[t])
+            for i, acc in enumerate(accs[t]):
+                nc.scalar.activation(out=h[t][:, i * width : (i + 1) * width], in_=acc[:], func=SILU)
 
-        direct = BLOCKS - 1
-        z_rows = [sb("z_rows%d" % b, [P, H], BF16) for b in range(direct)]
-        z_rows.append(sb("direct_pairs", [P, 2 * P], BF16))
-        direct_third = sb("direct_third", [P, P], F32)
         terms = {}
-
-        def term_room(t, d0, d1, width, tag, spare=0):
-            room = sb("terms%d_%d" % (t, d0), [P, (d1 - d0) * width + spare], F32, tag=tag)
-            for d in range(d0, d1):
-                terms[t, d] = room[:, (d - d0) * width : (d - d0 + 1) * width]
-            return room[:, (d1 - d0) * width :]
-
-        term_room(0, 0, D + 1, V, "stage1")
-        term_room(1, 0, 1, V, None)
-        term_room(1, 1, D + 1, V, "x_scale")
-        term_room(2, 0, D + 1, V, None)
-        term_room(3, 0, 2, direct * P, None)
-        factors = [minus_one] + gate_raw
-        sums = [bank("sum%d" % b, 4 + b, H) for b in range(BLOCKS)]
+        for t in range(TILES):
+            for d in range(D + 1):
+                terms[t, d] = sb("term%d_%d" % (t, d), [P, V], F32)
+        z_rows = sb("z_rows", [P, BLOCKS * H], BF16)
+        z_view = z_rows[:].rearrange("v (b u p e) -> v b u p e", b=BLOCKS, u=2, e=2)
+        add_order = [1, 0, 2, 3]
 
         def fetch(t, d, v0, n):
             src = h[t][:].indirect(entries(lists[d], v0, n))
-            nc.vector.tensor_tensor(terms[t, d][:, v0 : v0 + n], src, factors[d][:, v0 : v0 + n], MULT)
+            if d == 0:
+                nc.scalar.activation(out=terms[t, d][:, v0 : v0 + n], in_=src, func=COPY)
+            else:
+                nc.vector.tensor_tensor(terms[t, d][:, v0 : v0 + n], src, factors[d][:, v0 : v0 + n], MULT)
 
-        def turn_and_add(t, d, b):
-            nc.tensor.matmul(
-                out=sums[b][:, t * P : (t + 1) * P],
-                lhsT=terms[t, d][:, b * P : (b + 1) * P],
-                rhs=ident[:],
-                is_transpose=True,
-                start=(d == 0),
-                stop=(d == D),
-            )
+        def turn_and_add(total, t, d, b0, b1):
+            for b in range(b0, b1):
+                nc.tensor.matmul(
+                    out=total[:, (b - b0) * P : (b - b0 + 1) * P],
+                    lhsT=terms[t, d][:, b * P : (b + 1) * P],
+                    rhs=ident[:],
+                    is_transpose=True,
+                    start=(d == add_order[0] and b == b0),
+                    stop=(d == add_order[-1] and b == b1 - 1),
+                )
 
-        block_order = [direct] + list(range(direct))
-        third_runs = [(0, 80, 96), (80, P, 336)]
-        pair_runs = [(0, 0, 6), (P + 48, 6, 11), (2 * P, 11, 16)]
-
-        def round_pairs(t, b):
-            at, o0, o1 = pair_runs[t]
-            src = sums[b][:, at : at + 16 * (o1 - o0)]
+        def round_sum(total, t, b0, b1):
             nc.scalar.copy(
-                out=z_rows[b][:, 16 * o0 : 16 * o1].rearrange("v (o i e) -> v o i e", i=8, e=2),
-                in_=src.rearrange("v (o e i) -> v o i e", i=8, e=2),
+                out=z_view[:, b0:b1, :, 32 * t : 32 * (t + 1), :],
+                in_=total[:].rearrange("v (b p u e) -> v b u p e", b=b1 - b0, u=2, e=2),
             )
 
-        def round_slot(b, e, p0, p1, at):
-            dst = z_rows[b][:, 2 * P :].rearrange("v (p e) -> v p e", e=2)[:, p0:p1, e]
-            nc.scalar.copy(out=dst, in_=sums[b][:, at : at + p1 - p0])
+        totals = {}
 
-        def turn_back(b, u):
-            nc.tensor.transpose(
-                backs[b][:, u * P : (u + 1) * P], z_rows[b][:].bitcast(F32)[:, u * P : (u + 1) * P], ident[:]
-            )
+        def step(t, d):
+            if d == add_order[0]:
+                totals[t] = bank("total%d" % t, 4 + t, V)
+            fetch(t, d, 0, V)
+            turn_and_add(totals[t], t, d, 0, BLOCKS)
 
-        for t in range(TILES - 1):
-            if t == 1:
-                project(2)
-                project(3)
-            for d in range(D + 1):
-                fetch(t, d, 0, V)
-                for b in block_order:
-                    turn_and_add(t, d, b)
-            if t > 0:
-                p0, p1, at = third_runs[t - 1]
-                nc.scalar.copy(out=direct_third[:, p0:p1], in_=sums[direct][:, at : at + p1 - p0])
-            for b in block_order:
-                round_pairs(t, b)
-                if t > 0 and b < direct:
-                    round_slot(b, 0, *third_runs[t - 1])
+        project(0)
+        activate(0)
+        round_w1(1, 1, nc.vector.tensor_copy)
+        for z in range(PASSES):
+            quantise_w1(1, z)
+        round_w1(2, 0, nc.vector.tensor_copy)
+        project(1)
+        step(0, 1)
+        step(0, 0)
+        activate(1)
+        round_w1(2, 1, nc.scalar.copy, tag="w1_code0")
+        for z in range(PASSES):
+            round_w1(3, z, nc.scalar.copy)
+        step(0, 2)
+        step(0, 3)
+        for z in range(PASSES):
+            quantise_w1(2, z)
+        project(2)
+        step(1, 1)
+        for z in range(PASSES):
+            quantise_w1(3, z)
+        project(3)
+        step(1, 0)
+        activate(2)
+        round_sum(totals[0], 0, 0, BLOCKS)
+        activate(3)
+        step(1, 2)
+        step(1, 3)
+        step(2, 1)
+        step(2, 0)
+        round_sum(totals[1], 1, 0, BLOCKS)
+        w2_stage = sb("w2_stage", [P, part], BF16)
+        round_weights(w2_stage[:], w2_raw.rearrange("p (j m) -> p j m", j=PACK), nc.scalar.copy)
+        step(2, 2)
+        step(2, 3)
+        last = TILES - 1
+        fetch(last, 0, 0, V)
+        round_sum(totals[2], 2, 0, BLOCKS)
+        w2_code = sb("w2_code", [P, N], U32)
+        w2_scale = sb("w2_scale", [P, N], U8)
 
-        t = TILES - 1
-        groups = [(0, 1), (2,)]
-        back_tiles = [bank("back%d" % g, 2 + g, len(blocks) * 2 * P) for g, blocks in enumerate(groups)]
-        backs = [back_tiles[0][:, : 2 * P], back_tiles[0][:, 2 * P :], back_tiles[1][:]]
-        direct_back = bank("direct_back", 0, P)
-        backs.append(direct_back[:])
-        turn_back(direct, 0)
-        for b in range(direct):
-            turn_back(b, 0)
-        spare = term_room(3, 2, D + 1, direct * P, "direct_pairs", 3 * P)
-        near = spare[:, :P]
-        far = spare[:, P:]
-        direct_cols = sb("direct_cols", [P, P * PACK], BF16)
-        plus = sb("plus", [P, 2 * P], F32)
-        nc.scalar.copy(
-            out=direct_cols[:].bitcast(F32).rearrange("p (v u) -> p v u", u=2)[:, :, 0], in_=direct_back[:]
-        )
-        z_cols = [sb("z_cols%d" % g, [P, len(blocks) * P * PACK], BF16) for g, blocks in enumerate(groups)]
-        whole = 2
-
-        for d in range(whole):
-            fetch(t, d, 0, direct * P)
-            for b in range(direct):
-                turn_and_add(t, d, b)
-        for g, blocks in enumerate(groups):
-            for d in range(whole, D + 1):
-                fetch(t, d, blocks[0] * P, len(blocks) * P)
-                for b in blocks:
-                    turn_and_add(t, d, b)
-            for b in blocks:
-                round_slot(b, 1, 0, P, 3 * P)
-                turn_back(b, 1)
-            nc.scalar.copy(
-                out=z_cols[g][:].bitcast(F32).rearrange("p (b v u) -> p b v u", u=2, v=P),
-                in_=back_tiles[g][:].rearrange("p (b u v) -> p b v u", u=2, v=P),
-            )
-            if g == 0:
-                third_back = bank("third_back", 5, P)
-                nc.tensor.transpose(third_back[:], direct_third[:], ident[:])
-                nc.scalar.copy(out=plus[:, :P], in_=third_back[:])
-
-        v0 = direct * P
-        for d, dst in ((2, far[:, :P]), (3, far[:, P:]), (1, near)):
-            nc.vector.tensor_tensor(dst, h[t][:].indirect(entries(lists[d], v0, P)), factors[d][:, v0:], MULT)
-        nc.vector.tensor_tensor(plus[:, P:], far[:, :P], far[:, P:], ADD)
-        nc.vector.tensor_tensor(minus[:, P:], h[t][:].indirect(entries(lists[0], v0, P)), near, SUBTRACT)
-        w2_code = sb("w2_code", [P, N], U32, tag="stage0_0")
-        nc.vector.quantize_mx(out=w2_code[:].bitcast(FP8X4), scales=w2_scale[:], in_=w2_stage[:])
-        nc.vector.tensor_tensor(
-            direct_cols[:].rearrange("p (v u e) -> p v u e", u=2, e=2)[:, :, 1, :],
-            plus[:].rearrange("p (e v) -> p v e", e=2),
-            minus[:].rearrange("p (e v) -> p v e", e=2),
-            SUBTRACT,
-        )
-
-        codes = sb("codes", [P, V], U32, tag="h%d" % t)
         result = sb("result", [P, V], F32)
-        ends = [
-            (z_cols[0], 0, 2 * P, 4, nc.scalar.copy),
-            (z_cols[1], 2 * P, P, 6, nc.vector.tensor_copy),
-            (direct_cols, v0, P, 1, nc.scalar.copy),
-        ]
-        for cols, c0, n, b, copy in ends:
-            z_scale = sb("z_scale%d" % c0, [P, n], U8)
-            prod = bank("prod%d" % c0, b, n)
-            nc.vector.quantize_mx(out=codes[:, c0 : c0 + n].bitcast(FP8X4), scales=z_scale[:], in_=cols[:])
+        groups = [(0, 2, 7, 2, 6), (2, 3, 4, 3, 1), (3, 4, 5, 0, 7)]
+        z_cols = {}
+        for b0, b1, sum_bank, back_bank, prod_bank in groups:
+            n = (b1 - b0) * P
+            total = bank("last%d" % b0, sum_bank, n)
+            for d in add_order:
+                if d > 0:
+                    fetch(last, d, b0 * P, n)
+                turn_and_add(total, last, d, b0, b1)
+            round_sum(total, last, b0, b1)
+            back = bank("back%d" % b0, back_bank, 2 * n)
+            for w in range(2 * (b1 - b0)):
+                words = z_rows[:].bitcast(F32)[:, (2 * b0 + w) * P : (2 * b0 + w + 1) * P]
+                nc.tensor.transpose(back[:, w * P : (w + 1) * P], words, ident[:])
+            z_cols[b0] = sb("z_cols%d" % b0, [P, n * PACK], BF16)
+            nc.scalar.copy(
+                out=z_cols[b0][:].bitcast(F32).rearrange("p (b v u) -> p b v u", u=2, v=P),
+                in_=back[:].rearrange("p (b u v) -> p b v u", u=2, v=P),
+            )
+        nc.vector.quantize_mx(out=w2_code[:].bitcast(FP8X4), scales=w2_scale[:], in_=w2_stage[:])
+        for b0, b1, sum_bank, back_bank, prod_bank in groups:
+            n = (b1 - b0) * P
+            codes = sb("codes%d" % b0, [P, n], U32)
+            z_scale = sb("z_scale%d" % b0, [P, n], U8)
+            prod = bank("prod%d" % b0, prod_bank, n)
+            nc.vector.quantize_mx(out=codes[:].bitcast(FP8X4), scales=z_scale[:], in_=z_cols[b0][:])
             nc.tensor.matmul_mx(
                 out=prod[:],
                 lhsT=w2_code[:].bitcast(FP8X4),
                 lhsT_scale=w2_scale[:],
-                rhs=codes[:, c0 : c0 + n].bitcast(FP8X4),
+                rhs=codes[:].bitcast(FP8X4),
                 rhs_scale=z_scale[:],
                 start=True,
                 stop=True,
             )
-            copy(out=result[:, c0 : c0 + n], in_=prod[:])
-            nc.sync.dma_start(out=out[:, c0 : c0 + n], in_=result[:, c0 : c0 + n])
+            nc.vector.tensor_copy(out=result[:, b0 * P : b1 * P], in_=prod[:])
+            nc.sync.dma_start(out=out[:, b0 * P : b1 * P], in_=result[:, b0 * P : b1 * P])

@@ -63,7 +63,8 @@ def tile_picked_lapl_silu_p_kernel(
         offs_sb = held.tile([P, S // 16], U16, name="offs_sb")
         lists = [held.tile([P, V // 16], U16, name="list%d" % d) for d in range(D + 1)]
         list_src = [cen, pos1, pos2, pos3]
-        word_win = [sb("word_win%d" % z, [P, T], I32) for z in range(PASSES)]
+        first_words_at = 8192
+        word_win = [placed("word_win0", [P, T], I32, first_words_at), sb("word_win1", [P, T], I32)]
         w1_raw = {}
 
         def load_words(z):
@@ -78,12 +79,12 @@ def tile_picked_lapl_silu_p_kernel(
         nc.sync.dma_start(
             out=scale_win[:32, :].bitcast(I32), in_=x_scales.bitcast(I32).rearrange("z b n -> b z n")
         )
-        load_words(0)
         gate_col = sb("gate_col", [P, D * PACK], F32)
         nc.sync.dma_start(
             out=gate_col[:].rearrange("p (d j) -> p d j", j=PACK),
             in_=gate[:, 0, :].rearrange("d (p j) -> p d j", j=PACK),
         )
+        load_words(0)
         for d in range(D + 1):
             nc.sync.dma_start(lists[d][:], list_src[d])
         first_raw = sb("first_raw", [P, part], F32)
@@ -116,13 +117,14 @@ def tile_picked_lapl_silu_p_kernel(
             )
         second_raw = placed("second_raw", [P, part], F32, 64)
         load_w1(0, 1, second_raw[:])
-        late_raw = placed("late_raw", [P, (2 * (TILES - 1) + 1) * part], F32, 4032)
-        for t in range(1, TILES):
+        next_raw = placed("next_raw", [P, PASSES * part], F32, 4032)
+        for z in range(PASSES):
+            load_w1(1, z, next_raw[:, z * part : (z + 1) * part])
+        raw_at = {}
+        for t in range(2, TILES):
             for z in range(PASSES):
-                at = (2 * (t - 1) + z) * part
-                load_w1(t, z, late_raw[:, at : at + part])
-        w2_raw = late_raw[:, 2 * (TILES - 1) * part :]
-        nc.sync.dma_start(out=w2_raw, in_=w2.rearrange("(p j) m -> p (j m)", j=PACK))
+                raw_at[t, z] = first_words_at + (PASSES * (t - 2) + z) * part * 4
+                load_w1(t, z, placed("raw%d_%d" % (t, z), [P, part], F32, raw_at[t, z])[:])
 
         w1_code = [sb("w1_code%d" % t, [P, PASSES * P], U32) for t in range(TILES)]
         w1_scale = [sb("w1_scale%d" % t, [P, PASSES * P], U8) for t in range(TILES)]
@@ -158,6 +160,8 @@ def tile_picked_lapl_silu_p_kernel(
             nc.vector.tensor_copy(x_code(1, s0, n), word_win[1][:].bitcast(U32).indirect(entries(offs_sb, s0, n)))
 
         round_w1(0, 0, nc.scalar.copy)
+        w2_raw = sb("w2_raw", [P, part], F32, tag="first_raw")
+        nc.sync.dma_start(out=w2_raw[:], in_=w2.rearrange("(p j) m -> p (j m)", j=PACK))
         quantise_w1(0, 0)
         gather_late(0, cut)
         round_w1(0, 1, nc.scalar.copy)
@@ -196,12 +200,16 @@ def tile_picked_lapl_silu_p_kernel(
                 nc.scalar.activation(out=h[t][:, i * width : (i + 1) * width], in_=acc[:], func=SILU)
 
         terms = {}
+        behind = {(1, 1): (2, 1), (1, 3): (3, 1)}
         for t in range(TILES):
             for d in range(D + 1):
-                terms[t, d] = sb("term%d_%d" % (t, d), [P, V], F32)
+                if (t, d) in behind:
+                    terms[t, d] = placed("term%d_%d" % (t, d), [P, V], F32, raw_at[behind[t, d]])
+                else:
+                    terms[t, d] = sb("term%d_%d" % (t, d), [P, V], F32)
         z_rows = sb("z_rows", [P, BLOCKS * H], BF16)
         z_view = z_rows[:].rearrange("v (b u p e) -> v b u p e", b=BLOCKS, u=2, e=2)
-        add_order = [1, 0, 2, 3]
+        add_order = [1, 2, 3, 0]
 
         def fetch(t, d, v0, n):
             src = h[t][:].indirect(entries(lists[d], v0, n))
@@ -210,15 +218,15 @@ def tile_picked_lapl_silu_p_kernel(
             else:
                 nc.vector.tensor_tensor(terms[t, d][:, v0 : v0 + n], src, factors[d][:, v0 : v0 + n], MULT)
 
-        def turn_and_add(total, t, d, b0, b1):
+        def turn_and_add(total, t, d, b0, b1, order):
             for b in range(b0, b1):
                 nc.tensor.matmul(
                     out=total[:, (b - b0) * P : (b - b0 + 1) * P],
                     lhsT=terms[t, d][:, b * P : (b + 1) * P],
                     rhs=ident[:],
                     is_transpose=True,
-                    start=(d == add_order[0] and b == b0),
-                    stop=(d == add_order[-1] and b == b1 - 1),
+                    start=(d == order[0] and b == b0),
+                    stop=(d == order[-1] and b == b1 - 1),
                 )
 
         def round_sum(total, t, b0, b1):
@@ -228,48 +236,53 @@ def tile_picked_lapl_silu_p_kernel(
             )
 
         totals = {}
+        last_order = [1, 2, 0, 3]
 
         def step(t, d):
             if d == add_order[0]:
                 totals[t] = bank("total%d" % t, 4 + t, V)
-            fetch(t, d, 0, V)
-            turn_and_add(totals[t], t, d, 0, BLOCKS)
+            if d > 0:
+                fetch(t, d, 0, V)
+            turn_and_add(totals[t], t, d, 0, BLOCKS, add_order)
 
         project(0)
         activate(0)
         round_w1(1, 1, nc.vector.tensor_copy)
         for z in range(PASSES):
             quantise_w1(1, z)
-        round_w1(2, 0, nc.vector.tensor_copy)
         project(1)
+        fetch(0, 0, 0, V)
         step(0, 1)
-        step(0, 0)
         activate(1)
-        round_w1(2, 1, nc.scalar.copy, tag="w1_code0")
+        round_w1(2, 0, nc.scalar.copy, tag="w1_code0")
+        round_w1(2, 1, nc.scalar.copy, tag="w1_scale0")
         for z in range(PASSES):
             round_w1(3, z, nc.scalar.copy)
         step(0, 2)
         step(0, 3)
+        step(0, 0)
         for z in range(PASSES):
             quantise_w1(2, z)
         project(2)
         step(1, 1)
+        activate(2)
+        step(1, 2)
         for z in range(PASSES):
             quantise_w1(3, z)
         project(3)
-        step(1, 0)
-        activate(2)
+        fetch(1, 0, 0, V)
         round_sum(totals[0], 0, 0, BLOCKS)
         activate(3)
-        step(1, 2)
         step(1, 3)
+        step(1, 0)
+        fetch(2, 0, 0, V)
         step(2, 1)
-        step(2, 0)
         round_sum(totals[1], 1, 0, BLOCKS)
         w2_stage = sb("w2_stage", [P, part], BF16)
-        round_weights(w2_stage[:], w2_raw.rearrange("p (j m) -> p j m", j=PACK), nc.scalar.copy)
+        round_weights(w2_stage[:], w2_raw[:].rearrange("p (j m) -> p j m", j=PACK), nc.scalar.copy)
         step(2, 2)
         step(2, 3)
+        step(2, 0)
         last = TILES - 1
         fetch(last, 0, 0, V)
         round_sum(totals[2], 2, 0, BLOCKS)
@@ -282,10 +295,10 @@ def tile_picked_lapl_silu_p_kernel(
         for b0, b1, sum_bank, back_bank, prod_bank in groups:
             n = (b1 - b0) * P
             total = bank("last%d" % b0, sum_bank, n)
-            for d in add_order:
+            for d in last_order:
                 if d > 0:
                     fetch(last, d, b0 * P, n)
-                turn_and_add(total, last, d, b0, b1)
+                turn_and_add(total, last, d, b0, b1, last_order)
             round_sum(total, last, b0, b1)
             back = bank("back%d" % b0, back_bank, 2 * n)
             for w in range(2 * (b1 - b0)):

@@ -63,7 +63,7 @@ def tile_picked_lapl_silu_p_kernel(
         offs_sb = held.tile([P, S // 16], U16, name="offs_sb")
         lists = [held.tile([P, V // 16], U16, name="list%d" % d) for d in range(D + 1)]
         list_src = [cen, pos1, pos2, pos3]
-        first_words_at = 8192
+        first_words_at = 10240
         word_win = [placed("word_win0", [P, T], I32, first_words_at), sb("word_win1", [P, T], I32)]
         w1_raw = {}
 
@@ -117,9 +117,11 @@ def tile_picked_lapl_silu_p_kernel(
             )
         second_raw = placed("second_raw", [P, part], F32, 64)
         load_w1(0, 1, second_raw[:])
-        next_raw = placed("next_raw", [P, PASSES * part], F32, 4032)
+        next_raw = placed("next_raw", [P, (1 + PASSES) * part], F32, 4032)
+        w2_raw = next_raw[:, :part]
+        nc.sync.dma_start(out=w2_raw, in_=w2.rearrange("(p j) m -> p (j m)", j=PACK))
         for z in range(PASSES):
-            load_w1(1, z, next_raw[:, z * part : (z + 1) * part])
+            load_w1(1, z, next_raw[:, (1 + z) * part : (2 + z) * part])
         raw_at = {}
         for t in range(2, TILES):
             for z in range(PASSES):
@@ -160,14 +162,14 @@ def tile_picked_lapl_silu_p_kernel(
             nc.vector.tensor_copy(x_code(1, s0, n), word_win[1][:].bitcast(U32).indirect(entries(offs_sb, s0, n)))
 
         round_w1(0, 0, nc.scalar.copy)
-        w2_raw = sb("w2_raw", [P, part], F32, tag="first_raw")
-        nc.sync.dma_start(out=w2_raw[:], in_=w2.rearrange("(p j) m -> p (j m)", j=PACK))
         quantise_w1(0, 0)
         gather_late(0, cut)
         round_w1(0, 1, nc.scalar.copy)
         quantise_w1(0, 1)
         x_late.append(placed("x_late1", [P, S - cut], U32, 64))
         gather_late(cut, S - cut)
+        w2_stage = sb("w2_stage", [P, part], BF16)
+        round_weights(w2_stage[:], w2_raw.rearrange("p (j m) -> p j m", j=PACK), nc.scalar.copy)
         round_w1(1, 0, nc.scalar.copy)
 
         h = [sb("h%d" % t, [P, S], F32) for t in range(TILES)]
@@ -200,7 +202,7 @@ def tile_picked_lapl_silu_p_kernel(
                 nc.scalar.activation(out=h[t][:, i * width : (i + 1) * width], in_=acc[:], func=SILU)
 
         terms = {}
-        behind = {(1, 1): (2, 1), (1, 3): (3, 1)}
+        behind = {(0, 2): (2, 1), (1, 1): (3, 1)}
         for t in range(TILES):
             for d in range(D + 1):
                 if (t, d) in behind:
@@ -236,7 +238,7 @@ def tile_picked_lapl_silu_p_kernel(
             )
 
         totals = {}
-        last_order = [1, 2, 0, 3]
+        last_order = [1, 0, 2, 3]
 
         def step(t, d):
             if d == add_order[0]:
@@ -248,46 +250,46 @@ def tile_picked_lapl_silu_p_kernel(
         project(0)
         activate(0)
         round_w1(1, 1, nc.vector.tensor_copy)
+        w2_code = sb("w2_code", [P, N], U32)
+        w2_scale = sb("w2_scale", [P, N], U8)
+        nc.vector.quantize_mx(out=w2_code[:].bitcast(FP8X4), scales=w2_scale[:], in_=w2_stage[:])
         for z in range(PASSES):
             quantise_w1(1, z)
+        round_w1(2, 0, nc.vector.tensor_copy)
         project(1)
-        fetch(0, 0, 0, V)
+        round_w1(2, 1, nc.scalar.copy, tag="w1_code0")
         step(0, 1)
         activate(1)
-        round_w1(2, 0, nc.scalar.copy, tag="w1_code0")
-        round_w1(2, 1, nc.scalar.copy, tag="w1_scale0")
+        for z in range(PASSES):
+            quantise_w1(2, z)
+        project(2)
         for z in range(PASSES):
             round_w1(3, z, nc.scalar.copy)
+        fetch(0, 0, 0, V)
         step(0, 2)
         step(0, 3)
         step(0, 0)
         for z in range(PASSES):
-            quantise_w1(2, z)
-        project(2)
-        step(1, 1)
-        activate(2)
-        step(1, 2)
-        for z in range(PASSES):
             quantise_w1(3, z)
         project(3)
+        activate(2)
         fetch(1, 0, 0, V)
+        step(1, 1)
         round_sum(totals[0], 0, 0, BLOCKS)
         activate(3)
+        step(1, 2)
         step(1, 3)
         step(1, 0)
         fetch(2, 0, 0, V)
         step(2, 1)
         round_sum(totals[1], 1, 0, BLOCKS)
-        w2_stage = sb("w2_stage", [P, part], BF16)
-        round_weights(w2_stage[:], w2_raw[:].rearrange("p (j m) -> p j m", j=PACK), nc.scalar.copy)
         step(2, 2)
         step(2, 3)
         step(2, 0)
         last = TILES - 1
         fetch(last, 0, 0, V)
+        fetch(last, 1, 0, V)
         round_sum(totals[2], 2, 0, BLOCKS)
-        w2_code = sb("w2_code", [P, N], U32)
-        w2_scale = sb("w2_scale", [P, N], U8)
 
         result = sb("result", [P, V], F32)
         groups = [(0, 2, 7, 2, 6), (2, 3, 4, 3, 1), (3, 4, 5, 0, 7)]
@@ -296,7 +298,7 @@ def tile_picked_lapl_silu_p_kernel(
             n = (b1 - b0) * P
             total = bank("last%d" % b0, sum_bank, n)
             for d in last_order:
-                if d > 0:
+                if d in last_order[2:]:
                     fetch(last, d, b0 * P, n)
                 turn_and_add(total, last, d, b0, b1, last_order)
             round_sum(total, last, b0, b1)
@@ -309,7 +311,6 @@ def tile_picked_lapl_silu_p_kernel(
                 out=z_cols[b0][:].bitcast(F32).rearrange("p (b v u) -> p b v u", u=2, v=P),
                 in_=back[:].rearrange("p (b u v) -> p b v u", u=2, v=P),
             )
-        nc.vector.quantize_mx(out=w2_code[:].bitcast(FP8X4), scales=w2_scale[:], in_=w2_stage[:])
         for b0, b1, sum_bank, back_bank, prod_bank in groups:
             n = (b1 - b0) * P
             codes = sb("codes%d" % b0, [P, n], U32)

@@ -307,7 +307,8 @@ def tile_picked_lapl_silu_p_kernel(
                 words = z_rows[:].bitcast(F32)[:, (2 * b0 + w) * P : (2 * b0 + w + 1) * P]
                 nc.tensor.transpose(back[:, w * P : (w + 1) * P], words, ident[:])
             z_cols[b0] = sb("z_cols%d" % b0, [P, n * PACK], BF16)
-            nc.scalar.copy(
+            weave = nc.vector.tensor_copy if b0 == 0 else nc.scalar.copy
+            weave(
                 out=z_cols[b0][:].bitcast(F32).rearrange("p (b v u) -> p b v u", u=2, v=P),
                 in_=back[:].rearrange("p (b u v) -> p b v u", u=2, v=P),
             )
@@ -326,5 +327,6 @@ def tile_picked_lapl_silu_p_kernel(
                 start=True,
                 stop=True,
             )
-            nc.vector.tensor_copy(out=result[:, b0 * P : b1 * P], in_=prod[:])
+            leave = nc.scalar.copy if b0 == 0 else nc.vector.tensor_copy
+            leave(out=result[:, b0 * P : b1 * P], in_=prod[:])
             nc.sync.dma_start(out=out[:, b0 * P : b1 * P], in_=result[:, b0 * P : b1 * P])

@@ -123,10 +123,13 @@ def tile_picked_lapl_silu_p_kernel(
         for z in range(PASSES):
             load_w1(1, z, next_raw[:, (1 + z) * part : (2 + z) * part])
         raw_at = {}
-        for t in range(2, TILES):
-            for z in range(PASSES):
-                raw_at[t, z] = first_words_at + (PASSES * (t - 2) + z) * part * 4
-                load_w1(t, z, placed("raw%d_%d" % (t, z), [P, part], F32, raw_at[t, z])[:])
+        for z in range(PASSES):
+            raw_at[3, z] = first_words_at + z * 2 * part * 4
+            upper = placed("upper_raw%d" % z, [P, PACK, 2 * P], F32, raw_at[3, z])
+            rows = w1[z * part : (z + 1) * part, 2 * P :]
+            nc.sync.dma_start(out=upper[:], in_=rows.rearrange("(p j) c -> p j c", j=PACK))
+            for u in range(2):
+                w1_raw[2 + u, z] = upper[:].rearrange("p j (q u e) -> p u q j e", u=2, e=2)[:, u]
 
         w1_code = [sb("w1_code%d" % t, [P, PASSES * P], U32) for t in range(TILES)]
         w1_scale = [sb("w1_scale%d" % t, [P, PASSES * P], U8) for t in range(TILES)]
@@ -140,7 +143,10 @@ def tile_picked_lapl_silu_p_kernel(
 
         def round_w1(t, z, copy, tag=None):
             stage[t, z] = sb("stage%d_%d" % (t, z), [P, part], BF16, tag=tag)
-            round_weights(stage[t, z][:], w1_raw[t, z], copy)
+            if t < 2:
+                round_weights(stage[t, z][:], w1_raw[t, z], copy)
+            else:
+                copy(out=stage[t, z][:].rearrange("p (q e j) -> p q j e", e=2, j=PACK), in_=w1_raw[t, z])
 
         def quantise_w1(t, z):
             nc.vector.quantize_mx(
@@ -202,7 +208,7 @@ def tile_picked_lapl_silu_p_kernel(
                 nc.scalar.activation(out=h[t][:, i * width : (i + 1) * width], in_=acc[:], func=SILU)
 
         terms = {}
-        behind = {(0, 2): (2, 1), (1, 1): (3, 1)}
+        behind = {(1, 1): (3, 1)}
         for t in range(TILES):
             for d in range(D + 1):
                 if (t, d) in behind:
@@ -232,20 +238,27 @@ def tile_picked_lapl_silu_p_kernel(
                 )
 
         def round_sum(total, t, b0, b1):
-            nc.scalar.copy(
-                out=z_view[:, b0:b1, :, 32 * t : 32 * (t + 1), :],
-                in_=total[:].rearrange("v (b p u e) -> v b u p e", b=b1 - b0, u=2, e=2),
-            )
+            if t < 2:
+                nc.scalar.copy(
+                    out=z_view[:, b0:b1, :, 32 * t : 32 * (t + 1), :],
+                    in_=total[:].rearrange("v (b p u e) -> v b u p e", b=b1 - b0, u=2, e=2),
+                )
+            else:
+                nc.scalar.copy(
+                    out=z_view[:, b0:b1, t - 2, 64:, :],
+                    in_=total[:].rearrange("v (b q e) -> v b q e", b=b1 - b0, e=2),
+                )
 
         totals = {}
-        last_order = [1, 0, 2, 3]
+        third_order = [1, 2, 0, 3]
+        last_order = [0, 1, 2, 3]
 
-        def step(t, d):
-            if d == add_order[0]:
+        def step(t, d, order=add_order):
+            if d == order[0]:
                 totals[t] = bank("total%d" % t, 4 + t, V)
             if d > 0:
                 fetch(t, d, 0, V)
-            turn_and_add(totals[t], t, d, 0, BLOCKS, add_order)
+            turn_and_add(totals[t], t, d, 0, BLOCKS, order)
 
         project(0)
         activate(0)
@@ -255,9 +268,9 @@ def tile_picked_lapl_silu_p_kernel(
         nc.vector.quantize_mx(out=w2_code[:].bitcast(FP8X4), scales=w2_scale[:], in_=w2_stage[:])
         for z in range(PASSES):
             quantise_w1(1, z)
-        round_w1(2, 0, nc.vector.tensor_copy)
         project(1)
-        round_w1(2, 1, nc.scalar.copy, tag="w1_code0")
+        round_w1(2, 0, nc.scalar.copy, tag="w1_code0")
+        round_w1(2, 1, nc.scalar.copy)
         step(0, 1)
         activate(1)
         for z in range(PASSES):
@@ -281,31 +294,36 @@ def tile_picked_lapl_silu_p_kernel(
         step(1, 3)
         step(1, 0)
         fetch(2, 0, 0, V)
-        step(2, 1)
+        step(2, 1, third_order)
         round_sum(totals[1], 1, 0, BLOCKS)
-        step(2, 2)
-        step(2, 3)
-        step(2, 0)
         last = TILES - 1
         fetch(last, 0, 0, V)
-        fetch(last, 1, 0, V)
+        for d in third_order[1:]:
+            step(2, d, third_order)
         round_sum(totals[2], 2, 0, BLOCKS)
 
-        result = sb("result", [P, V], F32)
-        groups = [(0, 2, 7, 2, 6), (2, 3, 4, 3, 1), (3, 4, 5, 0, 7)]
+        groups = [(0, 2, 7, 2, 6), (2, 3, 4, 3, 5), (3, 4, 7, 0, 1)]
         z_cols = {}
+        backs = {g[0]: bank("back%d" % g[0], g[3], 2 * (g[1] - g[0]) * P) for g in groups}
+
+        def turn_back(b0, b1, u):
+            for b in range(b0, b1):
+                w = 2 * (b - b0) + u
+                words = z_rows[:].bitcast(F32)[:, (2 * b + u) * P : (2 * b + u + 1) * P]
+                nc.tensor.transpose(backs[b0][:, w * P : (w + 1) * P], words, ident[:])
+
+        for g in groups:
+            turn_back(g[0], g[1], 0)
         for b0, b1, sum_bank, back_bank, prod_bank in groups:
             n = (b1 - b0) * P
             total = bank("last%d" % b0, sum_bank, n)
             for d in last_order:
-                if d in last_order[2:]:
+                if d > 0:
                     fetch(last, d, b0 * P, n)
                 turn_and_add(total, last, d, b0, b1, last_order)
             round_sum(total, last, b0, b1)
-            back = bank("back%d" % b0, back_bank, 2 * n)
-            for w in range(2 * (b1 - b0)):
-                words = z_rows[:].bitcast(F32)[:, (2 * b0 + w) * P : (2 * b0 + w + 1) * P]
-                nc.tensor.transpose(back[:, w * P : (w + 1) * P], words, ident[:])
+            back = backs[b0]
+            turn_back(b0, b1, 1)
             z_cols[b0] = sb("z_cols%d" % b0, [P, n * PACK], BF16)
             weave = nc.vector.tensor_copy if b0 == 0 else nc.scalar.copy
             weave(
@@ -328,5 +346,6 @@ def tile_picked_lapl_silu_p_kernel(
                 stop=True,
             )
             leave = nc.scalar.copy if b0 == 0 else nc.vector.tensor_copy
-            leave(out=result[:, b0 * P : b1 * P], in_=prod[:])
-            nc.sync.dma_start(out=out[:, b0 * P : b1 * P], in_=result[:, b0 * P : b1 * P])
+            result = sb("result%d" % b0, [P, n], F32, tag="z_rows" if b0 == 0 else None)
+            leave(out=result[:], in_=prod[:])
+            nc.sync.dma_start(out=out[:, b0 * P : b1 * P], in_=result[:])

@@ -79,11 +79,10 @@ def tile_picked_lapl_silu_p_kernel(
         nc.sync.dma_start(
             out=scale_win[:32, :].bitcast(I32), in_=x_scales.bitcast(I32).rearrange("z b n -> b z n")
         )
-        gate_col = sb("gate_col", [P, D * PACK], F32)
-        nc.sync.dma_start(
-            out=gate_col[:].rearrange("p (d j) -> p d j", j=PACK),
-            in_=gate[:, 0, :].rearrange("d (p j) -> p d j", j=PACK),
-        )
+        run = 16
+        gate_col = sb("gate_col", [P, run], F32)
+        rows = gate.rearrange("d p v -> (d p) v")[0 : D * P : P - 1, :]
+        nc.sync.dma_start(out=gate_col[:], in_=rows.rearrange("a (b k) -> b a k", k=run))
         load_words(0)
         for d in range(D + 1):
             nc.sync.dma_start(lists[d][:], list_src[d])
@@ -91,20 +90,19 @@ def tile_picked_lapl_silu_p_kernel(
         load_w1(0, 0, first_raw[:])
         load_words(1)
 
-        factors = [None]
-        for d in range(D):
-            spread = bank("spread%d" % d, 4 + d, V)
+        weights = sb("weights", [P, D * V], F32)
+        for c in range(run // PACK):
+            spread = bank("spread%d" % c, 4 + c, PACK * P)
             for j in range(PACK):
-                column = gate_col[:, d * PACK + j : d * PACK + j + 1]
+                column = gate_col[:, c * PACK + j : c * PACK + j + 1]
                 nc.tensor.transpose(spread[:, j * P : (j + 1) * P], column.to_broadcast([P, P]), ident[:])
-            factor = sb("factor%d" % d, [P, V], F32)
             nc.scalar.activation(
-                out=factor[:].rearrange("p (n j) -> p n j", j=PACK),
-                in_=spread[:].rearrange("p (j n) -> p n j", j=PACK),
+                out=weights[:].rearrange("p (d b c j) -> p c d b j", d=D, c=run // PACK, j=PACK)[:, c],
+                in_=spread[:].rearrange("p (j b a) -> p a b j", j=PACK, a=D + 1)[:, 1:],
                 func=COPY,
                 scale=-1.0,
             )
-            factors.append(factor)
+        factors = [None] + [weights[:, d * V : (d + 1) * V] for d in range(D)]
 
         x_scale = sb("x_scale", [P, S], U8)
         x_early = sb("x_early", [P, S], U32)

@@ -49,10 +49,10 @@ def tile_picked_lapl_silu_p_kernel(
 
         part = PACK * P
         scale_win = placed("scale_win", [P, T], U8, 2048)
-        nc.gpsimd.memset(scale_win[64:, :].bitcast(I32), 0)
+        nc.vector.memset(scale_win[64:, :].bitcast(I32), 0)
         nc.vector.memset(scale_win[32:64, :].bitcast(I32), 0)
         x_plane = sb("x_plane", [P, PASSES * S], U8)
-        nc.vector.memset(x_plane[:].bitcast(I32), 0)
+        nc.gpsimd.memset(x_plane[:].bitcast(I32), 0)
         warm_in = sb("warm_in", [P, 1], F32)
         warm_out = sb("warm_out", [P, 1], F32)
         nc.gpsimd.memset(warm_in[:], 0.0)
@@ -75,10 +75,10 @@ def tile_picked_lapl_silu_p_kernel(
             rows = w1[z * part : (z + 1) * part, t * P : (t + 1) * P]
             nc.sync.dma_start(out=w1_raw[t, z], in_=rows.rearrange("(p j) c -> p j c", j=PACK))
 
-        nc.sync.dma_start(offs_sb[:], offs)
         nc.sync.dma_start(
             out=scale_win[:32, :].bitcast(I32), in_=x_scales.bitcast(I32).rearrange("z b n -> b z n")
         )
+        nc.sync.dma_start(offs_sb[:], offs)
         run = 16
         gate_col = sb("gate_col", [P, run], F32)
         rows = gate.rearrange("d p v -> (d p) v")[0 : D * P : P - 1, :]

@@ -213,8 +213,6 @@ def tile_picked_lapl_silu_p_kernel(
                     terms[t, d] = placed("term%d_%d" % (t, d), [P, V], F32, raw_at[behind[t, d]])
                 else:
                     terms[t, d] = sb("term%d_%d" % (t, d), [P, V], F32)
-        z_rows = sb("z_rows", [P, BLOCKS * H], BF16)
-        z_view = z_rows[:].rearrange("v (b u p e) -> v b u p e", b=BLOCKS, u=2, e=2)
         add_order = [1, 2, 3, 0]
 
         def fetch(t, d, v0, n):
@@ -286,21 +284,22 @@ def tile_picked_lapl_silu_p_kernel(
         activate(2)
         fetch(1, 0, 0, V)
         step(1, 1)
-        round_sum(totals[0], 0, 0, BLOCKS)
         activate(3)
         step(1, 2)
         step(1, 3)
         step(1, 0)
         fetch(2, 0, 0, V)
-        step(2, 1, third_order)
-        round_sum(totals[1], 1, 0, BLOCKS)
         last = TILES - 1
         fetch(last, 0, 0, V)
-        for d in third_order[1:]:
+        for d in third_order:
             step(2, d, third_order)
+        z_rows = sb("z_rows", [P, BLOCKS * H], BF16, tag="term2_0")
+        z_view = z_rows[:].rearrange("v (b u p e) -> v b u p e", b=BLOCKS, u=2, e=2)
+        for t in range(2):
+            round_sum(totals[t], t, 0, BLOCKS)
         round_sum(totals[2], 2, 0, BLOCKS)
 
-        groups = [(0, 2, 7, 2, 6), (2, 3, 4, 3, 5), (3, 4, 7, 0, 1)]
+        groups = [(0, 2, 7, 2, 1), (2, 3, 6, 3, 5), (3, 4, 7, 0, 4)]
         z_cols = {}
         backs = {g[0]: bank("back%d" % g[0], g[3], 2 * (g[1] - g[0]) * P) for g in groups}
 
@@ -310,9 +309,7 @@ def tile_picked_lapl_silu_p_kernel(
                 words = z_rows[:].bitcast(F32)[:, (2 * b + u) * P : (2 * b + u + 1) * P]
                 nc.tensor.transpose(backs[b0][:, w * P : (w + 1) * P], words, ident[:])
 
-        for g in groups:
-            turn_back(g[0], g[1], 0)
-        for b0, b1, sum_bank, back_bank, prod_bank in groups:
+        def sum_group(b0, b1, sum_bank):
             n = (b1 - b0) * P
             total = bank("last%d" % b0, sum_bank, n)
             for d in last_order:
@@ -320,14 +317,25 @@ def tile_picked_lapl_silu_p_kernel(
                     fetch(last, d, b0 * P, n)
                 turn_and_add(total, last, d, b0, b1, last_order)
             round_sum(total, last, b0, b1)
-            back = backs[b0]
-            turn_back(b0, b1, 1)
-            z_cols[b0] = sb("z_cols%d" % b0, [P, n * PACK], BF16)
-            weave = nc.vector.tensor_copy if b0 == 0 else nc.scalar.copy
-            weave(
+
+        def weave(b0, b1, copy):
+            z_cols[b0] = sb("z_cols%d" % b0, [P, (b1 - b0) * P * PACK], BF16)
+            copy(
                 out=z_cols[b0][:].bitcast(F32).rearrange("p (b v u) -> p b v u", u=2, v=P),
-                in_=back[:].rearrange("p (b u v) -> p b v u", u=2, v=P),
+                in_=backs[b0][:].rearrange("p (b u v) -> p b v u", u=2, v=P),
             )
+
+        first, second, third = groups
+        turn_back(first[0], first[1], 0)
+        sum_group(*first[:3])
+        sum_group(*second[:3])
+        turn_back(first[0], first[1], 1)
+        weave(first[0], first[1], nc.vector.tensor_copy)
+        sum_group(*third[:3])
+        for g in (second, third):
+            for u in range(2):
+                turn_back(g[0], g[1], u)
+            weave(g[0], g[1], nc.scalar.copy)
         for b0, b1, sum_bank, back_bank, prod_bank in groups:
             n = (b1 - b0) * P
             codes = sb("codes%d" % b0, [P, n], U32)
@@ -344,6 +352,6 @@ def tile_picked_lapl_silu_p_kernel(
                 stop=True,
             )
             leave = nc.scalar.copy if b0 == 0 else nc.vector.tensor_copy
-            result = sb("result%d" % b0, [P, n], F32, tag="z_rows" if b0 == 0 else None)
+            result = sb("result%d" % b0, [P, n], F32, tag="term2_0" if b0 == 0 else None)
             leave(out=result[:], in_=prod[:])
             nc.sync.dma_start(out=out[:, b0 * P : b1 * P], in_=result[:])

@@ -19,10 +19,14 @@ MULT = mybir.AluOpType.mult
 
 P = 128
 PACK = 4
-PASSES = K // (P * PACK)
+PART = P * PACK
+PASSES = K // PART
 TILES = H // P
 BLOCKS = V // P
+HALF = S // 2
 ENTRIES_PER_COLUMN = 16
+GATE_RUN = 16
+CUT = 768
 
 
 def tile_picked_lapl_silu_p_kernel(
@@ -35,8 +39,8 @@ def tile_picked_lapl_silu_p_kernel(
         laid = ctx.enter_context(tc.tile_pool(name="laid", bufs=1))
         psum = ctx.enter_context(tc.psum_pool(name="psum", bufs=1))
 
-        def sb(name, shape, dtype, tag=None):
-            return keep.tile(shape, dtype, name=name, tag=tag or name, align_bytes=64)
+        def sb(name, shape, dtype, over=None):
+            return keep.tile(shape, dtype, name=name, tag=over or name, align_bytes=64)
 
         def placed(name, shape, dtype, offset):
             return laid.tile(shape, dtype, name=name, tag=name, align_bytes=64, offset=offset)
@@ -47,7 +51,6 @@ def tile_picked_lapl_silu_p_kernel(
         def entries(lst, start, count):
             return lst[:, start // ENTRIES_PER_COLUMN : (start + count) // ENTRIES_PER_COLUMN]
 
-        part = PACK * P
         scale_win = placed("scale_win", [P, T], U8, 2048)
         nc.vector.memset(scale_win[64:, :].bitcast(I32), 0)
         nc.vector.memset(scale_win[32:64, :].bitcast(I32), 0)
@@ -62,8 +65,7 @@ def tile_picked_lapl_silu_p_kernel(
 
         offs_sb = held.tile([P, S // 16], U16, name="offs_sb")
         lists = [held.tile([P, V // 16], U16, name="list%d" % d) for d in range(D + 1)]
-        list_src = [cen, pos1, pos2, pos3]
-        first_words_at = 10240
+        first_words_at = 18432
         word_win = [placed("word_win0", [P, T], I32, first_words_at), sb("word_win1", [P, T], I32)]
         w1_raw = {}
 
@@ -72,37 +74,35 @@ def tile_picked_lapl_silu_p_kernel(
 
         def load_w1(t, z, room):
             w1_raw[t, z] = room.rearrange("p (j c) -> p j c", j=PACK)
-            rows = w1[z * part : (z + 1) * part, t * P : (t + 1) * P]
+            rows = w1[z * PART : (z + 1) * PART, t * P : (t + 1) * P]
             nc.sync.dma_start(out=w1_raw[t, z], in_=rows.rearrange("(p j) c -> p j c", j=PACK))
 
         nc.sync.dma_start(
             out=scale_win[:32, :].bitcast(I32), in_=x_scales.bitcast(I32).rearrange("z b n -> b z n")
         )
         nc.sync.dma_start(offs_sb[:], offs)
-        run = 16
-        gate_col = sb("gate_col", [P, run], F32)
-        rows = gate.rearrange("d p v -> (d p) v")[0 : D * P : P - 1, :]
-        nc.sync.dma_start(out=gate_col[:], in_=rows.rearrange("a (b k) -> b a k", k=run))
+        gate_col = sb("gate_col", [P, GATE_RUN], F32)
+        gate_rows = gate.rearrange("d p v -> (d p) v")[0 : D * P : P - 1, :]
+        nc.sync.dma_start(out=gate_col[:], in_=gate_rows.rearrange("a (b k) -> b a k", k=GATE_RUN))
         load_words(0)
-        for d in range(D + 1):
-            nc.sync.dma_start(lists[d][:], list_src[d])
-        first_raw = sb("first_raw", [P, part], F32)
+        for lst, src in zip(lists, (cen, pos1, pos2, pos3)):
+            nc.sync.dma_start(lst[:], src)
+        first_raw = sb("first_raw", [P, PART], F32)
         load_w1(0, 0, first_raw[:])
         load_words(1)
 
         weights = sb("weights", [P, D * V], F32)
-        for c in range(run // PACK):
+        for c in range(GATE_RUN // PACK):
             spread = bank("spread%d" % c, 4 + c, PACK * P)
             for j in range(PACK):
                 column = gate_col[:, c * PACK + j : c * PACK + j + 1]
                 nc.tensor.transpose(spread[:, j * P : (j + 1) * P], column.to_broadcast([P, P]), ident[:])
             nc.scalar.activation(
-                out=weights[:].rearrange("p (d b c j) -> p c d b j", d=D, c=run // PACK, j=PACK)[:, c],
+                out=weights[:].rearrange("p (d b c j) -> p c d b j", d=D, c=GATE_RUN // PACK, j=PACK)[:, c],
                 in_=spread[:].rearrange("p (j b a) -> p a b j", j=PACK, a=D + 1)[:, 1:],
                 func=COPY,
                 scale=-1.0,
             )
-        factors = [None] + [weights[:, d * V : (d + 1) * V] for d in range(D)]
 
         x_scale = sb("x_scale", [P, S], U8)
         x_early = sb("x_early", [P, S], U32)
@@ -113,127 +113,130 @@ def tile_picked_lapl_silu_p_kernel(
                 out=x_plane[32 * q : 32 * q + 4, :].bitcast(I32).rearrange("p (z n) -> p z n", z=PASSES),
                 in_=x_scale[8 * q : 8 * q + 8, :].bitcast(I32),
             )
-        second_raw = placed("second_raw", [P, part], F32, 64)
+        second_raw = placed("second_raw", [P, PART], F32, 64)
         load_w1(0, 1, second_raw[:])
-        next_raw = placed("next_raw", [P, (1 + PASSES) * part], F32, 4032)
-        w2_raw = next_raw[:, :part]
+        next_raw = placed("next_raw", [P, (1 + PASSES) * PART], F32, 4032)
+        w2_raw = next_raw[:, :PART]
         nc.sync.dma_start(out=w2_raw, in_=w2.rearrange("(p j) m -> p (j m)", j=PACK))
         for z in range(PASSES):
-            load_w1(1, z, next_raw[:, (1 + z) * part : (2 + z) * part])
-        raw_at = {}
+            load_w1(1, z, next_raw[:, (1 + z) * PART : (2 + z) * PART])
+        upper_at = [first_words_at + 64 - 4 * S, first_words_at + 4 * T - 64]
         for z in range(PASSES):
-            raw_at[3, z] = first_words_at + z * 2 * part * 4
-            upper = placed("upper_raw%d" % z, [P, PACK, 2 * P], F32, raw_at[3, z])
-            rows = w1[z * part : (z + 1) * part, 2 * P :]
+            upper = placed("upper_raw%d" % z, [P, PACK, 2 * P], F32, upper_at[z])
+            rows = w1[z * PART : (z + 1) * PART, 2 * P :]
             nc.sync.dma_start(out=upper[:], in_=rows.rearrange("(p j) c -> p j c", j=PACK))
             for u in range(2):
                 w1_raw[2 + u, z] = upper[:].rearrange("p j (q u e) -> p u q j e", u=2, e=2)[:, u]
 
-        w1_code = [sb("w1_code%d" % t, [P, PASSES * P], U32) for t in range(TILES)]
-        w1_scale = [sb("w1_scale%d" % t, [P, PASSES * P], U8) for t in range(TILES)]
-        stage = {}
+        stage, code, scale = {}, {}, {}
 
-        def round_weights(dst, src, copy):
+        def round_rows(dst, src, copy):
             copy(
                 out=dst.rearrange("p (c i j) -> p c j i", i=4, j=PACK),
                 in_=src.rearrange("p j (c i) -> p c j i", i=4),
             )
 
-        def round_w1(t, z, copy, tag=None):
-            stage[t, z] = sb("stage%d_%d" % (t, z), [P, part], BF16, tag=tag)
+        def round_w1(t, z, copy=nc.scalar.copy):
+            stage[t, z] = sb("stage%d_%d" % (t, z), [P, PART], BF16)
             if t < 2:
-                round_weights(stage[t, z][:], w1_raw[t, z], copy)
+                round_rows(stage[t, z][:], w1_raw[t, z], copy)
             else:
                 copy(out=stage[t, z][:].rearrange("p (q e j) -> p q j e", e=2, j=PACK), in_=w1_raw[t, z])
 
-        def quantise_w1(t, z):
-            nc.vector.quantize_mx(
-                out=w1_code[t][:, z * P : (z + 1) * P].bitcast(FP8X4),
-                scales=w1_scale[t][:, z * P : (z + 1) * P],
-                in_=stage[t, z][:],
-            )
+        def quantise_w1(t, z, over=None, at=None):
+            name = "code%d_%d" % (t, z)
+            code[t, z] = sb(name, [P, P], U32, over) if at is None else placed(name, [P, P], U32, at)
+            scale[t, z] = sb("scale%d_%d" % (t, z), [P, P], U8)
+            nc.vector.quantize_mx(out=code[t, z][:].bitcast(FP8X4), scales=scale[t, z][:], in_=stage[t, z][:])
 
-        cut = 768
-        half = S // 2
-        x_late = [sb("x_late0", [P, cut], U32)]
+        x_late = [sb("x_late0", [P, CUT], U32)]
 
         def x_code(z, s0, n):
             if z == 0:
                 return x_early[:, s0 : s0 + n]
-            return x_late[s0 // cut][:, s0 % cut : s0 % cut + n]
+            return x_late[s0 // CUT][:, s0 % CUT : s0 % CUT + n]
 
         def gather_late(s0, n):
             nc.vector.tensor_copy(x_code(1, s0, n), word_win[1][:].bitcast(U32).indirect(entries(offs_sb, s0, n)))
 
-        round_w1(0, 0, nc.scalar.copy)
-        quantise_w1(0, 0)
-        gather_late(0, cut)
-        round_w1(0, 1, nc.scalar.copy)
-        quantise_w1(0, 1)
-        x_late.append(placed("x_late1", [P, S - cut], U32, 64))
-        gather_late(cut, S - cut)
-        w2_stage = sb("w2_stage", [P, part], BF16)
-        round_weights(w2_stage[:], w2_raw.rearrange("p (j m) -> p j m", j=PACK), nc.scalar.copy)
-        round_w1(1, 0, nc.scalar.copy)
-
-        h = [sb("h%d" % t, [P, S], F32) for t in range(TILES)]
-        first_groups = [[(0, 256)], [(256, 256)], [(512, 256)], [(768, 256)]]
-        later_groups = [[(0, half)], [(half, cut - half), (cut, S - cut)]]
-        h_banks = [(0, 1, 2, 3), (0, 1), (2, 3), (0, 1)]
+        h = {t: sb("h%d" % t, [P, S], F32) for t in (0, 2, 3)}
+        h[1] = placed("h1", [P, S], F32, upper_at[0] + 64 - 4 * S)
+        acc_banks = [(0, 1, 2, 3), (0, 1), (2, 3), (0, 1)]
         accs = {}
 
-        def project(t):
-            groups = first_groups if t == 0 else later_groups
-            accs[t] = [bank("acc%d_%d" % (t, i), h_banks[t][i], sum(n for s0, n in g)) for i, g in enumerate(groups)]
-            order = [(z, i, piece) for i, g in enumerate(groups) for piece in g for z in range(PASSES)]
-            if t == 0:
-                order = sorted(order)
-            for z, i, (s0, n) in order:
-                g0 = groups[i][0][0]
-                nc.tensor.matmul_mx(
-                    out=accs[t][i][:, s0 - g0 : s0 - g0 + n],
-                    lhsT=w1_code[t][:, z * P : (z + 1) * P].bitcast(FP8X4),
-                    lhsT_scale=w1_scale[t][:, z * P : (z + 1) * P],
-                    rhs=x_code(z, s0, n).bitcast(FP8X4),
-                    rhs_scale=x_plane[:, z * S + s0 : z * S + s0 + n],
-                    start=(z == 0),
-                    stop=(z == PASSES - 1),
-                )
+        def project(t, z):
+            width = S // len(acc_banks[t])
+            if z == 0:
+                accs[t] = [bank("acc%d_%d" % (t, i), b, width) for i, b in enumerate(acc_banks[t])]
+            for i, acc in enumerate(accs[t]):
+                g0 = i * width
+                cuts = [g0, CUT, g0 + width] if z == 1 and g0 < CUT < g0 + width else [g0, g0 + width]
+                for s0, s1 in zip(cuts, cuts[1:]):
+                    nc.tensor.matmul_mx(
+                        out=acc[:, s0 - g0 : s1 - g0],
+                        lhsT=code[t, z][:].bitcast(FP8X4),
+                        lhsT_scale=scale[t, z][:],
+                        rhs=x_code(z, s0, s1 - s0).bitcast(FP8X4),
+                        rhs_scale=x_plane[:, z * S + s0 : z * S + s1],
+                        start=(z == 0),
+                        stop=(z == PASSES - 1 and s1 == g0 + width),
+                    )
 
         def activate(t):
             width = S // len(accs[t])
             for i, acc in enumerate(accs[t]):
                 nc.scalar.activation(out=h[t][:, i * width : (i + 1) * width], in_=acc[:], func=SILU)
 
-        terms = {}
-        behind = {(1, 1): (3, 1)}
-        for t in range(TILES):
-            for d in range(D + 1):
-                if (t, d) in behind:
-                    terms[t, d] = placed("term%d_%d" % (t, d), [P, V], F32, raw_at[behind[t, d]])
-                else:
-                    terms[t, d] = sb("term%d_%d" % (t, d), [P, V], F32)
-        add_order = [1, 2, 3, 0]
+        terms, totals = {}, {}
 
-        def fetch(t, d, v0, n):
+        def room_for(t, d, over=None, at=None):
+            name = "term%d_%d" % (t, d)
+            terms[t, d] = sb(name, [P, V], F32, over) if at is None else placed(name, [P, V], F32, at)
+
+        def fetch(t, d, v0=0, n=V):
             src = h[t][:].indirect(entries(lists[d], v0, n))
             if d == 0:
                 nc.scalar.activation(out=terms[t, d][:, v0 : v0 + n], in_=src, func=COPY)
             else:
-                nc.vector.tensor_tensor(terms[t, d][:, v0 : v0 + n], src, factors[d][:, v0 : v0 + n], MULT)
+                factor = weights[:, (d - 1) * V + v0 : (d - 1) * V + v0 + n]
+                nc.vector.tensor_tensor(terms[t, d][:, v0 : v0 + n], src, factor, MULT)
 
-        def turn_and_add(total, t, d, b0, b1, order):
+        def turn_and_add(total, t, d, b0, b1, first, last):
             for b in range(b0, b1):
                 nc.tensor.matmul(
                     out=total[:, (b - b0) * P : (b - b0 + 1) * P],
                     lhsT=terms[t, d][:, b * P : (b + 1) * P],
                     rhs=ident[:],
                     is_transpose=True,
-                    start=(d == order[0] and b == b0),
-                    stop=(d == order[-1] and b == b1 - 1),
+                    start=(first and b == b0),
+                    stop=(last and b == b1 - 1),
                 )
 
-        def round_sum(total, t, b0, b1):
+        add_order = [(1, 2, 3, 0), (1, 2, 0, 3), (1, 0, 2, 3)]
+
+        def add(t, d):
+            if d == add_order[t][0]:
+                totals[t] = bank("total%d" % t, 4 + t, V)
+            turn_and_add(totals[t], t, d, 0, BLOCKS, d == add_order[t][0], d == add_order[t][-1])
+
+        def room_for_two(t, d, at):
+            both = placed("terms%d_%d" % (t, d), [P, 2, V], F32, at)
+            terms[t, d], terms[t, d + 1] = both[:, 0, :], both[:, 1, :]
+
+        def neighbour(t, d, over=None, at=None):
+            if (t, d) not in terms:
+                room_for(t, d, over, at)
+            fetch(t, d)
+            add(t, d)
+
+        def centre(t, over=None, at=None):
+            room_for(t, 0, over, at)
+            fetch(t, 0)
+
+        z_rows = sb("z_rows", [P, BLOCKS * H], BF16)
+        z_view = z_rows[:].rearrange("v (b u p e) -> v b u p e", b=BLOCKS, u=2, e=2)
+
+        def round_sum(total, t, b0=0, b1=BLOCKS):
             if t < 2:
                 nc.scalar.copy(
                     out=z_view[:, b0:b1, :, 32 * t : 32 * (t + 1), :],
@@ -245,18 +248,18 @@ def tile_picked_lapl_silu_p_kernel(
                     in_=total[:].rearrange("v (b q e) -> v b q e", b=b1 - b0, e=2),
                 )
 
-        totals = {}
-        third_order = [1, 2, 0, 3]
-        last_order = [0, 1, 2, 3]
-
-        def step(t, d, order=add_order):
-            if d == order[0]:
-                totals[t] = bank("total%d" % t, 4 + t, V)
-            if d > 0:
-                fetch(t, d, 0, V)
-            turn_and_add(totals[t], t, d, 0, BLOCKS, order)
-
-        project(0)
+        round_w1(0, 0)
+        quantise_w1(0, 0)
+        gather_late(0, CUT)
+        round_w1(0, 1)
+        quantise_w1(0, 1)
+        x_late.append(placed("x_late1", [P, S - CUT], U32, 64))
+        gather_late(CUT, S - CUT)
+        w2_stage = sb("w2_stage", [P, PART], BF16)
+        round_rows(w2_stage[:], w2_raw.rearrange("p (j m) -> p j m", j=PACK), nc.scalar.copy)
+        round_w1(1, 0)
+        project(0, 0)
+        project(0, 1)
         activate(0)
         round_w1(1, 1, nc.vector.tensor_copy)
         w2_code = sb("w2_code", [P, N], U32)
@@ -264,40 +267,47 @@ def tile_picked_lapl_silu_p_kernel(
         nc.vector.quantize_mx(out=w2_code[:].bitcast(FP8X4), scales=w2_scale[:], in_=w2_stage[:])
         for z in range(PASSES):
             quantise_w1(1, z)
-        project(1)
-        round_w1(2, 0, nc.scalar.copy, tag="w1_code0")
-        round_w1(2, 1, nc.scalar.copy)
-        step(0, 1)
+            project(1, z)
+
+        round_w1(2, 0)
+        round_w1(3, 0)
+        neighbour(0, 1)
+        quantise_w1(2, 0)
+        project(2, 0)
         activate(1)
-        for z in range(PASSES):
-            quantise_w1(2, z)
-        project(2)
-        for z in range(PASSES):
-            round_w1(3, z, nc.scalar.copy)
-        fetch(0, 0, 0, V)
-        step(0, 2)
-        step(0, 3)
-        step(0, 0)
-        for z in range(PASSES):
-            quantise_w1(3, z)
-        project(3)
+        round_w1(2, 1)
+        round_w1(3, 1)
+        room_for_two(0, 2, first_words_at)
+        neighbour(0, 2)
+        neighbour(0, 3)
+        centre(0, at=upper_at[0] + 64)
+        quantise_w1(2, 1)
+        project(2, 1)
+        add(0, 0)
         activate(2)
-        fetch(1, 0, 0, V)
-        step(1, 1)
+        round_sum(totals[0], 0)
+        neighbour(1, 1, at=first_words_at + 6144)
+        neighbour(1, 2, at=first_words_at + 12160)
+        quantise_w1(3, 0, at=first_words_at + 6208)
+        project(3, 0)
+        centre(1, over="code2_1")
+        add(1, 0)
+        neighbour(1, 3, at=first_words_at + 4160)
+        quantise_w1(3, 1, at=first_words_at + 12224)
+        project(3, 1)
+        centre(2)
+        room_for_two(2, 1, first_words_at + 14144)
+        neighbour(2, 1)
+        add(2, 0)
         activate(3)
-        step(1, 2)
-        step(1, 3)
-        step(1, 0)
-        fetch(2, 0, 0, V)
+        round_sum(totals[1], 1)
+        neighbour(2, 2)
         last = TILES - 1
-        fetch(last, 0, 0, V)
-        for d in third_order:
-            step(2, d, third_order)
-        z_rows = sb("z_rows", [P, BLOCKS * H], BF16, tag="term2_0")
-        z_view = z_rows[:].rearrange("v (b u p e) -> v b u p e", b=BLOCKS, u=2, e=2)
-        for t in range(2):
-            round_sum(totals[t], t, 0, BLOCKS)
-        round_sum(totals[2], 2, 0, BLOCKS)
+        centre(last)
+        neighbour(2, 3, at=first_words_at + 10240)
+        round_sum(totals[2], 2)
+        for d in range(1, D + 1):
+            room_for(last, d)
 
         groups = [(0, 2, 7, 2, 1), (2, 3, 6, 3, 5), (3, 4, 7, 0, 4)]
         z_cols = {}
@@ -312,10 +322,10 @@ def tile_picked_lapl_silu_p_kernel(
         def sum_group(b0, b1, sum_bank):
             n = (b1 - b0) * P
             total = bank("last%d" % b0, sum_bank, n)
-            for d in last_order:
+            for d in range(D + 1):
                 if d > 0:
                     fetch(last, d, b0 * P, n)
-                turn_and_add(total, last, d, b0, b1, last_order)
+                turn_and_add(total, last, d, b0, b1, d == 0, d == D)
             round_sum(total, last, b0, b1)
 
         def weave(b0, b1, copy):
@@ -352,6 +362,6 @@ def tile_picked_lapl_silu_p_kernel(
                 stop=True,
             )
             leave = nc.scalar.copy if b0 == 0 else nc.vector.tensor_copy
-            result = sb("result%d" % b0, [P, n], F32, tag="term2_0" if b0 == 0 else None)
+            result = sb("result%d" % b0, [P, n], F32, over="z_rows" if b0 == 0 else None)
             leave(out=result[:], in_=prod[:])
             nc.sync.dma_start(out=out[:, b0 * P : b1 * P], in_=result[:])

@@ -233,8 +233,6 @@ def tile_picked_lapl_silu_p_kernel(
             room_for(t, 0, over, at)
             fetch(t, 0)
 
-        z_rows = sb("z_rows", [P, BLOCKS * H], BF16)
-        z_view = z_rows[:].rearrange("v (b u p e) -> v b u p e", b=BLOCKS, u=2, e=2)
 
         def round_sum(total, t, b0=0, b1=BLOCKS):
             if t < 2:
@@ -285,7 +283,6 @@ def tile_picked_lapl_silu_p_kernel(
         project(2, 1)
         add(0, 0)
         activate(2)
-        round_sum(totals[0], 0)
         neighbour(1, 1, at=first_words_at + 6144)
         neighbour(1, 2, at=first_words_at + 12160)
         quantise_w1(3, 0, at=first_words_at + 6208)
@@ -300,12 +297,14 @@ def tile_picked_lapl_silu_p_kernel(
         neighbour(2, 1)
         add(2, 0)
         activate(3)
-        round_sum(totals[1], 1)
         neighbour(2, 2)
         last = TILES - 1
         centre(last)
         neighbour(2, 3, at=first_words_at + 10240)
-        round_sum(totals[2], 2)
+        z_rows = sb("z_rows", [P, BLOCKS * H], BF16, over="scale3_1")
+        z_view = z_rows[:].rearrange("v (b u p e) -> v b u p e", b=BLOCKS, u=2, e=2)
+        for t in range(last):
+            round_sum(totals[t], t)
         for d in range(1, D + 1):
             room_for(last, d)
 
@@ -362,6 +361,6 @@ def tile_picked_lapl_silu_p_kernel(
                 stop=True,
             )
             leave = nc.scalar.copy if b0 == 0 else nc.vector.tensor_copy
-            result = sb("result%d" % b0, [P, n], F32, over="z_rows" if b0 == 0 else None)
+            result = sb("result%d" % b0, [P, n], F32, over="scale3_1" if b0 == 0 else None)
             leave(out=result[:], in_=prod[:])
             nc.sync.dma_start(out=out[:, b0 * P : b1 * P], in_=result[:])

@@ -115,11 +115,9 @@ def tile_picked_lapl_silu_p_kernel(
             )
         second_raw = placed("second_raw", [P, PART], F32, 64)
         load_w1(0, 1, second_raw[:])
-        next_raw = placed("next_raw", [P, (1 + PASSES) * PART], F32, 4032)
-        w2_raw = next_raw[:, :PART]
-        nc.sync.dma_start(out=w2_raw, in_=w2.rearrange("(p j) m -> p (j m)", j=PACK))
+        next_raw = placed("next_raw", [P, PASSES * PART], F32, 4032)
         for z in range(PASSES):
-            load_w1(1, z, next_raw[:, (1 + z) * PART : (2 + z) * PART])
+            load_w1(1, z, next_raw[:, z * PART : (z + 1) * PART])
         upper_at = [first_words_at + 64 - 4 * S, first_words_at + 4 * T - 64]
         for z in range(PASSES):
             upper = placed("upper_raw%d" % z, [P, PACK, 2 * P], F32, upper_at[z])
@@ -127,6 +125,8 @@ def tile_picked_lapl_silu_p_kernel(
             nc.sync.dma_start(out=upper[:], in_=rows.rearrange("(p j) c -> p j c", j=PACK))
             for u in range(2):
                 w1_raw[2 + u, z] = upper[:].rearrange("p j (q u e) -> p u q j e", u=2, e=2)[:, u]
+        w2_raw = placed("w2_raw", [P, PART], F32, first_words_at + 64)
+        nc.sync.dma_start(out=w2_raw[:], in_=w2.rearrange("(p j) m -> p (j m)", j=PACK))
 
         stage, code, scale = {}, {}, {}
 
@@ -136,8 +136,8 @@ def tile_picked_lapl_silu_p_kernel(
                 in_=src.rearrange("p j (c i) -> p c j i", i=4),
             )
 
-        def round_w1(t, z, copy=nc.scalar.copy):
-            stage[t, z] = sb("stage%d_%d" % (t, z), [P, PART], BF16)
+        def round_w1(t, z, copy=nc.scalar.copy, over=None):
+            stage[t, z] = sb("stage%d_%d" % (t, z), [P, PART], BF16, over)
             if t < 2:
                 round_rows(stage[t, z][:], w1_raw[t, z], copy)
             else:
@@ -159,8 +159,7 @@ def tile_picked_lapl_silu_p_kernel(
         def gather_late(s0, n):
             nc.vector.tensor_copy(x_code(1, s0, n), word_win[1][:].bitcast(U32).indirect(entries(offs_sb, s0, n)))
 
-        h = {t: sb("h%d" % t, [P, S], F32) for t in (0, 2, 3)}
-        h[1] = placed("h1", [P, S], F32, upper_at[0] + 64 - 4 * S)
+        h = [sb("h%d" % t, [P, S], F32) for t in range(TILES)]
         acc_banks = [(0, 1, 2, 3), (0, 1), (2, 3), (0, 1)]
         accs = {}
 
@@ -212,16 +211,17 @@ def tile_picked_lapl_silu_p_kernel(
                     stop=(last and b == b1 - 1),
                 )
 
-        add_order = [(1, 2, 3, 0), (1, 2, 0, 3), (1, 0, 2, 3)]
+        add_order = [(0, 1, 2, 3), (1, 0, 2, 3), (0, 1, 2, 3)]
 
         def add(t, d):
             if d == add_order[t][0]:
                 totals[t] = bank("total%d" % t, 4 + t, V)
             turn_and_add(totals[t], t, d, 0, BLOCKS, d == add_order[t][0], d == add_order[t][-1])
 
-        def room_for_two(t, d, at):
-            both = placed("terms%d_%d" % (t, d), [P, 2, V], F32, at)
-            terms[t, d], terms[t, d + 1] = both[:, 0, :], both[:, 1, :]
+        def room_for_all(t, over):
+            three = sb("terms%d" % t, [P, D, V], F32, over)
+            for d in range(1, D + 1):
+                terms[t, d] = three[:, d - 1, :]
 
         def neighbour(t, d, over=None, at=None):
             if (t, d) not in terms:
@@ -253,58 +253,50 @@ def tile_picked_lapl_silu_p_kernel(
         quantise_w1(0, 1)
         x_late.append(placed("x_late1", [P, S - CUT], U32, 64))
         gather_late(CUT, S - CUT)
-        w2_stage = sb("w2_stage", [P, PART], BF16)
-        round_rows(w2_stage[:], w2_raw.rearrange("p (j m) -> p j m", j=PACK), nc.scalar.copy)
         round_w1(1, 0)
         project(0, 0)
         project(0, 1)
         activate(0)
-        round_w1(1, 1, nc.vector.tensor_copy)
-        w2_code = sb("w2_code", [P, N], U32)
-        w2_scale = sb("w2_scale", [P, N], U8)
-        nc.vector.quantize_mx(out=w2_code[:].bitcast(FP8X4), scales=w2_scale[:], in_=w2_stage[:])
+        round_w1(1, 1, nc.vector.tensor_copy, over="word_win1")
         for z in range(PASSES):
             quantise_w1(1, z)
             project(1, z)
 
+        centre(0)
+        add(0, 0)
         round_w1(2, 0)
-        round_w1(3, 0)
-        neighbour(0, 1)
-        quantise_w1(2, 0)
-        project(2, 0)
         activate(1)
         round_w1(2, 1)
+        round_w1(3, 0)
         round_w1(3, 1)
-        room_for_two(0, 2, first_words_at)
-        neighbour(0, 2)
-        neighbour(0, 3)
-        centre(0, at=upper_at[0] + 64)
-        quantise_w1(2, 1)
-        project(2, 1)
-        add(0, 0)
-        activate(2)
-        neighbour(1, 1, at=first_words_at + 6144)
-        neighbour(1, 2, at=first_words_at + 12160)
-        quantise_w1(3, 0, at=first_words_at + 6208)
-        project(3, 0)
-        centre(1, over="code2_1")
+        for d in range(1, D + 1):
+            neighbour(0, d)
+        for t, z in ((2, 0), (2, 1)):
+            quantise_w1(t, z)
+            project(t, z)
+        room_for_all(1, "stage2_1")
+        neighbour(1, 1)
+        centre(1)
         add(1, 0)
-        neighbour(1, 3, at=first_words_at + 4160)
-        quantise_w1(3, 1, at=first_words_at + 12224)
-        project(3, 1)
+        activate(2)
+        neighbour(1, 2)
+        for z in range(PASSES):
+            quantise_w1(3, z, over="term0_3" if z == 0 else None)
+            project(3, z)
+        neighbour(1, 3)
         centre(2)
-        room_for_two(2, 1, first_words_at + 14144)
-        neighbour(2, 1)
         add(2, 0)
         activate(3)
-        neighbour(2, 2)
         last = TILES - 1
         centre(last)
-        neighbour(2, 3, at=first_words_at + 10240)
+        for d in range(1, D + 1):
+            neighbour(2, d)
         z_rows = sb("z_rows", [P, BLOCKS * H], BF16, over="scale3_1")
         z_view = z_rows[:].rearrange("v (b u p e) -> v b u p e", b=BLOCKS, u=2, e=2)
         for t in range(last):
             round_sum(totals[t], t)
+        w2_stage = sb("w2_stage", [P, PART], BF16, over="term2_3")
+        round_rows(w2_stage[:], w2_raw[:].rearrange("p (j m) -> p j m", j=PACK), nc.scalar.copy)
         for d in range(1, D + 1):
             room_for(last, d)
 
@@ -341,6 +333,9 @@ def tile_picked_lapl_silu_p_kernel(
         turn_back(first[0], first[1], 1)
         weave(first[0], first[1], nc.vector.tensor_copy)
         sum_group(*third[:3])
+        w2_code = sb("w2_code", [P, N], U32)
+        w2_scale = sb("w2_scale", [P, N], U8)
+        nc.vector.quantize_mx(out=w2_code[:].bitcast(FP8X4), scales=w2_scale[:], in_=w2_stage[:])
         for g in (second, third):
             for u in range(2):
                 turn_back(g[0], g[1], u)

@@ -119,12 +119,11 @@ def tile_picked_lapl_silu_p_kernel(
         for z in range(PASSES):
             load_w1(1, z, next_raw[:, z * PART : (z + 1) * PART])
         upper_at = [first_words_at + 64 - 4 * S, first_words_at + 4 * T - 64]
+        upper = []
         for z in range(PASSES):
-            upper = placed("upper_raw%d" % z, [P, PACK, 2 * P], F32, upper_at[z])
+            upper.append(placed("upper_raw%d" % z, [P, PACK, 2 * P], F32, upper_at[z]))
             rows = w1[z * PART : (z + 1) * PART, 2 * P :]
-            nc.sync.dma_start(out=upper[:], in_=rows.rearrange("(p j) c -> p j c", j=PACK))
-            for u in range(2):
-                w1_raw[2 + u, z] = upper[:].rearrange("p j (q u e) -> p u q j e", u=2, e=2)[:, u]
+            nc.sync.dma_start(out=upper[z][:], in_=rows.rearrange("(p j) c -> p j c", j=PACK))
         w2_raw = placed("w2_raw", [P, PART], F32, first_words_at + 64)
         nc.sync.dma_start(out=w2_raw[:], in_=w2.rearrange("(p j) m -> p (j m)", j=PACK))
 
@@ -138,10 +137,15 @@ def tile_picked_lapl_silu_p_kernel(
 
         def round_w1(t, z, copy=nc.scalar.copy, over=None):
             stage[t, z] = sb("stage%d_%d" % (t, z), [P, PART], BF16, over)
-            if t < 2:
-                round_rows(stage[t, z][:], w1_raw[t, z], copy)
-            else:
-                copy(out=stage[t, z][:].rearrange("p (q e j) -> p q j e", e=2, j=PACK), in_=w1_raw[t, z])
+            round_rows(stage[t, z][:], w1_raw[t, z], copy)
+
+        def round_upper(z):
+            both = sb("stage_upper%d" % z, [P, 2 * PART], BF16)
+            nc.scalar.copy(
+                out=both[:].rearrange("p (u q e j) -> p q j u e", u=2, e=2, j=PACK),
+                in_=upper[z][:].rearrange("p j (q u e) -> p q j u e", u=2, e=2),
+            )
+            stage[2, z], stage[3, z] = both[:, :PART], both[:, PART:]
 
         def quantise_w1(t, z, over=None, at=None):
             name = "code%d_%d" % (t, z)
@@ -163,23 +167,25 @@ def tile_picked_lapl_silu_p_kernel(
         acc_banks = [(0, 1, 2, 3), (0, 1), (2, 3), (0, 1)]
         accs = {}
 
-        def project(t, z):
-            width = S // len(acc_banks[t])
-            if z == 0:
-                accs[t] = [bank("acc%d_%d" % (t, i), b, width) for i, b in enumerate(acc_banks[t])]
-            for i, acc in enumerate(accs[t]):
-                g0 = i * width
-                cuts = [g0, CUT, g0 + width] if z == 1 and g0 < CUT < g0 + width else [g0, g0 + width]
-                for s0, s1 in zip(cuts, cuts[1:]):
-                    nc.tensor.matmul_mx(
-                        out=acc[:, s0 - g0 : s1 - g0],
-                        lhsT=code[t, z][:].bitcast(FP8X4),
-                        lhsT_scale=scale[t, z][:],
-                        rhs=x_code(z, s0, s1 - s0).bitcast(FP8X4),
-                        rhs_scale=x_plane[:, z * S + s0 : z * S + s1],
-                        start=(z == 0),
-                        stop=(z == PASSES - 1 and s1 == g0 + width),
-                    )
+        spans = [[(256 * i, 256)] for i in range(4)], [[(0, HALF)], [(HALF, CUT - HALF), (CUT, S - CUT)]]
+
+        def project(t):
+            groups = spans[min(t, 1)]
+            accs[t] = [bank("acc%d_%d" % (t, i), acc_banks[t][i], S // len(groups)) for i in range(len(groups))]
+            order = [(z, i, piece) for i, g in enumerate(groups) for piece in g for z in range(PASSES)]
+            if t == 0:
+                order = sorted(order)
+            for z, i, (s0, n) in order:
+                g0 = groups[i][0][0]
+                nc.tensor.matmul_mx(
+                    out=accs[t][i][:, s0 - g0 : s0 - g0 + n],
+                    lhsT=code[t, z][:].bitcast(FP8X4),
+                    lhsT_scale=scale[t, z][:],
+                    rhs=x_code(z, s0, n).bitcast(FP8X4),
+                    rhs_scale=x_plane[:, z * S + s0 : z * S + s0 + n],
+                    start=(z == 0),
+                    stop=(z == PASSES - 1),
+                )
 
         def activate(t):
             width = S // len(accs[t])
@@ -211,17 +217,12 @@ def tile_picked_lapl_silu_p_kernel(
                     stop=(last and b == b1 - 1),
                 )
 
-        add_order = [(0, 1, 2, 3), (1, 0, 2, 3), (0, 1, 2, 3)]
+        add_order = [(1, 2, 3, 0), (1, 0, 2, 3), (0, 1, 2, 3)]
 
         def add(t, d):
             if d == add_order[t][0]:
                 totals[t] = bank("total%d" % t, 4 + t, V)
             turn_and_add(totals[t], t, d, 0, BLOCKS, d == add_order[t][0], d == add_order[t][-1])
-
-        def room_for_all(t, over):
-            three = sb("terms%d" % t, [P, D, V], F32, over)
-            for d in range(1, D + 1):
-                terms[t, d] = three[:, d - 1, :]
 
         def neighbour(t, d, over=None, at=None):
             if (t, d) not in terms:
@@ -254,35 +255,31 @@ def tile_picked_lapl_silu_p_kernel(
         x_late.append(placed("x_late1", [P, S - CUT], U32, 64))
         gather_late(CUT, S - CUT)
         round_w1(1, 0)
-        project(0, 0)
-        project(0, 1)
+        project(0)
         activate(0)
         round_w1(1, 1, nc.vector.tensor_copy, over="word_win1")
         for z in range(PASSES):
             quantise_w1(1, z)
-            project(1, z)
+        project(1)
 
-        centre(0)
-        add(0, 0)
-        round_w1(2, 0)
+        for z in range(PASSES):
+            round_upper(z)
         activate(1)
-        round_w1(2, 1)
-        round_w1(3, 0)
-        round_w1(3, 1)
+        centre(0)
         for d in range(1, D + 1):
             neighbour(0, d)
-        for t, z in ((2, 0), (2, 1)):
-            quantise_w1(t, z)
-            project(t, z)
-        room_for_all(1, "stage2_1")
+        for z in range(PASSES):
+            quantise_w1(2, z)
+        project(2)
+        add(0, 0)
         neighbour(1, 1)
         centre(1)
         add(1, 0)
         activate(2)
         neighbour(1, 2)
         for z in range(PASSES):
-            quantise_w1(3, z, over="term0_3" if z == 0 else None)
-            project(3, z)
+            quantise_w1(3, z, over="term1_1" if z == 0 else "term0_0")
+        project(3)
         neighbour(1, 3)
         centre(2)
         add(2, 0)

@@ -145,7 +145,14 @@ def tile_picked_lapl_silu_p_kernel(
                 out=both[:].rearrange("p (u q e j) -> p q j u e", u=2, e=2, j=PACK),
                 in_=upper[z][:].rearrange("p j (q u e) -> p q j u e", u=2, e=2),
             )
-            stage[2, z], stage[3, z] = both[:, :PART], both[:, PART:]
+            stage["upper", z] = both
+
+        def quantise_upper(z):
+            codes = sb("code_upper%d" % z, [P, 2 * P], U32)
+            scales = sb("scale_upper%d" % z, [P, 2 * P], U8)
+            nc.vector.quantize_mx(out=codes[:].bitcast(FP8X4), scales=scales[:], in_=stage["upper", z][:])
+            for u in range(2):
+                code[2 + u, z], scale[2 + u, z] = codes[:, u * P : (u + 1) * P], scales[:, u * P : (u + 1) * P]
 
         def quantise_w1(t, z, over=None, at=None):
             name = "code%d_%d" % (t, z)
@@ -217,7 +224,7 @@ def tile_picked_lapl_silu_p_kernel(
                     stop=(last and b == b1 - 1),
                 )
 
-        add_order = [(1, 2, 3, 0), (1, 0, 2, 3), (0, 1, 2, 3)]
+        add_order = [(1, 2, 3, 0), (1, 2, 3, 0), (1, 2, 0, 3)]
 
         def add(t, d):
             if d == add_order[t][0]:
@@ -269,26 +276,25 @@ def tile_picked_lapl_silu_p_kernel(
         for d in range(1, D + 1):
             neighbour(0, d)
         for z in range(PASSES):
-            quantise_w1(2, z)
+            quantise_upper(z)
         project(2)
         add(0, 0)
+        project(3)
         neighbour(1, 1)
         centre(1)
-        add(1, 0)
         activate(2)
         neighbour(1, 2)
-        for z in range(PASSES):
-            quantise_w1(3, z, over="term1_1" if z == 0 else "term0_0")
-        project(3)
         neighbour(1, 3)
-        centre(2)
-        add(2, 0)
+        add(1, 0)
         activate(3)
+        centre(2)
         last = TILES - 1
         centre(last)
-        for d in range(1, D + 1):
-            neighbour(2, d)
-        z_rows = sb("z_rows", [P, BLOCKS * H], BF16, over="scale3_1")
+        neighbour(2, 1)
+        neighbour(2, 2)
+        add(2, 0)
+        neighbour(2, 3)
+        z_rows = sb("z_rows", [P, BLOCKS * H], BF16, over="term2_0")
         z_view = z_rows[:].rearrange("v (b u p e) -> v b u p e", b=BLOCKS, u=2, e=2)
         for t in range(last):
             round_sum(totals[t], t)
@@ -353,6 +359,6 @@ def tile_picked_lapl_silu_p_kernel(
                 stop=True,
             )
             leave = nc.scalar.copy if b0 == 0 else nc.vector.tensor_copy
-            result = sb("result%d" % b0, [P, n], F32, over="scale3_1" if b0 == 0 else None)
+            result = sb("result%d" % b0, [P, n], F32, over="term2_0" if b0 == 0 else None)
             leave(out=result[:], in_=prod[:])
             nc.sync.dma_start(out=out[:, b0 * P : b1 * P], in_=result[:])

@@ -124,7 +124,8 @@ def tile_picked_lapl_silu_p_kernel(
             upper.append(placed("upper_raw%d" % z, [P, PACK, 2 * P], F32, upper_at[z]))
             rows = w1[z * PART : (z + 1) * PART, 2 * P :]
             nc.sync.dma_start(out=upper[z][:], in_=rows.rearrange("(p j) c -> p j c", j=PACK))
-        w2_raw = placed("w2_raw", [P, PART], F32, first_words_at + 64)
+        w2_at = first_words_at + 64
+        w2_raw = placed("w2_raw", [P, PART], F32, w2_at)
         nc.sync.dma_start(out=w2_raw[:], in_=w2.rearrange("(p j) m -> p (j m)", j=PACK))
 
         stage, code, scale = {}, {}, {}
@@ -174,12 +175,16 @@ def tile_picked_lapl_silu_p_kernel(
         acc_banks = [(0, 1, 2, 3), (0, 1), (2, 3), (0, 1)]
         accs = {}
 
-        spans = [[(256 * i, 256)] for i in range(4)], [[(0, HALF)], [(HALF, CUT - HALF), (CUT, S - CUT)]]
+        spans = [[(256 * i, 256)] for i in range(4)], [[(0, HALF)], [(HALF, CUT - HALF), (CUT, S - CUT)]], [[(0, HALF)], [(HALF, HALF)]]
 
-        def project(t):
+        def project(t, passes=range(PASSES)):
             groups = spans[min(t, 1)]
-            accs[t] = [bank("acc%d_%d" % (t, i), acc_banks[t][i], S // len(groups)) for i in range(len(groups))]
-            order = [(z, i, piece) for i, g in enumerate(groups) for piece in g for z in range(PASSES)]
+            if 0 in passes:
+                accs[t] = [bank("acc%d_%d" % (t, i), acc_banks[t][i], S // len(groups)) for i in range(len(groups))]
+            if t < 2:
+                order = [(z, i, piece) for i, g in enumerate(groups) for piece in g for z in passes]
+            else:
+                order = [(z, i, piece) for z in passes for i, g in enumerate(spans[1 + (z == 0)]) for piece in g]
             if t == 0:
                 order = sorted(order)
             for z, i, (s0, n) in order:
@@ -191,7 +196,7 @@ def tile_picked_lapl_silu_p_kernel(
                     rhs=x_code(z, s0, n).bitcast(FP8X4),
                     rhs_scale=x_plane[:, z * S + s0 : z * S + s0 + n],
                     start=(z == 0),
-                    stop=(z == PASSES - 1),
+                    stop=(z == PASSES - 1 and (t < 2 or s0 + n in (HALF, S))),
                 )
 
         def activate(t):
@@ -213,23 +218,24 @@ def tile_picked_lapl_silu_p_kernel(
                 factor = weights[:, (d - 1) * V + v0 : (d - 1) * V + v0 + n]
                 nc.vector.tensor_tensor(terms[t, d][:, v0 : v0 + n], src, factor, MULT)
 
-        def turn_and_add(total, t, d, b0, b1, first, last):
-            for b in range(b0, b1):
+        def turn_and_add(total, term, first, final):
+            blocks = term.shape[-1] // P
+            for b in range(blocks):
                 nc.tensor.matmul(
-                    out=total[:, (b - b0) * P : (b - b0 + 1) * P],
-                    lhsT=terms[t, d][:, b * P : (b + 1) * P],
+                    out=total[:, b * P : (b + 1) * P],
+                    lhsT=term[:, b * P : (b + 1) * P],
                     rhs=ident[:],
                     is_transpose=True,
-                    start=(first and b == b0),
-                    stop=(last and b == b1 - 1),
+                    start=(first and b == 0),
+                    stop=(final and b == blocks - 1),
                 )
 
-        add_order = [(1, 2, 3, 0), (1, 2, 3, 0), (1, 2, 0, 3)]
+        add_order = [(1, 2, 3, 0), (1, 0, 2, 3), (1, 0, 2, 3)]
 
         def add(t, d):
             if d == add_order[t][0]:
                 totals[t] = bank("total%d" % t, 4 + t, V)
-            turn_and_add(totals[t], t, d, 0, BLOCKS, d == add_order[t][0], d == add_order[t][-1])
+            turn_and_add(totals[t], terms[t, d][:], d == add_order[t][0], d == add_order[t][-1])
 
         def neighbour(t, d, over=None, at=None):
             if (t, d) not in terms:
@@ -269,60 +275,73 @@ def tile_picked_lapl_silu_p_kernel(
             quantise_w1(1, z)
         project(1)
 
-        for z in range(PASSES):
-            round_upper(z)
+        round_upper(0)
         activate(1)
-        centre(0)
-        for d in range(1, D + 1):
-            neighbour(0, d)
-        for z in range(PASSES):
-            quantise_upper(z)
-        project(2)
+        round_upper(1)
+        centre(0, at=upper_at[1] + 64 - 4 * V)
+        neighbour(0, 1)
+        neighbour(0, 2)
+        quantise_upper(0)
+        for t in (2, 3):
+            project(t, [0])
+        neighbour(0, 3, at=upper_at[0])
+        quantise_upper(1)
+        for t in (2, 3):
+            project(t, [1])
         add(0, 0)
-        project(3)
+        three = placed("terms1", [P, D, V], F32, upper_at[1] + 64)
+        for d in range(1, D + 1):
+            terms[1, d] = three[:, d - 1, :]
         neighbour(1, 1)
         centre(1)
+        add(1, 0)
         activate(2)
+        activate(3)
         neighbour(1, 2)
         neighbour(1, 3)
-        add(1, 0)
-        activate(3)
         centre(2)
         last = TILES - 1
         centre(last)
         neighbour(2, 1)
-        neighbour(2, 2)
         add(2, 0)
+        neighbour(2, 2)
+
+        groups = [(0, 2, 7, 2, 1), (2, 3, 0, 7, 5), (3, 4, 1, 0, 6)]
+        sums = {}
+        for b0, b1, sum_bank, back_bank, prod_bank in groups:
+            sums[b0] = bank("last%d" % b0, sum_bank, (b1 - b0) * P)
+            turn_and_add(sums[b0], terms[last, 0][:, b0 * P : b1 * P], True, False)
         neighbour(2, 3)
         z_rows = sb("z_rows", [P, BLOCKS * H], BF16, over="term2_0")
         z_view = z_rows[:].rearrange("v (b u p e) -> v b u p e", b=BLOCKS, u=2, e=2)
+        w2_stage = sb("w2_stage", [P, PART], BF16, over="term2_1")
+        round_rows(w2_stage[:], w2_raw[:].rearrange("p (j m) -> p j m", j=PACK), nc.scalar.copy)
         for t in range(last):
             round_sum(totals[t], t)
-        w2_stage = sb("w2_stage", [P, PART], BF16, over="term2_3")
-        round_rows(w2_stage[:], w2_raw[:].rearrange("p (j m) -> p j m", j=PACK), nc.scalar.copy)
-        for d in range(1, D + 1):
-            room_for(last, d)
+        halves = [sb("last_terms0", [P, D, V // 2], F32), sb("last_terms1", [P, D, V // 2], F32)]
 
-        groups = [(0, 2, 7, 2, 1), (2, 3, 6, 3, 5), (3, 4, 7, 0, 4)]
-        z_cols = {}
-        backs = {g[0]: bank("back%d" % g[0], g[3], 2 * (g[1] - g[0]) * P) for g in groups}
+        z_cols, backs = {}, {}
 
-        def turn_back(b0, b1, u):
+        def turn_back(group, u):
+            b0, b1 = group[:2]
+            if u == 0:
+                backs[b0] = bank("back%d" % b0, group[3], 2 * (b1 - b0) * P)
             for b in range(b0, b1):
                 w = 2 * (b - b0) + u
                 words = z_rows[:].bitcast(F32)[:, (2 * b + u) * P : (2 * b + u + 1) * P]
                 nc.tensor.transpose(backs[b0][:, w * P : (w + 1) * P], words, ident[:])
 
-        def sum_group(b0, b1, sum_bank):
-            n = (b1 - b0) * P
-            total = bank("last%d" % b0, sum_bank, n)
-            for d in range(D + 1):
-                if d > 0:
-                    fetch(last, d, b0 * P, n)
-                turn_and_add(total, last, d, b0, b1, d == 0, d == D)
-            round_sum(total, last, b0, b1)
+        def sum_group(group):
+            b0, b1 = group[:2]
+            v0, n = b0 * P, (b1 - b0) * P
+            for d in range(1, D + 1):
+                term = halves[2 * v0 // V][:, d - 1, v0 % (V // 2) : v0 % (V // 2) + n]
+                factor = weights[:, (d - 1) * V + v0 : (d - 1) * V + v0 + n]
+                nc.vector.tensor_tensor(term, h[last][:].indirect(entries(lists[d], v0, n)), factor, MULT)
+                turn_and_add(sums[b0], term, False, d == D)
 
-        def weave(b0, b1, copy):
+        def weave(group, copy):
+            b0, b1 = group[:2]
             z_cols[b0] = sb("z_cols%d" % b0, [P, (b1 - b0) * P * PACK], BF16)
             copy(
                 out=z_cols[b0][:].bitcast(F32).rearrange("p (b v u) -> p b v u", u=2, v=P),
@@ -330,19 +349,22 @@ def tile_picked_lapl_silu_p_kernel(
             )
 
         first, second, third = groups
-        turn_back(first[0], first[1], 0)
-        sum_group(*first[:3])
-        sum_group(*second[:3])
-        turn_back(first[0], first[1], 1)
-        weave(first[0], first[1], nc.vector.tensor_copy)
-        sum_group(*third[:3])
-        w2_code = sb("w2_code", [P, N], U32)
+        sum_group(first)
+        turn_back(first, 0)
+        round_sum(sums[first[0]], last, *first[:2])
+        sum_group(second)
+        round_sum(sums[second[0]], last, *second[:2])
+        turn_back(first, 1)
+        weave(first, nc.vector.tensor_copy)
+        sum_group(third)
+        round_sum(sums[third[0]], last, *third[:2])
+        w2_code = sb("w2_code", [P, N], U32, over="last_terms1")
         w2_scale = sb("w2_scale", [P, N], U8)
         nc.vector.quantize_mx(out=w2_code[:].bitcast(FP8X4), scales=w2_scale[:], in_=w2_stage[:])
         for g in (second, third):
             for u in range(2):
-                turn_back(g[0], g[1], u)
-            weave(g[0], g[1], nc.scalar.copy)
+                turn_back(g, u)
+            weave(g, nc.scalar.copy)
         for b0, b1, sum_bank, back_bank, prod_bank in groups:
             n = (b1 - b0) * P
             codes = sb("codes%d" % b0, [P, n], U32)

@@ -140,24 +140,14 @@ def tile_picked_lapl_silu_p_kernel(
             stage[t, z] = sb("stage%d_%d" % (t, z), [P, PART], BF16, over)
             round_rows(stage[t, z][:], w1_raw[t, z], copy)
 
-        def round_upper(z):
-            both = sb("stage_upper%d" % z, [P, 2 * PART], BF16)
+        def round_upper(z, dst):
             nc.scalar.copy(
-                out=both[:].rearrange("p (u q e j) -> p q j u e", u=2, e=2, j=PACK),
+                out=dst.rearrange("p (u q e j) -> p q j u e", u=2, e=2, j=PACK),
                 in_=upper[z][:].rearrange("p j (q u e) -> p q j u e", u=2, e=2),
             )
-            stage["upper", z] = both
 
-        def quantise_upper(z):
-            codes = sb("code_upper%d" % z, [P, 2 * P], U32)
-            scales = sb("scale_upper%d" % z, [P, 2 * P], U8)
-            nc.vector.quantize_mx(out=codes[:].bitcast(FP8X4), scales=scales[:], in_=stage["upper", z][:])
-            for u in range(2):
-                code[2 + u, z], scale[2 + u, z] = codes[:, u * P : (u + 1) * P], scales[:, u * P : (u + 1) * P]
-
-        def quantise_w1(t, z, over=None, at=None):
-            name = "code%d_%d" % (t, z)
-            code[t, z] = sb(name, [P, P], U32, over) if at is None else placed(name, [P, P], U32, at)
+        def quantise_w1(t, z):
+            code[t, z] = sb("code%d_%d" % (t, z), [P, P], U32)
             scale[t, z] = sb("scale%d_%d" % (t, z), [P, P], U8)
             nc.vector.quantize_mx(out=code[t, z][:].bitcast(FP8X4), scales=scale[t, z][:], in_=stage[t, z][:])
 
@@ -175,16 +165,12 @@ def tile_picked_lapl_silu_p_kernel(
         acc_banks = [(0, 1, 2, 3), (0, 1), (2, 3), (0, 1)]
         accs = {}
 
-        spans = [[(256 * i, 256)] for i in range(4)], [[(0, HALF)], [(HALF, CUT - HALF), (CUT, S - CUT)]], [[(0, HALF)], [(HALF, HALF)]]
+        spans = [[(256 * i, 256)] for i in range(4)], [[(0, HALF)], [(HALF, CUT - HALF), (CUT, S - CUT)]]
 
-        def project(t, passes=range(PASSES)):
+        def project(t):
             groups = spans[min(t, 1)]
-            if 0 in passes:
-                accs[t] = [bank("acc%d_%d" % (t, i), acc_banks[t][i], S // len(groups)) for i in range(len(groups))]
-            if t < 2:
-                order = [(z, i, piece) for i, g in enumerate(groups) for piece in g for z in passes]
-            else:
-                order = [(z, i, piece) for z in passes for i, g in enumerate(spans[1 + (z == 0)]) for piece in g]
+            accs[t] = [bank("acc%d_%d" % (t, i), acc_banks[t][i], S // len(groups)) for i in range(len(groups))]
+            order = [(z, i, piece) for i, g in enumerate(groups) for piece in g for z in range(PASSES)]
             if t == 0:
                 order = sorted(order)
             for z, i, (s0, n) in order:
@@ -196,13 +182,13 @@ def tile_picked_lapl_silu_p_kernel(
                     rhs=x_code(z, s0, n).bitcast(FP8X4),
                     rhs_scale=x_plane[:, z * S + s0 : z * S + s0 + n],
                     start=(z == 0),
-                    stop=(z == PASSES - 1 and (t < 2 or s0 + n in (HALF, S))),
+                    stop=(z == PASSES - 1),
                 )
 
-        def activate(t):
+        def activate(t, which=None):
             width = S // len(accs[t])
-            for i, acc in enumerate(accs[t]):
-                nc.scalar.activation(out=h[t][:, i * width : (i + 1) * width], in_=acc[:], func=SILU)
+            for i in which or range(len(accs[t])):
+                nc.scalar.activation(out=h[t][:, i * width : (i + 1) * width], in_=accs[t][i][:], func=SILU)
 
         terms, totals = {}, {}
 
@@ -230,7 +216,7 @@ def tile_picked_lapl_silu_p_kernel(
                     stop=(final and b == blocks - 1),
                 )
 
-        add_order = [(1, 2, 3, 0), (1, 0, 2, 3), (1, 0, 2, 3)]
+        add_order = [(1, 2, 0, 3), (1, 0, 2, 3), (1, 0, 2, 3)]
 
         def add(t, d):
             if d == add_order[t][0]:
@@ -275,23 +261,26 @@ def tile_picked_lapl_silu_p_kernel(
             quantise_w1(1, z)
         project(1)
 
-        round_upper(0)
-        activate(1)
-        round_upper(1)
+        activate(1, [0])
+        upper_stage = sb("upper_stage", [P, PASSES * 2 * PART], BF16, over="code1_1")
+        for z in range(PASSES):
+            round_upper(z, upper_stage[:, z * 2 * PART : (z + 1) * 2 * PART])
+        activate(1, [1])
         centre(0, at=upper_at[1] + 64 - 4 * V)
         neighbour(0, 1)
         neighbour(0, 2)
-        quantise_upper(0)
+        room_for(0, 3)
+        fetch(0, 3)
+        upper_code = sb("upper_code", [P, PASSES * 2 * P], U32)
+        upper_scale = sb("upper_scale", [P, PASSES * 2 * P], U8)
+        nc.vector.quantize_mx(out=upper_code[:].bitcast(FP8X4), scales=upper_scale[:], in_=upper_stage[:])
         for t in (2, 3):
-            project(t, [0])
-        neighbour(0, 3, at=upper_at[0])
-        quantise_upper(1)
-        for t in (2, 3):
-            project(t, [1])
+            for z in range(PASSES):
+                cols = slice((2 * z + t - 2) * P, (2 * z + t - 1) * P)
+                code[t, z], scale[t, z] = upper_code[:, cols], upper_scale[:, cols]
+            project(t)
         add(0, 0)
-        three = placed("terms1", [P, D, V], F32, upper_at[1] + 64)
-        for d in range(1, D + 1):
-            terms[1, d] = three[:, d - 1, :]
+        add(0, 3)
         neighbour(1, 1)
         centre(1)
         add(1, 0)

@@ -140,9 +140,9 @@ def tile_picked_lapl_silu_p_kernel(
             stage[t, z] = sb("stage%d_%d" % (t, z), [P, PART], BF16, over)
             round_rows(stage[t, z][:], w1_raw[t, z], copy)
 
-        def round_upper(z, dst):
+        def round_upper(z, staged):
             nc.scalar.copy(
-                out=dst.rearrange("p (u q e j) -> p q j u e", u=2, e=2, j=PACK),
+                out=staged.rearrange("p (u z q e j) -> p z q j u e", u=2, z=PASSES, e=2, j=PACK)[:, z],
                 in_=upper[z][:].rearrange("p j (q u e) -> p q j u e", u=2, e=2),
             )
 
@@ -264,20 +264,20 @@ def tile_picked_lapl_silu_p_kernel(
         activate(1, [0])
         upper_stage = sb("upper_stage", [P, PASSES * 2 * PART], BF16, over="code1_1")
         for z in range(PASSES):
-            round_upper(z, upper_stage[:, z * 2 * PART : (z + 1) * 2 * PART])
+            round_upper(z, upper_stage[:])
         activate(1, [1])
         centre(0, at=upper_at[1] + 64 - 4 * V)
         neighbour(0, 1)
         neighbour(0, 2)
         room_for(0, 3)
         fetch(0, 3)
-        upper_code = sb("upper_code", [P, PASSES * 2 * P], U32)
-        upper_scale = sb("upper_scale", [P, PASSES * 2 * P], U8)
-        nc.vector.quantize_mx(out=upper_code[:].bitcast(FP8X4), scales=upper_scale[:], in_=upper_stage[:])
         for t in (2, 3):
+            codes = sb("code%d" % t, [P, PASSES * P], U32)
+            scales = sb("scale%d" % t, [P, PASSES * P], U8)
+            staged = upper_stage[:, (t - 2) * K : (t - 1) * K]
+            nc.vector.quantize_mx(out=codes[:].bitcast(FP8X4), scales=scales[:], in_=staged)
             for z in range(PASSES):
-                cols = slice((2 * z + t - 2) * P, (2 * z + t - 1) * P)
-                code[t, z], scale[t, z] = upper_code[:, cols], upper_scale[:, cols]
+                code[t, z], scale[t, z] = codes[:, z * P : (z + 1) * P], scales[:, z * P : (z + 1) * P]
             project(t)
         add(0, 0)
         add(0, 3)
@@ -291,6 +291,8 @@ def tile_picked_lapl_silu_p_kernel(
         centre(2)
         last = TILES - 1
         centre(last)
+        plain = sb("plain", [P, V // 2], F32)
+        nc.scalar.activation(out=plain[:], in_=h[last][:].indirect(entries(lists[D], 0, V // 2)), func=COPY)
         neighbour(2, 1)
         add(2, 0)
         neighbour(2, 2)
@@ -303,11 +305,9 @@ def tile_picked_lapl_silu_p_kernel(
         neighbour(2, 3)
         z_rows = sb("z_rows", [P, BLOCKS * H], BF16, over="term2_0")
         z_view = z_rows[:].rearrange("v (b u p e) -> v b u p e", b=BLOCKS, u=2, e=2)
-        w2_stage = sb("w2_stage", [P, PART], BF16, over="term2_1")
-        round_rows(w2_stage[:], w2_raw[:].rearrange("p (j m) -> p j m", j=PACK), nc.scalar.copy)
         for t in range(last):
             round_sum(totals[t], t)
-        halves = [sb("last_terms0", [P, D, V // 2], F32), sb("last_terms1", [P, D, V // 2], F32)]
+        halves = [sb("last_terms0", [P, D, V // 2], F32), sb("last_terms1", [P, D, V // 2], F32, over="term3_0")]
 
         z_cols, backs = {}, {}
 
@@ -326,7 +326,8 @@ def tile_picked_lapl_silu_p_kernel(
             for d in range(1, D + 1):
                 term = halves[2 * v0 // V][:, d - 1, v0 % (V // 2) : v0 % (V // 2) + n]
                 factor = weights[:, (d - 1) * V + v0 : (d - 1) * V + v0 + n]
-                nc.vector.tensor_tensor(term, h[last][:].indirect(entries(lists[d], v0, n)), factor, MULT)
+                src = plain[:] if (b0, d) == (0, D) else h[last][:].indirect(entries(lists[d], v0, n))
+                nc.vector.tensor_tensor(term, src, factor, MULT)
                 turn_and_add(sums[b0], term, False, d == D)
 
         def weave(group, copy):
@@ -341,13 +342,15 @@ def tile_picked_lapl_silu_p_kernel(
         sum_group(first)
         turn_back(first, 0)
         round_sum(sums[first[0]], last, *first[:2])
+        w2_stage = sb("w2_stage", [P, PART], BF16, over="last_terms0")
+        round_rows(w2_stage[:], w2_raw[:].rearrange("p (j m) -> p j m", j=PACK), nc.scalar.copy)
         sum_group(second)
         round_sum(sums[second[0]], last, *second[:2])
         turn_back(first, 1)
         weave(first, nc.vector.tensor_copy)
         sum_group(third)
         round_sum(sums[third[0]], last, *third[:2])
-        w2_code = sb("w2_code", [P, N], U32, over="last_terms1")
+        w2_code = sb("w2_code", [P, N], U32, over="term3_0")
         w2_scale = sb("w2_scale", [P, N], U8)
         nc.vector.quantize_mx(out=w2_code[:].bitcast(FP8X4), scales=w2_scale[:], in_=w2_stage[:])
         for g in (second, third):

@@ -291,8 +291,8 @@ def tile_picked_lapl_silu_p_kernel(
         centre(2)
         last = TILES - 1
         centre(last)
-        plain = sb("plain", [P, V // 2], F32)
-        nc.scalar.activation(out=plain[:], in_=h[last][:].indirect(entries(lists[D], 0, V // 2)), func=COPY)
+        plain = sb("plain", [P, V - P], F32)
+        nc.scalar.activation(out=plain[:], in_=h[last][:].indirect(entries(lists[D], 0, V - P)), func=COPY)
         neighbour(2, 1)
         add(2, 0)
         neighbour(2, 2)
@@ -326,7 +326,8 @@ def tile_picked_lapl_silu_p_kernel(
             for d in range(1, D + 1):
                 term = halves[2 * v0 // V][:, d - 1, v0 % (V // 2) : v0 % (V // 2) + n]
                 factor = weights[:, (d - 1) * V + v0 : (d - 1) * V + v0 + n]
-                src = plain[:] if (b0, d) == (0, D) else h[last][:].indirect(entries(lists[d], v0, n))
+                plainly = d == D and b1 < BLOCKS
+                src = plain[:, v0 : v0 + n] if plainly else h[last][:].indirect(entries(lists[d], v0, n))
                 nc.vector.tensor_tensor(term, src, factor, MULT)
                 turn_and_add(sums[b0], term, False, d == D)
 

from contextlib import ExitStack

import concourse.mybir as mybir
from concourse.masks import make_identity

K, T, S, D, V, H, N = 1024, 2048, 1024, 3, 512, 512, 128
FLOPS = 2 * K * H * S + 2 * H * N * V

F32 = mybir.dt.float32
BF16 = mybir.dt.bfloat16
I32 = mybir.dt.int32
U32 = mybir.dt.uint32
U16 = mybir.dt.uint16
U8 = mybir.dt.uint8
FP8X4 = mybir.dt.float8_e4m3fn_x4
SILU = mybir.ActivationFunctionType.Silu
COPY = mybir.ActivationFunctionType.Copy
MULT = mybir.AluOpType.mult

P = 128
PACK = 4
PART = P * PACK
PASSES = K // PART
TILES = H // P
BLOCKS = V // P
HALF = S // 2
ENTRIES_PER_COLUMN = 16
GATE_RUN = 16
CUT = 768


def tile_picked_lapl_silu_p_kernel(
    tc, x_words, x_scales, w1, w2, gate, offs, cen, pos1, pos2, pos3, out
):
    nc = tc.nc
    with ExitStack() as ctx:
        held = ctx.enter_context(tc.tile_pool(name="held", bufs=1))
        keep = ctx.enter_context(tc.tile_pool(name="keep", bufs=1))
        laid = ctx.enter_context(tc.tile_pool(name="laid", bufs=1))
        psum = ctx.enter_context(tc.psum_pool(name="psum", bufs=1))

        def sb(name, shape, dtype, over=None):
            return keep.tile(shape, dtype, name=name, tag=over or name, align_bytes=64)

        def placed(name, shape, dtype, offset):
            return laid.tile(shape, dtype, name=name, tag=name, align_bytes=64, offset=offset)

        def bank(name, b, cols):
            return psum.tile([P, cols], F32, name=name, tag="bank%d" % b)

        def entries(lst, start, count):
            return lst[:, start // ENTRIES_PER_COLUMN : (start + count) // ENTRIES_PER_COLUMN]

        scale_win = placed("scale_win", [P, T], U8, 2048)
        nc.vector.memset(scale_win[64:, :].bitcast(I32), 0)
        nc.vector.memset(scale_win[32:64, :].bitcast(I32), 0)
        x_plane = sb("x_plane", [P, PASSES * S], U8)
        nc.gpsimd.memset(x_plane[:].bitcast(I32), 0)
        warm_in = sb("warm_in", [P, 1], F32)
        warm_out = sb("warm_out", [P, 1], F32)
        nc.gpsimd.memset(warm_in[:], 0.0)
        nc.scalar.activation(out=warm_out[:], in_=warm_in[:], func=SILU)
        ident = sb("ident", [P, P], F32)
        make_identity(nc, ident[:])

        offs_sb = held.tile([P, S // 16], U16, name="offs_sb")
        lists = [held.tile([P, V // 16], U16, name="list%d" % d) for d in range(D + 1)]
        first_words_at = 18432
        word_win = [placed("word_win0", [P, T], I32, first_words_at), sb("word_win1", [P, T], I32)]
        w1_raw = {}

        def load_words(z):
            nc.sync.dma_start(out=word_win[z][:], in_=x_words[z].rearrange("p n t -> p (n t)").bitcast(I32))

        def load_w1(t, z, room):
            w1_raw[t, z] = room.rearrange("p (j c) -> p j c", j=PACK)
            rows = w1[z * PART : (z + 1) * PART, t * P : (t + 1) * P]
            nc.sync.dma_start(out=w1_raw[t, z], in_=rows.rearrange("(p j) c -> p j c", j=PACK))

        nc.sync.dma_start(
            out=scale_win[:32, :].bitcast(I32), in_=x_scales.bitcast(I32).rearrange("z b n -> b z n")
        )
        nc.sync.dma_start(offs_sb[:], offs)
        gate_col = sb("gate_col", [P, GATE_RUN], F32)
        gate_rows = gate.rearrange("d p v -> (d p) v")[0 : D * P : P - 1, :]
        nc.sync.dma_start(out=gate_col[:], in_=gate_rows.rearrange("a (b k) -> b a k", k=GATE_RUN))
        load_words(0)
        for lst, src in zip(lists, (cen, pos1, pos2, pos3)):
            nc.sync.dma_start(lst[:], src)
        first_raw = sb("first_raw", [P, PART], F32)
        load_w1(0, 0, first_raw[:])
        load_words(1)

        weights = sb("weights", [P, D * V], F32)
        for c in range(GATE_RUN // PACK):
            spread = bank("spread%d" % c, 4 + c, PACK * P)
            for j in range(PACK):
                column = gate_col[:, c * PACK + j : c * PACK + j + 1]
                nc.tensor.transpose(spread[:, j * P : (j + 1) * P], column.to_broadcast([P, P]), ident[:])
            nc.scalar.activation(
                out=weights[:].rearrange("p (d b c j) -> p c d b j", d=D, c=GATE_RUN // PACK, j=PACK)[:, c],
                in_=spread[:].rearrange("p (j b a) -> p a b j", j=PACK, a=D + 1)[:, 1:],
                func=COPY,
                scale=-1.0,
            )

        x_scale = sb("x_scale", [P, S], U8)
        x_early = sb("x_early", [P, S], U32)
        nc.vector.tensor_copy(x_scale[:], scale_win[:].indirect(offs_sb[:]))
        nc.vector.tensor_copy(x_early[:], word_win[0][:].bitcast(U32).indirect(offs_sb[:]))
        for q in range(4):
            nc.sync.dma_start(
                out=x_plane[32 * q : 32 * q + 4, :].bitcast(I32).rearrange("p (z n) -> p z n", z=PASSES),
                in_=x_scale[8 * q : 8 * q + 8, :].bitcast(I32),
            )
        second_raw = placed("second_raw", [P, PART], F32, 64)
        load_w1(0, 1, second_raw[:])
        next_raw = placed("next_raw", [P, PASSES * PART], F32, 4032)
        for z in range(PASSES):
            load_w1(1, z, next_raw[:, z * PART : (z + 1) * PART])
        upper_at = [first_words_at + 64 - 4 * S, first_words_at + 4 * T - 64]
        upper = []
        for z in range(PASSES):
            upper.append(placed("upper_raw%d" % z, [P, PACK, 2 * P], F32, upper_at[z]))
            rows = w1[z * PART : (z + 1) * PART, 2 * P :]
            nc.sync.dma_start(out=upper[z][:], in_=rows.rearrange("(p j) c -> p j c", j=PACK))
        w2_at = first_words_at + 64
        w2_raw = placed("w2_raw", [P, PART], F32, w2_at)
        nc.sync.dma_start(out=w2_raw[:], in_=w2.rearrange("(p j) m -> p (j m)", j=PACK))

        stage, code, scale = {}, {}, {}

        def round_rows(dst, src, copy):
            copy(
                out=dst.rearrange("p (c i j) -> p c j i", i=4, j=PACK),
                in_=src.rearrange("p j (c i) -> p c j i", i=4),
            )

        def round_w1(t, z, copy=nc.scalar.copy, over=None):
            stage[t, z] = sb("stage%d_%d" % (t, z), [P, PART], BF16, over)
            round_rows(stage[t, z][:], w1_raw[t, z], copy)

        def round_upper(z, staged):
            nc.scalar.copy(
                out=staged.rearrange("p (u z q e j) -> p z q j u e", u=2, z=PASSES, e=2, j=PACK)[:, z],
                in_=upper[z][:].rearrange("p j (q u e) -> p q j u e", u=2, e=2),
            )

        def quantise_w1(t, z):
            code[t, z] = sb("code%d_%d" % (t, z), [P, P], U32)
            scale[t, z] = sb("scale%d_%d" % (t, z), [P, P], U8)
            nc.vector.quantize_mx(out=code[t, z][:].bitcast(FP8X4), scales=scale[t, z][:], in_=stage[t, z][:])

        x_late = [sb("x_late0", [P, CUT], U32)]

        def x_code(z, s0, n):
            if z == 0:
                return x_early[:, s0 : s0 + n]
            return x_late[s0 // CUT][:, s0 % CUT : s0 % CUT + n]

        def gather_late(s0, n):
            nc.vector.tensor_copy(x_code(1, s0, n), word_win[1][:].bitcast(U32).indirect(entries(offs_sb, s0, n)))

        h = [sb("h%d" % t, [P, S], F32) for t in range(TILES)]
        acc_banks = [(0, 1, 2, 3), (0, 1), (2, 3), (0, 1)]
        accs = {}

        spans = [[(256 * i, 256)] for i in range(4)], [[(0, HALF)], [(HALF, CUT - HALF), (CUT, S - CUT)]]

        def project(t):
            groups = spans[min(t, 1)]
            accs[t] = [bank("acc%d_%d" % (t, i), acc_banks[t][i], S // len(groups)) for i in range(len(groups))]
            order = [(z, i, piece) for i, g in enumerate(groups) for piece in g for z in range(PASSES)]
            if t == 0:
                order = sorted(order)
            for z, i, (s0, n) in order:
                g0 = groups[i][0][0]
                nc.tensor.matmul_mx(
                    out=accs[t][i][:, s0 - g0 : s0 - g0 + n],
                    lhsT=code[t, z][:].bitcast(FP8X4),
                    lhsT_scale=scale[t, z][:],
                    rhs=x_code(z, s0, n).bitcast(FP8X4),
                    rhs_scale=x_plane[:, z * S + s0 : z * S + s0 + n],
                    start=(z == 0),
                    stop=(z == PASSES - 1),
                )

        def activate(t, which=None):
            width = S // len(accs[t])
            for i in which or range(len(accs[t])):
                nc.scalar.activation(out=h[t][:, i * width : (i + 1) * width], in_=accs[t][i][:], func=SILU)

        terms, totals = {}, {}

        def room_for(t, d, over=None, at=None):
            name = "term%d_%d" % (t, d)
            terms[t, d] = sb(name, [P, V], F32, over) if at is None else placed(name, [P, V], F32, at)

        def fetch(t, d, v0=0, n=V):
            src = h[t][:].indirect(entries(lists[d], v0, n))
            if d == 0:
                nc.scalar.activation(out=terms[t, d][:, v0 : v0 + n], in_=src, func=COPY)
            else:
                factor = weights[:, (d - 1) * V + v0 : (d - 1) * V + v0 + n]
                nc.vector.tensor_tensor(terms[t, d][:, v0 : v0 + n], src, factor, MULT)

        def turn_and_add(total, term, first, final):
            blocks = term.shape[-1] // P
            for b in range(blocks):
                nc.tensor.matmul(
                    out=total[:, b * P : (b + 1) * P],
                    lhsT=term[:, b * P : (b + 1) * P],
                    rhs=ident[:],
                    is_transpose=True,
                    start=(first and b == 0),
                    stop=(final and b == blocks - 1),
                )

        add_order = [(1, 2, 0, 3), (1, 0, 2, 3), (1, 0, 2, 3)]

        def add(t, d):
            if d == add_order[t][0]:
                totals[t] = bank("total%d" % t, 4 + t, V)
            turn_and_add(totals[t], terms[t, d][:], d == add_order[t][0], d == add_order[t][-1])

        def neighbour(t, d, over=None, at=None):
            if (t, d) not in terms:
                room_for(t, d, over, at)
            fetch(t, d)
            add(t, d)

        def centre(t, over=None, at=None):
            room_for(t, 0, over, at)
            fetch(t, 0)


        def round_sum(total, t, b0=0, b1=BLOCKS):
            if t < 2:
                nc.scalar.copy(
                    out=z_view[:, b0:b1, :, 32 * t : 32 * (t + 1), :],
                    in_=total[:].rearrange("v (b p u e) -> v b u p e", b=b1 - b0, u=2, e=2),
                )
            else:
                nc.scalar.copy(
                    out=z_view[:, b0:b1, t - 2, 64:, :],
                    in_=total[:].rearrange("v (b q e) -> v b q e", b=b1 - b0, e=2),
                )

        round_w1(0, 0)
        quantise_w1(0, 0)
        gather_late(0, CUT)
        round_w1(0, 1)
        quantise_w1(0, 1)
        x_late.append(placed("x_late1", [P, S - CUT], U32, 64))
        gather_late(CUT, S - CUT)
        round_w1(1, 0)
        project(0)
        activate(0)
        round_w1(1, 1, nc.vector.tensor_copy, over="word_win1")
        for z in range(PASSES):
            quantise_w1(1, z)
        project(1)

        activate(1, [0])
        upper_stage = sb("upper_stage", [P, PASSES * 2 * PART], BF16, over="code1_1")
        for z in range(PASSES):
            round_upper(z, upper_stage[:])
        activate(1, [1])
        centre(0, at=upper_at[1] + 64 - 4 * V)
        neighbour(0, 1)
        neighbour(0, 2)
        room_for(0, 3)
        fetch(0, 3)
        for t in (2, 3):
            codes = sb("code%d" % t, [P, PASSES * P], U32)
            scales = sb("scale%d" % t, [P, PASSES * P], U8)
            staged = upper_stage[:, (t - 2) * K : (t - 1) * K]
            nc.vector.quantize_mx(out=codes[:].bitcast(FP8X4), scales=scales[:], in_=staged)
            for z in range(PASSES):
                code[t, z], scale[t, z] = codes[:, z * P : (z + 1) * P], scales[:, z * P : (z + 1) * P]
            project(t)
        add(0, 0)
        add(0, 3)
        neighbour(1, 1)
        centre(1)
        add(1, 0)
        activate(2)
        activate(3)
        neighbour(1, 2)
        neighbour(1, 3)
        centre(2)
        last = TILES - 1
        centre(last)
        plain = sb("plain", [P, V - P], F32)
        nc.scalar.activation(out=plain[:], in_=h[last][:].indirect(entries(lists[D], 0, V - P)), func=COPY)
        neighbour(2, 1)
        add(2, 0)
        neighbour(2, 2)

        groups = [(0, 2, 7, 2, 1), (2, 3, 0, 7, 5), (3, 4, 1, 0, 6)]
        sums = {}
        for b0, b1, sum_bank, back_bank, prod_bank in groups:
            sums[b0] = bank("last%d" % b0, sum_bank, (b1 - b0) * P)
            turn_and_add(sums[b0], terms[last, 0][:, b0 * P : b1 * P], True, False)
        neighbour(2, 3)
        z_rows = sb("z_rows", [P, BLOCKS * H], BF16, over="term2_0")
        z_view = z_rows[:].rearrange("v (b u p e) -> v b u p e", b=BLOCKS, u=2, e=2)
        for t in range(last):
            round_sum(totals[t], t)
        halves = [sb("last_terms0", [P, D, V // 2], F32), sb("last_terms1", [P, D, V // 2], F32, over="term3_0")]

        z_cols, backs = {}, {}

        def turn_back(group, u):
            b0, b1 = group[:2]
            if u == 0:
                backs[b0] = bank("back%d" % b0, group[3], 2 * (b1 - b0) * P)
            for b in range(b0, b1):
                w = 2 * (b - b0) + u
                words = z_rows[:].bitcast(F32)[:, (2 * b + u) * P : (2 * b + u + 1) * P]
                nc.tensor.transpose(backs[b0][:, w * P : (w + 1) * P], words, ident[:])

        def sum_group(group):
            b0, b1 = group[:2]
            v0, n = b0 * P, (b1 - b0) * P
            for d in range(1, D + 1):
                term = halves[2 * v0 // V][:, d - 1, v0 % (V // 2) : v0 % (V // 2) + n]
                factor = weights[:, (d - 1) * V + v0 : (d - 1) * V + v0 + n]
                plainly = d == D and b1 < BLOCKS
                src = plain[:, v0 : v0 + n] if plainly else h[last][:].indirect(entries(lists[d], v0, n))
                nc.vector.tensor_tensor(term, src, factor, MULT)
                turn_and_add(sums[b0], term, False, d == D)

        def weave(group, copy):
            b0, b1 = group[:2]
            z_cols[b0] = sb("z_cols%d" % b0, [P, (b1 - b0) * P * PACK], BF16)
            copy(
                out=z_cols[b0][:].bitcast(F32).rearrange("p (b v u) -> p b v u", u=2, v=P),
                in_=backs[b0][:].rearrange("p (b u v) -> p b v u", u=2, v=P),
            )

        first, second, third = groups
        sum_group(first)
        turn_back(first, 0)
        round_sum(sums[first[0]], last, *first[:2])
        w2_stage = sb("w2_stage", [P, PART], BF16, over="last_terms0")
        round_rows(w2_stage[:], w2_raw[:].rearrange("p (j m) -> p j m", j=PACK), nc.scalar.copy)
        sum_group(second)
        round_sum(sums[second[0]], last, *second[:2])
        turn_back(first, 1)
        weave(first, nc.vector.tensor_copy)
        sum_group(third)
        round_sum(sums[third[0]], last, *third[:2])
        w2_code = sb("w2_code", [P, N], U32, over="term3_0")
        w2_scale = sb("w2_scale", [P, N], U8)
        nc.vector.quantize_mx(out=w2_code[:].bitcast(FP8X4), scales=w2_scale[:], in_=w2_stage[:])
        for g in (second, third):
            for u in range(2):
                turn_back(g, u)
            weave(g, nc.scalar.copy)
        for b0, b1, sum_bank, back_bank, prod_bank in groups:
            n = (b1 - b0) * P
            codes = sb("codes%d" % b0, [P, n], U32)
            z_scale = sb("z_scale%d" % b0, [P, n], U8)
            prod = bank("prod%d" % b0, prod_bank, n)
            nc.vector.quantize_mx(out=codes[:].bitcast(FP8X4), scales=z_scale[:], in_=z_cols[b0][:])
            nc.tensor.matmul_mx(
                out=prod[:],
                lhsT=w2_code[:].bitcast(FP8X4),
                lhsT_scale=w2_scale[:],
                rhs=codes[:].bitcast(FP8X4),
                rhs_scale=z_scale[:],
                start=True,
                stop=True,
            )
            leave = nc.scalar.copy if b0 == 0 else nc.vector.tensor_copy
            result = sb("result%d" % b0, [P, n], F32, over="term2_0" if b0 == 0 else None)
            leave(out=result[:], in_=prod[:])
            nc.sync.dma_start(out=out[:, b0 * P : b1 * P], in_=result[:])
